import numpy as np, ml_dtypes
CORES = [36,164,52,180,100,228,116,244]
N = 8
import mx_ref
BF = ml_dtypes.bfloat16
def cols(t, e):
    v = np.concatenate([t.reshape(128, -1, 4), np.zeros((128, 1, 4), BF)], axis=1)
    return np.ascontiguousarray(v[:, e]).reshape(128, -1)
def cut(t, i, w=512):
    return t[:, w * i:w * i + w]
def pick(q, e):
    c = np.concatenate([q[0].reshape(128, -1, 4), np.zeros((128, 1, 4), np.uint8)], axis=1); s = np.concatenate([q[1], np.ones((16, 1), np.uint8)], axis=1)
    return (np.ascontiguousarray(c[:, e].reshape(128, -1)), np.ascontiguousarray(s[:, e]))
def join(*qs):
    return (np.concatenate([q[0] for q in qs], axis=1), np.concatenate([q[1] for q in qs], axis=1))
def put(q, e, v):
    c, s = q[0].reshape(128, -1, 4).copy(), q[1].copy(); c[:, e] = v[0].reshape(128, -1, 4); s[:, e] = v[1]
    return (c.reshape(128, -1), s)
def pk(c, s):
    return (np.ascontiguousarray(c), mx_ref.live(s))
def emit(q):
    return q[0], q[1]
def decode(q):
    o = []
    for b in range(4):
        e = np.zeros((128, 128, 4), np.float32); e[np.arange(128), np.arange(128), b] = 1
        o.append(mx_ref.matmul(mx_ref.quantize(e.reshape(128, 512).astype(BF)), q))
    return np.stack(o, axis=2).reshape(128, -1)
def f(rng, *shape):
    return mx_ref.flush((rng.standard_normal(shape, dtype=np.float32) * np.exp2(rng.integers(-2, 3, shape[:-1] + (1,)))).astype(BF))
def wide(rng, *shape, cols=0):
    v = rng.standard_normal(shape, dtype=np.float32) * np.exp2(rng.integers(-12, 13, shape)).astype(np.float32)
    if cols: v *= np.repeat(np.exp2(rng.integers(-cols, cols + 1, shape[:-2] + (1, shape[-1] // 4))) * (rng.random(shape[:-2] + (1, shape[-1] // 4)) > 0.0625), 4, axis=-1).astype(np.float32)
    return mx_ref.flush(v.astype(BF))
P, K, R, O = 128, 16, 2, 1
def big(v):
    v = v.astype(np.float32)
    v[np.abs(v) < np.float32(2.0 ** -16)] = 0
    return v.astype(BF)
def times(t, k):
    return mx_ref.flush((t.astype(np.float32) * np.float32(k)).astype(BF))
def signs(d, v, s):
    g = np.where(d["u"][0, :, :4].astype(np.float32) < 0, -1, 1)
    a = np.abs(v.astype(np.float32)).reshape(N, 128, -1, 4) * g[None, :, None, :] * s[:, None, :, None]
    return big(a.reshape(N, 128, -1))
def counted(rng, d):
    n = P // 2 + rng.permutation(K)[:N]
    return signs(d, d["tb"], np.stack([np.where(rng.permutation(P) < n[r], 1, -1) for r in range(N)]))
def setup_inputs(rng):
    v = np.zeros((128, 512), np.float32)
    v[:, :4] = f(rng, 128, 4).astype(np.float32)
    return {"tb": big(f(rng, N, 128, 4 * P)), "nz": big(f(rng, N, 128, 4 * R * K)), "u": np.stack([v.astype(BF)] * N), "w": f(rng, N, 128, 512 * O)}
def setup_inputs_down(rng):
    d = setup_inputs(rng)
    d["tb"] = counted(rng, d)
    d["nz"] = signs(d, 64 * (1 + rng.random((N, 128, 4 * R * K))), np.full((N, R * K), -1))
    return d
def setup_inputs_spread(rng):
    d = setup_inputs(rng)
    t, r = big(wide(rng, N, 128, 4 * P, cols=6)), int(rng.integers(0, N))
    x = (1 + rng.random((N, 128, 4 * P))) * np.exp2(rng.integers(12, 18, (N, 128, 4 * P)) + np.repeat(rng.integers(0, 4, (N, 1, P)), 4, axis=2))
    t[r] = signs(d, x, np.ones((N, P), np.int64))[r]
    return {**d, "tb": t, "nz": big(wide(rng, N, 128, 4 * R * K, cols=6)), "u": times(d["u"], 2.0 ** 24)}
def setup_inputs_swap(rng):
    d = setup_inputs(rng)
    d["tb"] = counted(rng, d)
    d["nz"] = signs(d, 64 * (1 + rng.random((N, 128, 4 * R * K))), np.full((N, R * K), 1))
    return d
def setup_inputs_ties(rng):
    d = setup_inputs(rng)
    a = rng.permutation(N) <= N // 2
    d["tb"] = np.stack([cols(d["tb"][int(a[r])], rng.permutation(P) % (P // (K + 1))) for r in range(N)])
    d["nz"] = np.stack([d["nz"][0]] * N)
    return d
def setup_inputs_zero(rng):
    d = setup_inputs(rng)
    d["u"] = times(np.abs(d["u"].astype(np.float32)), 2.0 ** -26)
    d["tb"], d["nz"] = big(times(d["tb"], 2.0 ** -10)), big(times(d["nz"], 2.0 ** -10))
    s, a = np.zeros((N, P), np.int64), rng.permutation(N)
    for i in range(N - 1):
        m, n, e = P // 2 - 4 * i, K // 2 - i, rng.permutation(P)
        s[a[i], e[:m]] = 1
        s[a[i], e[m:m + n]] = -1
    d["tb"] = signs(d, d["tb"], s)
    for r in range(N):
        d["tb"][r].reshape(128, P, 4)[:, np.flatnonzero(s[r] == 0)[1::2]] = BF(-0.0)
    d["nz"] = big(d["nz"].astype(np.float32) * np.repeat(rng.random((N, 1, R * K)) > 0.25, 4, axis=2))
    return d
def check_inputs(d):
    b = []
    for k, low, high in (("tb", -16, 26), ("nz", -16, 26), ("u", -30, 30), ("w", -30, 30)):
        v = np.abs(d[k].astype(np.float32))
        if not (np.isfinite(v).all() and ((v == 0) | (v >= 2.0 ** low) & (v <= 2.0 ** high)).all()): b.append("a value of " + k)
    v = d["u"].astype(np.float32)
    if (v[:, :, 4:] != 0).any(): b.append("u has numbers behind its column 0")
    if (v != v[:1]).any(): b.append("u isn't the same on all ranks")
    return b
def reference(tb, nz, u, w):
    T = [mx_ref.quantize(tb[r]) for r in range(N)]
    qu = [mx_ref.quantize(u[r]) for r in range(N)]
    od = np.zeros((N, R, N), np.float32)
    for t in range(R):
        s = [mx_ref.matmul(qu[r], T[r])[0] + np.float32(0) for r in range(N)]
        fitness = np.array([np.count_nonzero(s[r] > 0) for r in range(N)])
        place = np.argsort(-fitness, kind="stable")
        od[:, t] = place
        new = T[:]
        for i in range(N // 2):
            a, b = place[i], place[N - 1 - i]
            j = np.argsort(s[a], kind="stable")[:K]
            noise = mx_ref.quantize(np.ascontiguousarray(nz[b][:, 4 * t * K:4 * (t + 1) * K]))
            v = np.float32(0.5) * decode(pick(T[a], j)) + np.float32(0.5) * decode(noise)
            new[b] = put(T[a], j, mx_ref.quantize(np.ascontiguousarray(v.astype(BF))))
        T = new
    oc, osc, y = np.zeros((N, 128, 4 * P), np.uint8), np.zeros((N, 16, P), np.uint8), np.zeros((N, 128, O * P), np.float32)
    for r in range(N):
        oc[r], osc[r] = emit(T[r])
        for o in range(O):
            y[r, :, o * P:(o + 1) * P] = mx_ref.matmul(mx_ref.quantize(np.ascontiguousarray(cut(w[r], o))), T[r])
    return {"oc": oc, "osc": osc, "od": od, "y": y}

@@ -1,0 +1,532 @@
+from concourse.bass import DstId, RemoteDMATransfer
+from concourse.mybir import dt, AluOpType, AxisListType, ActivationFunctionType
+
+A = AluOpType
+F = ActivationFunctionType
+NR, SL = 8, 18
+ROWS = {"KR": 32, "KT": 32, "KR1": 32, "KT1": 32, "FS": 16, "FBR": 16, "BR": 16, "B16": 16, "BS": 16, "A1": 16, "F16": 16, "J18": 16}
+RN = list(ROWS)
+TINY, BIG = 2.0 ** -100, 1e29
+
+_f, _b, _u = "float32", "bfloat16", "uint16"
+
+
+def _mx(d, name, n):
+    d[name] = ("sbuf", [128, n], "float8_e4m3fn_x4")
+    d[name + "s"] = ("sbuf", [128, n], "uint8")
+
+
+SCRATCH = {}
+for _n, _w, _t in (
+        ("TB", 512, _b), ("UC", 4, _b), ("NUC", 4, _b), ("NZ", 128, _b), ("WT", 512, _b), ("ZB", 576, _b), ("UT", 512, _b), ("NU", 512, _b),
+        ("CI", 8, "int32"), ("CF", 8, _f), ("CK", 16, _f), ("J32", 32, _f), ("KI", 128, _b), ("IREF", 128, _b), ("OH2", 256, _b),
+        ("OHREF", 512, _b), ("QR", 128, _b), ("ZE", 520, _b), ("TIE", 128, _f), ("DIAG", 128, _f), ("RM", 128, _f),
+        ("M32", 32, _f), ("MS", 8, _f), ("JC", 8, _f), ("TIE8", 8, _f), ("WN", 32, _f), ("O0", 16, _f), ("O1", 16, _f),
+        ("MVC", 512, _b), ("ONE", 512, _b), ("ZW", 512, _b), ("ST4", 512, _b), ("NT0", 576, _b), ("NT1", 576, _b),
+        ("INFO", 512, _b), ("OHT", 512, _b), ("CMP", 128, _f), ("SM", 384, _f), ("R32", 32 * len(ROWS), _f),
+        ("V0", 576, _b), ("V1", 576, _b), ("NZ1", 80, _f), ("TH8", 8, _f), ("THR", 128, _f), ("ZT", 512, _b),
+        ("TI1", 128, _f), ("TA", 128, _f), ("IND", 128, _f), ("CS", 128, _f),
+        ("D5", 512, _f), ("MT", 512, _b), ("VT", 512, _b), ("OHL", 128, _b), ("STT", 512, _b), ("NT", 512, _b), ("Y", 128, _f), ("CM1", 128, _f),
+        ("OFF1", 4, _u), ("OFFH", 18, _u), ("OFF3", 16, _u), ("OP0", 2, _u), ("OP1", 2, _u), ("OX0", 2, _u), ("TG0", 2, _u), ("TG1", 2, _u),
+        ("OFFO", 2, _u), ("OFFG", 32, _u), ("OFFF", 8, _u), ("OFT", 8, _u)):
+    SCRATCH[_n] = ("sbuf", [128, _w], _t)
+for _n, _w in (("UQ", 128), ("NUQ", 128), ("TQ", 128), ("MVQ", 128), ("OHQ", 128), ("ONQ", 128), ("EQ", 512), ("N0Q", 144), ("N1Q", 144),
+               ("WQ", 128), ("ZWQ", 128), ("S4Q", 128), ("L1S", 144), ("LD1", 144), ("NB", 160), ("W2", 528), ("PH1", 128), ("S3", 128),
+               ("ZQ", 128), ("MQ", 128), ("STQ", 128), ("NTQ", 128), ("FT", 128), ("HT", 128)):
+    _mx(SCRATCH, _n, _w)
+for _n, _w in (("PV", 2048), ("PA", 512), ("PB", 512), ("PC", 512), ("PD", 512)):
+    SCRATCH[_n] = ("psum", [128, _w], _f)
+
+SEMAPHORES = ["sv", "sa", "st", "sg", "arrh", "arrg", "arr1", "arr2", "arr3", "arrp"]
+SEMAPHORES += ["d%d" % i for i in range(24)] + ["l%d" % i for i in range(12)]
+
+
+def _helper_of(topo, core):
+    return [c for c in topo.cores_of(core) if topo.die(c) != topo.die(core)][0]
+
+
+def _dst(topo, d, s):
+    rid, pid = topo.addr(d, s)
+    return DstId(rid=rid, pnc=pid)
+
+
+def _hand_on(g, core, T, topo, owner):
+    me = T.rank_of(owner)
+    near, far = topo.engines(owner, core), len(topo.engines(owner, T.cores[me - 1]))
+    for k, (src, dst, sem, n) in enumerate((("HT", "PH1", "arrh", len(near)), ("HTs", "PH1s", "arrg", len(near) - far))):
+        g.wait_ge(T.sem[sem], n)
+        tr = []
+        for i, d in enumerate((me + x) % NR for x in range(1, NR)):
+            c = T.cores[d]
+            s, t = T[src][:, 16 * d:16 * d + 16], T[dst][:, 16 * me:16 * me + 16]
+            if k == 0:
+                s, t = s.bitcast(dt.uint8), t.bitcast(dt.uint8)
+            tr.append(RemoteDMATransfer(dst_ids=[_dst(topo, c, core)], dma_engine_mask=1 << topo.engines(core, c)[i],
+                                        remote_sem=T.sem.arrp, srcs=[s], dsts=[t]))
+        g.remote_dma_fused(tr, local_sem=T.sem["l%d" % k])
+    for k in range(2):
+        g.wait_ge(T.sem["l%d" % k], NR - 1)
+
+
+def rank_program(g, core, T, topo):
+    me = T.rank_of(core)
+    if me is None:
+        for c in T.cores:
+            if _helper_of(topo, c) == core:
+                _hand_on(g, core, T, topo, c)
+        return
+    ENG = {"v": g.vector, "a": g.scalar, "t": g.tensor, "g": g, "s": g.sync}
+    SEM = {"v": "sv", "a": "sa", "t": "st", "g": "sg"}
+    cnt, seen, acc, nd, nl, ends = {}, {q: {} for q in ENG}, {}, [0], [0], []
+
+    def clash(a, lo, hi, st):
+        if a[1] <= lo or hi <= a[0]:
+            return False
+        return not (a[2] == st and st > 1 and a[0] % st != lo % st)
+
+    def span(x):
+        if SCRATCH[x[0]][0] == "psum":
+            return x[0], x[1] // 512 * 512, (x[2] + 511) // 512 * 512, 1
+        return x[0], x[1], x[2], x[3]
+
+    def waits(q, rd, wr, dma=False):
+        need = {}
+        for w, xs in ((False, rd), (True, wr)):
+            for x in xs:
+                if x[0] not in SCRATCH:
+                    continue
+                n, lo, hi, st = span(x)
+                ps = SCRATCH[n][0] == "psum"
+                for a in acc.get(n, []):
+                    if not clash(a, lo, hi, st):
+                        continue
+                    same = a[4] == q and not dma and not a[6]
+                    if same and (q == "t" or not a[3]):
+                        continue
+                    if not (w or a[3]) and (same or not ps):
+                        continue
+                    need[a[5][0]] = max(need.get(a[5][0], 0), a[5][1])
+        for s, val in need.items():
+            if seen[q].get(s, 0) < val:
+                ENG[q].wait_ge(T.sem[s], val)
+                seen[q][s] = val
+
+    def note(q, rd, wr, tok, dma=False):
+        for w, xs in ((False, rd), (True, wr)):
+            for x in xs:
+                if x[0] in SCRATCH:
+                    n, lo, hi, st = span(x)
+                    acc.setdefault(n, []).append((lo, hi, st, w, q, tok, dma))
+
+    def v(n, lo=0, hi=None, st=1):
+        if n in ROWS:
+            o = 32 * RN.index(n)
+            return ("R32", o + lo, o + (ROWS[n] if hi is None else hi), st)
+        return (n, lo, SCRATCH[n][1][1] if hi is None else hi, st)
+
+    def ap(x):
+        return T[x[0]][:, x[1]:x[2]] if x[3] == 1 else T[x[0]][:, x[1]:x[2]:x[3]]
+
+    def op(q, fn, rd, wr):
+        waits(q, rd, wr)
+        cnt[q] = cnt.get(q, 0) + 1
+        fn().then_inc(T.sem[SEM[q]], 1)
+        note(q, rd, wr, (SEM[q], cnt[q]))
+
+    def sc(x):
+        return ap(x) if isinstance(x, tuple) else x
+
+    def ts(out, in0, s1, op0, s2=None, op1=None):
+        rd = [in0] + [s for s in (s1, s2) if isinstance(s, tuple)]
+        if op1 is None:
+            op("v", lambda: g.vector.tensor_scalar(ap(out), ap(in0), sc(s1), None, op0), rd, [out])
+        else:
+            op("v", lambda: g.vector.tensor_scalar(ap(out), ap(in0), sc(s1), sc(s2), op0, op1), rd, [out])
+
+    def tt(out, a, b, o):
+        op("v", lambda: g.vector.tensor_tensor(ap(out), ap(a), ap(b), o), [a, b], [out])
+
+    def red(out, a):
+        op("v", lambda: g.vector.tensor_reduce(ap(out), ap(a), AxisListType.X, A.add), [a], [out])
+
+    def cp(out, a):
+        op("v", lambda: g.vector.tensor_copy(ap(out), ap(a)), [a], [out])
+
+    def tr(out, a):
+        op("v", lambda: g.vector.transpose(ap(out), ap(a)), [a], [out])
+
+    def ms(out, c):
+        op("v", lambda: g.vector.memset(ap(out), c), [], [out])
+
+    def act(out, a, fn=F.Copy, **kw):
+        k2 = {k: sc(x) for k, x in kw.items()}
+        op("a", lambda: g.scalar.activation(ap(out), ap(a), fn, **k2), [a] + [x for x in kw.values() if isinstance(x, tuple)], [out])
+
+    def quant(out, in_):
+        o2 = v(out[0] + "s", out[1], out[2])
+        op("v", lambda: g.vector.quantize_mx(ap(out), ap(o2), ap(in_)), [in_], [out, o2])
+
+    def mm(out, w, x, start=True, stop=True):
+        ws, xs = v(w[0] + "s", w[1], w[2]), v(x[0] + "s", x[1], x[2])
+        op("t", lambda: g.tensor.matmul_mx(ap(out), ap(w), ap(ws), ap(x), ap(xs), start, stop), [w, ws, x, xs], [out])
+
+    def scatter(out, in_, off):
+        op("v", lambda: g.vector.tensor_copy(ap(out).indirect(ap(off)), ap(in_)), [in_, off], [out])
+
+    def gather(out, win, off):
+        op("v", lambda: g.vector.tensor_copy(ap(out), ap(win).indirect(ap(off))), [win, off], [out])
+
+    def gather_add(out, win, off, col):
+        op("v", lambda: g.vector.tensor_scalar(ap(out), ap(win).indirect(ap(off)), ap(col), None, A.add), [win, off, col], [out])
+
+    def pick_c(out, win, off):
+        op("v", lambda: g.vector.tensor_copy(ap(out).bitcast(dt.uint32), ap(win).bitcast(dt.uint32).indirect(ap(off))), [win, off], [out])
+
+    def pick_s(out, win, off):
+        out, win = v(out[0] + "s", out[1], out[2]), v(win[0] + "s", win[1], win[2])
+        op("a", lambda: g.scalar.activation(ap(out), ap(win).indirect(ap(off)), F.Copy), [win, off], [out])
+
+    def dma(q, out, in_, oap=None, iap=None):
+        waits(q, [in_], [out], True)
+        s = "d%d" % nd[0]
+        nd[0] += 1
+        ENG[q].dma_start(ap(out) if oap is None else oap, ap(in_) if iap is None else iap).then_inc(T.sem[s], 16)
+        note(q, [in_], [out], (s, 16), True)
+        ends.append((s, 16))
+
+    def codes(x):
+        return ap(x).bitcast(dt.uint8)
+
+    def landed(n, lo, hi, tok):
+        if hi > lo:
+            for m in (n, n + "s"):
+                note("-", [], [v(m, lo, hi)], tok, True)
+
+    def send(x, transfers):
+        waits("g", [t[2] for t in transfers], [], True)
+        s, n = "l%d" % nl[0], 0
+        nl[0] += 1
+        out = []
+        for dc, y, z, mask, sem in transfers:
+            cast = codes if x else ap
+            out.append(RemoteDMATransfer(dst_ids=[_dst(topo, c, core) for c in dc], dma_engine_mask=mask, remote_sem=T.sem[sem],
+                                         srcs=[cast(z)], dsts=[cast(y) for c in dc]))
+            n += bin(mask).count("1")
+        g.remote_dma_fused(out, local_sem=T.sem[s])
+        note("g", [t[2] for t in transfers], [], (s, n), True)
+        ends.append((s, n))
+
+    others = [(me + i) % NR for i in range(1, NR)]
+    oc_ = [T.cores[d] for d in others]
+    helper = _helper_of(topo, core)
+    engs = topo.engines(core, oc_[0])
+    m_all = topo.mask(core, oc_[0])
+    m_help = topo.mask(core, helper)
+    m_far = m_help & ~m_all
+    bcast = 2 * len(engs) * (NR - 1)
+
+    smn = [0]
+
+    def sm(n=1):
+        smn[0] += n
+        return ("SM", smn[0] - n, smn[0], 1)
+
+    dma("s", v("TB"), v("TB"), None, T.tb[:, :])
+    dma("a", v("UC"), v("UC"), None, T.u[:, 0:4])
+    dma("a", v("NZ"), v("NZ"), None, T.nz[:, :])
+    dma("s", v("WT"), v("WT"), None, T.w[:, :])
+
+    def iota(out, pattern, mult, small=True, base=0):
+        if small:
+            op("g", lambda: g.iota(ap(out), pattern, base, mult, allow_small_or_imprecise_dtypes=True), [], [out])
+        else:
+            op("g", lambda: g.iota(ap(out), pattern, base, mult), [], [out])
+
+    iota(v("CI", 0, 1), [[0, 1]], 1, False)
+    iota(v("KI"), [[1, 128]], 0)
+    iota(v("OH2"), [[0, 8], [1, 16], [16, 2]], 0)
+    iota(v("J32"), [[1, 32]], 0)
+    iota(v("IREF"), [[0, 8], [1, 16]], 0)
+
+    ms(v("ZB"), 0.0)
+    act(v("MVC"), v("ZB", 0, 512))
+    ci, cf, ck = (lambda i: v("CI", i, i + 1)), (lambda i: v("CF", i, i + 1)), (lambda i: v("CK", i, i + 1))
+    J8, J16 = v("J32", 0, 8), v("J32", 0, 16)
+    ts(ci(1), ci(0), 15, A.bitwise_and)
+    ts(ci(2), ci(0), 4, A.logical_shift_right)
+    ts(ci(4), ci(0), 3, A.bitwise_and)
+    ts(ci(5), ci(0), 2, A.logical_shift_right)
+    ts(ci(3), ci(0), 31, A.bitwise_and)
+    cp(v("CF", 0, 6), v("CI", 0, 6))
+    P, I16, S16, Q4, P4 = cf(0), cf(1), cf(2), cf(4), cf(5)
+    ts(v("TIE"), v("KI"), P, A.is_lt, TINY, A.mult)
+    for h in range(2):
+        act(v("OHREF", h, 512, 2), v("OH2"))
+    ts(ck(1), S16, 16.0, A.mult)
+    for e, x in ((0, ck(1)), (1, I16), (10, ck(1)), (11, I16), (16, S16), (21, I16), (26, S16), (31, I16)):
+        act(v("MVC", e, e + 1), x)
+
+    ts(v("NUC"), v("UC"), -1.0, A.mult)
+    for b in range(4):
+        ts(v("UT", b, 512, 4), v("ZB", 0, 128), v("UC", b, b + 1), A.add)
+        act(v("NU", b, 512, 4), v("ZB", 0, 128), F.Identity, bias=v("NUC", b, b + 1))
+    act(v("INFO"), v("ZB", 0, 512))
+    act(v("ZE"), v("ZB", 0, 520))
+
+    TQ = v("TQ")
+    quant(TQ, v("TB"))
+    send(True, [([helper], v("HT"), TQ, m_help, "arrh")])
+    quant(v("UQ"), v("UT"))
+    quant(v("NUQ"), v("NU"))
+    PX, PS, PL, PF = v("PA", 0, 128), v("PB", 0, 128), v("PC", 0, 128), v("PD", 0, 144)
+    mm(PX, v("UQ"), TQ, True, False)
+    mm(PX, TQ, v("NUQ"), False, True)
+    mm(PS, TQ, v("UQ"))
+    quant(v("MVQ"), v("MVC"))
+    rk = sm()
+    tt(v("CMP"), PX, v("TIE"), A.is_lt)
+    red(rk, v("CMP"))
+    ts(v("OHT"), v("OHREF"), rk, A.is_equal)
+    quant(v("OHQ"), v("OHT"))
+    ts(v("INFO", 0, 1), v("PB", 0, 1), 0.0, A.is_gt)
+    mm(PL, v("OHQ"), v("MVQ"))
+    cp(v("OFF1"), v("PC", 0, 4))
+    cp(v("INFO", 4, 8), v("PC", 4, 8))
+    pick_s(v("L1S", 0, 16), TQ, v("OFF1", 0, 1))
+    pick_c(v("L1S", 0, 16), TQ, v("OFF1", 0, 1))
+    quant(v("L1S", 16, 144), v("INFO"))
+    own = v("LD1", SL * me, SL * me + SL)
+    send(True, [(oc_, own, v("L1S", 0, SL), m_all, "arr1")])
+    send(False, [(oc_, v("LD1s", own[1], own[2]), v("L1Ss", 0, SL), m_all, "arr1")])
+    send(False, [([helper], v("HTs"), v("TQs"), m_far, "arrg")])
+    dma("s", own, v("L1S", 0, SL), codes(own), codes(v("L1S", 0, SL)))
+    dma("s", v("LD1s", own[1], own[2]), v("L1Ss", 0, SL))
+    pown = v("PH1", 16 * me, 16 * me + 16)
+    town = v("TQ", 16 * me, 16 * me + 16)
+    dma("s", pown, town, codes(pown), codes(town))
+    dma("s", v("PH1s", pown[1], pown[2]), v("TQs", town[1], town[2]))
+    pick_s(v("NB", 144, 160), TQ, v("OFF1", 2, 3))
+    pick_c(v("NB", 144, 160), TQ, v("OFF1", 2, 3))
+
+    for n in ("KR", "KR1"):
+        iota(v(n), [[0, 2], [-1, 16]], 0, True, 7)
+    iota(v("QR"), [[0, 8], [1, 4], [0, 4]], 0)
+    ts(v("ZE", 4, 516, 4), v("KI"), P, A.is_equal, 0.5, A.mult)
+    ts(v("TIE8"), J8, -0.125, A.mult, 0.875, A.add)
+    for b in range(4):
+        quant(v("EQ", 128 * b, 128 * b + 128), v("ZE", 4 - b, 516 - b))
+    E = [v("EQ", 128 * b, 128 * b + 128) for b in range(4)]
+    for t in (0, 1):
+        n = "NT%d" % t
+        act(v(n), v("ZB"))
+        for a in range(NR):
+            act(v(n, 72 * a, 72 * a + 64), v("NZ", 64 * t, 64 * t + 64))
+        quant(v("N%dQ" % t), v(n))
+        if t == 0:
+            act(v("ONE"), v("ZB", 0, 512))
+            ms(v("ONE", 0, 512, 4), 1.0)
+            ts(v("J18"), J16, float(SL), A.mult)
+            ms(v("WN", 16, 32), float(SL * NR))
+            quant(v("ONQ"), v("ONE"))
+    PVb = [v("PV", 512 * b, 512 * b + 144) for b in range(4)]
+    for b in range(4):
+        mm(PVb[b], E[b], v("N1Q"))
+    ms(v("NZ1", 64, 80), 0.0)
+    for b in range(4):
+        act(v("NZ1", b, 64, 4), v("PV", 512 * b, 512 * b + 16))
+    for b in range(4):
+        mm(PVb[b], E[b], v("N0Q"), True, False)
+    ms(v("F16"), 0.0)
+    ts(v("OFT"), J8, 0.0, A.add)
+    ts(v("RM"), v("IREF"), 0.0, A.is_gt)
+    ts(v("MS"), J8, S16, A.is_equal)
+    ms(v("ZW"), 0.0)
+    ts(v("DIAG"), v("KI"), P, A.is_equal)
+    for b, x in ((0, 16.0), (1, 1.0)):
+        ms(v("ZW", b, 512, 4), x)
+    quant(v("ZWQ"), v("ZW"))
+
+    landed("LD1", 0, own[1], ("arr1", bcast))
+    landed("LD1", own[2], 144, ("arr1", bcast))
+    mm(PF, v("ONQ"), v("LD1"))
+    for b in range(4):
+        mm(PVb[b], E[b], v("LD1"), False, True)
+    for b in range(4):
+        act(v("V0", b, 576, 4), PVb[b])
+    FIT = v("PD", 16, 144, SL)
+
+    def places(kr, kt, off):
+        pl, c16 = sm(), sm(16)
+        tr(v(kt), v(kr))
+        ts(c16, v(kr, 0, 16), v(kt, 0, 1), A.is_gt)
+        red(pl, c16)
+        ts(v(off, 0, 1), pl, 0.0, A.add)
+        return pl
+
+    for o in (0, 16):
+        tt(v("KR", o, o + 8), FIT, v("TIE8"), A.add)
+    pl0 = places("KR", "KT", "OP0")
+    gv = sm()
+    ts(gv, pl0, 3.5, A.is_lt, 16.0, A.mult)
+    scatter(v("WN", 0, 16), v("J18"), v("OP0", 0, 1))
+    ts(v("OX0", 0, 1), gv, pl0, A.subtract, 7.0, A.add)
+    sh = me % 2
+    gather_add(v("OFFH", sh, sh + 16), v("WN"), v("OX0", 0, 1), I16)
+    oh = v("OFFH", me + sh, me + sh + 1)
+    quant(v("NB", 0, 144), v("V0"))
+    hown = v("W2", 128 + 16 * me, 144 + 16 * me)
+    pick_c(hown, v("NB"), oh)
+    pick_s(hown, v("NB"), oh)
+    hos = v("W2s", hown[1], hown[2])
+    send(True, [(oc_, hown, hown, m_all, "arr2")])
+    send(False, [(oc_, hos, hos, m_all, "arr2")])
+
+    for b in range(4):
+        mm(PVb[b], E[b], v("N1Q"), True, False)
+        mm(PVb[b], E[b], v("LD1"), False, True)
+    for b in range(4):
+        act(v("V1", b, 576, 4), PVb[b])
+    TK, t1, CAP, KB = sm(8), sm(), sm(8), sm(8)
+    ts(t1, pl0, -1.0, A.mult, 7.0, A.add)
+    cp(v("F16", 0, 8), FIT)
+    scatter(v("O0"), J16, v("OP0", 0, 1))
+    ts(v("TG0", 0, 1), t1, pl0, A.min)
+    scatter(v("FS"), v("F16"), v("OP0", 0, 1))
+    gather(v("BR"), v("O0"), v("TG0", 0, 1))
+    gather(v("FBR"), v("FS"), v("TG0", 0, 1))
+    BR = v("BR", 0, 8)
+    dma("s", ("od", 0, 1, 1), v("O0"), T.od[0:1, :], T.O0[0:1, 0:8])
+    TKp, BSp, HIp, LOp, Zp, xa, xb = sm(), sm(), sm(), sm(), sm(), sm(8), sm(8)
+    tt(TK, BR, J8, A.not_equal)
+    tt(xb, BR, v("MS"), A.mult)
+    ts(v("B16"), v("BR"), 16.0, A.mult)
+    ts(v("TH8"), TK, -BIG, A.mult, BIG, A.add)
+    ts(CAP, TK, -1000.0, A.mult, 1112.0, A.add)
+    tt(xa, TK, v("MS"), A.mult)
+    red(BSp, xb)
+    gather(v("THR"), v("TH8"), v("OFT"))
+    tt(CAP, v("FBR", 0, 8), CAP, A.min)
+    red(TKp, xa)
+    sl, s0, s1 = sm(8), sm(8), sm(8)
+    ts(sl, J8, BSp, A.is_equal, 2.0, A.mult)
+    tt(KB, CAP, v("TIE8"), A.add)
+    ts(v("M32"), v("J32"), P4, A.is_equal)
+    ts(s0, sl, TKp, A.mult)
+    gather(v("TA"), BR, v("OFT"))
+    tt(s1, sl, s0, A.subtract)
+    xs = [(sm(16), out, e) for out, e in ((HIp, 68), (LOp, 69))]
+    for x16, out, e in xs:
+        tt(("SM", x16[1], x16[1] + 8, 1), s0, v("V0", e, 576, 72), A.mult)
+    for x16, out, e in xs:
+        tt(("SM", x16[1] + 8, x16[1] + 16, 1), s1, v("V0", e + 2, 576, 72), A.mult)
+    ms(v("ST4"), 0.0)
+    for x16, out, e in xs:
+        red(out, x16)
+    act(v("ZT"), v("ZB", 0, 512))
+    act(v("MT"), v("ZB", 0, 512))
+    for b, x in ((0, HIp), (1, LOp)):
+        act(v("ZT", b, 512, 4), v("DIAG"), F.Identity, scale=x)
+    ts(v("TA"), v("TA"), BSp, A.not_equal, -BIG, A.mult)
+    ts(v("OHL"), v("IREF"), LOp, A.is_equal)
+    ts(Zp, HIp, 16.0, A.mult, LOp, A.add)
+    quant(v("W2", 384, 528), v("V1"))
+    quant(v("ZQ"), v("ZT"))
+    mm(PL, v("ZWQ"), v("ZQ"))
+    for b, x in ((0, 16.0), (1, 1.0), (2, 128.0), (3, 1.0)):
+        act(v("STT", b, 512, 4), v("OHL"), F.Identity, scale=x)
+    act(v("NT"), v("ZB", 0, 512))
+    D0, D1, X0, X3, TK2 = sm(), sm(), sm(), sm(), sm()
+    ts(D0, S16, HIp, A.subtract, 8.0, A.add)
+    tt(D1, I16, LOp, A.subtract)
+    ts(X0, BSp, S16, A.subtract, TKp, A.mult)
+    ts(X3, BSp, 2.0, A.mult, TKp, A.mult)
+    ts(TK2, TKp, 2.0, A.mult)
+    ts(v("TI1"), PL, Zp, A.is_lt, TINY, A.mult)
+    ts(v("ST4", 0, 512, 4), v("QR"), Q4, A.is_equal, 4.0, A.mult)
+    ts(v("JC"), J8, 16.0, A.mult, I16, A.add)
+    tt(v("TI1"), v("TI1"), v("TA"), A.add)
+    quant(v("S4Q"), v("ST4"))
+
+    landed("W2", 128, hown[1], ("arr2", bcast))
+    landed("W2", hown[2], 256, ("arr2", bcast))
+    H = v("W2", 128, 256)
+    mm(PS, v("UQ"), H)
+    mm(PX, v("UQ"), H, True, False)
+    mm(PX, H, v("NUQ"), False, True)
+    for b in range(4):
+        mm(v("PV", 512 * b, 512 * b + 128), E[b], H)
+    for b in range(4):
+        act(v("D5", b, 512, 4), v("PV", 512 * b, 512 * b + 128))
+    tt(v("IND"), PS, v("THR"), A.is_gt)
+    op("v", lambda: g.vector.tensor_tensor_scan(ap(v("CS")), ap(v("RM")), ap(v("IND")), 0.0, A.mult, A.add), [v("RM"), v("IND")], [v("CS")])
+    for o in (0, 16):
+        tt(v("KR1", o, o + 8), v("CS", 15, 128, 16), KB, A.add)
+    pl1 = places("KR1", "KT1", "OP1")
+    t2 = sm()
+    ts(t2, pl1, -1.0, A.mult, 7.0, A.add)
+    scatter(v("BS"), v("B16"), v("OP1", 0, 1))
+    ts(v("TG1", 0, 1), t2, pl1, A.min)
+    gather_add(v("OFF3"), v("BS"), v("TG1", 0, 1), I16)
+    landed("PH1", 0, pown[1], ("arrp", 2 * (NR - 1)))
+    landed("PH1", pown[2], 128, ("arrp", 2 * (NR - 1)))
+    pick_s(v("S3"), v("PH1"), v("OFF3", 0, 8))
+    pick_c(v("S3"), v("PH1"), v("OFF3", 0, 8))
+    bown = v("W2", 16 * me, 16 * me + 16)
+    send(True, [([c], bown, v("S3", 16 * d, 16 * d + 16), 1 << engs[i], "arr3") for i, (d, c) in enumerate(zip(others, oc_))])
+    send(False, [([c], v("W2s", bown[1], bown[2]), v("S3s", 16 * d, 16 * d + 16), 1 << engs[i], "arr3") for i, (d, c) in enumerate(zip(others, oc_))])
+
+    Mp, T1, PTm, fm = sm(), sm(), sm(), sm()
+    c1, c2, nw, nk, sel, G, r1, D2, Y0, D3, fl = sm(), sm(), sm(), sm(), sm(), sm(8), sm(), sm(), sm(), sm(), sm(8)
+    am = v("A1", me, me + 1)
+    tt(v("CM1"), PX, v("TI1"), A.is_lt)
+    scatter(v("O1"), J16, v("OP1", 0, 1))
+    ts(v("OFFO", 0, 1), v("OFF3", me, me + 1), 0.0, A.add)
+    red(Mp, v("CM1"))
+    ts(fm, v("OFF3", me, me + 1), I16, A.subtract, 0.0625, A.mult)
+    gather(v("A1"), v("O1"), v("TG1", 0, 1))
+    dma("s", ("od", 0, 1, 1), v("O1"), T.od[1:2, :], T.O1[0:1, 0:8])
+    ts(v("MT", 0, 128, 4), v("M32"), Mp, A.mult, 16.0, A.min)
+    ts(T1, am, float(me), A.not_equal)
+    tt(PTm, am, fm, A.not_equal)
+    quant(v("MQ"), v("MT"))
+    mm(PL, v("S4Q"), v("MQ"))
+    tt(c1, T1, PTm, A.mult)
+    pick_c(bown, v("PH1"), v("OFFO", 0, 1))
+    pick_s(bown, v("PH1"), v("OFFO", 0, 1))
+    tt(c2, T1, c1, A.subtract)
+    ts(r1, Mp, 15.5, A.is_lt, c1, A.mult)
+    ts(v("OFFG"), v("PC", 0, 32), Q4, A.add)
+    ts(nw, c2, PTm, A.add, -1.0, A.add)
+    ts(Y0, X0, c2, A.mult, D0, A.add)
+    op("v", lambda: g.vector.tensor_tensor(ap(v("VT")), ap(v("NZ1", 0, 72)).indirect(ap(v("OFFG"))), ap(v("D5")), A.add),
+       [v("NZ1", 0, 72), v("OFFG"), v("D5")], [v("VT")])
+    ts(nk, TKp, nw, A.mult, 1.0, A.add)
+    ts(D3, X3, c2, A.mult)
+    ts(D2, TK2, c2, A.mult, r1, A.add)
+    ts(sel, BSp, fm, A.is_equal, nk, A.mult)
+    quant(v("W2", 256, 384), v("VT"))
+    ts(G, J8, HIp, A.is_equal, sel, A.mult)
+    quant(v("STQ"), v("STT"))
+    for b, x in enumerate((Y0, D1, D2, D3)):
+        ts(v("NT", b, 32, 4), G, x, A.mult)
+    quant(v("NTQ"), v("NT"))
+    mm(v("PD", 0, 128), v("STQ"), v("NTQ"))
+    quant(v("WQ"), v("WT"))
+    tt(fl, v("PD", 0, 8), v("JC"), A.add)
+    cp(v("OFFF"), fl)
+
+    landed("W2", 0, bown[1], ("arr3", 2 * (NR - 1)))
+    landed("W2", bown[2], 128, ("arr3", 2 * (NR - 1)))
+    pick_c(v("FT"), v("W2"), v("OFFF"))
+    pick_s(v("FT"), v("W2"), v("OFFF"))
+    dma("s", ("oc", 0, 1, 1), v("FT"), T.oc[:, :], codes(v("FT")))
+    mm(PS, v("WQ"), v("FT"))
+    for k in range(4):
+        dma("a", ("osc", 0, 1, 1), v("FTs"), T.osc[4 * k:4 * k + 4, :], T.FTs[32 * k:32 * k + 4, 0:128])
+    cp(v("Y"), PS)
+    dma("s", ("y", 0, 1, 1), v("Y"), T.y[:, :])
+
+    for q in ("v", "a", "t", "g"):
+        g.wait_ge(T.sem[SEM[q]], cnt[q])
+    for s, n in ends:
+        g.wait_ge(T.sem[s], n)

@@ -4,40 +4,30 @@ from concourse.mybir import dt, AluOpType, AxisListType, ActivationFunctionType
 A = AluOpType
 F = ActivationFunctionType
 NR, SL = 8, 18
-ROWS = {"KR": 32, "KT": 32, "KR1": 32, "KT1": 32, "FS": 16, "FBR": 16, "BR": 16, "B16": 16, "BS": 16, "A1": 16, "F16": 16, "J18": 16}
-RN = list(ROWS)
-TINY, BIG = 2.0 ** -100, 1e29
+TINY, BIG, MK, RND = 2.0 ** -100, 1e29, 256.0, 2.0 ** 27
 
 _f, _b, _u = "float32", "bfloat16", "uint16"
-
-
-def _mx(d, name, n):
-    d[name] = ("sbuf", [128, n], "float8_e4m3fn_x4")
-    d[name + "s"] = ("sbuf", [128, n], "uint8")
-
-
 SCRATCH = {}
 for _n, _w, _t in (
-        ("TB", 512, _b), ("UC", 4, _b), ("NUC", 4, _b), ("NZ", 128, _b), ("WT", 512, _b), ("ZB", 576, _b), ("UT", 512, _b), ("NU", 512, _b),
-        ("CI", 8, "int32"), ("CF", 8, _f), ("CK", 16, _f), ("J32", 32, _f), ("KI", 128, _b), ("IREF", 128, _b), ("OH2", 256, _b),
-        ("OHREF", 512, _b), ("QR", 128, _b), ("ZE", 520, _b), ("TIE", 128, _f), ("DIAG", 128, _f), ("RM", 128, _f),
-        ("M32", 32, _f), ("MS", 8, _f), ("JC", 8, _f), ("TIE8", 8, _f), ("WN", 32, _f), ("O0", 16, _f), ("O1", 16, _f),
-        ("MVC", 512, _b), ("ONE", 512, _b), ("ZW", 512, _b), ("ST4", 512, _b), ("NT0", 576, _b), ("NT1", 576, _b),
-        ("INFO", 512, _b), ("OHT", 512, _b), ("CMP", 128, _f), ("SM", 384, _f), ("R32", 32 * len(ROWS), _f),
-        ("V0", 576, _b), ("V1", 576, _b), ("NZ1", 80, _f), ("TH8", 8, _f), ("THR", 128, _f), ("ZT", 512, _b),
+        ("TB", 512, _b), ("UC", 4, _b), ("NZ", 128, _b), ("WT", 512, _b), ("ZB", 576, _b), ("UT", 512, _b), ("NU", 512, _b),
+        ("CI", 8, "int32"), ("CF", 8, _f), ("CK", 96, _f), ("J32", 32, _f), ("KI", 128, _b), ("IREF", 128, _b), ("OH2", 256, _b),
+        ("OHREF", 512, _b), ("QR", 128, _b), ("ZE", 520, _b), ("TIE", 128, _f), ("DIAG", 128, _b), ("RM", 128, _f),
+        ("M32", 32, _f), ("C256", 256, _b), ("MASK", 256, _b), ("OXI", 16, _f),
+        ("MVC", 512, _b), ("S1", 512, _b), ("ZW", 512, _b), ("SC", 512, _b), ("NT0", 576, _b), ("NT1", 576, _b),
+        ("INFO", 512, _b), ("OHT", 512, _b), ("CMP", 128, _f), ("SM", 1280, _f),
+        ("V0", 576, _b), ("V1", 576, _b), ("NZ1", 80, _f), ("ZT", 512, _b), ("XT", 512, _b),
         ("TI1", 128, _f), ("TA", 128, _f), ("IND", 128, _f), ("CS", 128, _f),
-        ("D5", 512, _f), ("MT", 512, _b), ("VT", 512, _b), ("OHL", 128, _b), ("STT", 512, _b), ("NT", 512, _b), ("Y", 128, _f), ("CM1", 128, _f),
-        ("OFF1", 4, _u), ("OFFH", 18, _u), ("OFF3", 16, _u), ("OP0", 2, _u), ("OP1", 2, _u), ("OX0", 2, _u), ("TG0", 2, _u), ("TG1", 2, _u),
-        ("OFFO", 2, _u), ("OFFG", 32, _u), ("OFFF", 8, _u), ("OFT", 8, _u)):
+        ("D5", 512, _f), ("MT", 512, _b), ("VT", 512, _b), ("Y", 128, _f), ("CM1", 128, _f), ("OF", 256, _u)):
     SCRATCH[_n] = ("sbuf", [128, _w], _t)
-for _n, _w in (("UQ", 128), ("NUQ", 128), ("TQ", 128), ("MVQ", 128), ("OHQ", 128), ("ONQ", 128), ("EQ", 512), ("N0Q", 144), ("N1Q", 144),
-               ("WQ", 128), ("ZWQ", 128), ("S4Q", 128), ("L1S", 144), ("LD1", 144), ("NB", 160), ("W2", 528), ("PH1", 128), ("S3", 128),
-               ("ZQ", 128), ("MQ", 128), ("STQ", 128), ("NTQ", 128), ("FT", 128), ("HT", 128)):
-    _mx(SCRATCH, _n, _w)
+for _n, _w in (("UQ", 128), ("NUQ", 128), ("TQ", 128), ("MVQ", 128), ("OHQ", 128), ("S1Q", 128), ("EQ", 512), ("N0Q", 144), ("N1Q", 144),
+               ("WQ", 128), ("ZWQ", 128), ("SCQ", 128), ("L1S", 144), ("LD1", 144), ("NB", 160), ("W2", 416), ("PH1", 128), ("PG", 128),
+               ("S3", 96), ("W3", 160), ("ZQ", 128), ("MQ", 128), ("XQ", 128), ("FT", 128), ("HT", 128)):
+    SCRATCH[_n] = ("sbuf", [128, _w], "float8_e4m3fn_x4")
+    SCRATCH[_n + "s"] = ("sbuf", [128, _w], "uint8")
 for _n, _w in (("PV", 2048), ("PA", 512), ("PB", 512), ("PC", 512), ("PD", 512)):
     SCRATCH[_n] = ("psum", [128, _w], _f)
 
-SEMAPHORES = ["sv", "sa", "st", "sg", "arrh", "arrg", "arr1", "arr2", "arr3", "arrp"]
+SEMAPHORES = ["sv", "sa", "st", "sg", "arrh", "arrg", "arr1", "arr2", "arr3", "arrp", "arrx"]
 SEMAPHORES += ["d%d" % i for i in range(24)] + ["l%d" % i for i in range(12)]
 
 
@@ -119,9 +109,8 @@ def rank_program(g, core, T, topo):
                     acc.setdefault(n, []).append((lo, hi, st, w, q, tok, dma))
 
     def v(n, lo=0, hi=None, st=1):
-        if n in ROWS:
-            o = 32 * RN.index(n)
-            return ("R32", o + lo, o + (ROWS[n] if hi is None else hi), st)
+        if isinstance(n, tuple):
+            return (n[0], n[1] + lo, n[2] if hi is None else n[1] + hi, st)
         return (n, lo, SCRATCH[n][1][1] if hi is None else hi, st)
 
     def ap(x):
@@ -136,39 +125,40 @@ def rank_program(g, core, T, topo):
     def sc(x):
         return ap(x) if isinstance(x, tuple) else x
 
-    def ts(out, in0, s1, op0, s2=None, op1=None):
-        rd = [in0] + [s for s in (s1, s2) if isinstance(s, tuple)]
+    def ts(out, in0, s1, op0, s2=None, op1=None, off=None):
+        rd = [in0] + [s for s in (s1, s2, off) if isinstance(s, tuple)]
+        a = ap(in0) if off is None else ap(in0).indirect(ap(off))
         if op1 is None:
-            op("v", lambda: g.vector.tensor_scalar(ap(out), ap(in0), sc(s1), None, op0), rd, [out])
+            op("v", lambda: g.vector.tensor_scalar(ap(out), a, sc(s1), None, op0), rd, [out])
         else:
-            op("v", lambda: g.vector.tensor_scalar(ap(out), ap(in0), sc(s1), sc(s2), op0, op1), rd, [out])
+            op("v", lambda: g.vector.tensor_scalar(ap(out), a, sc(s1), sc(s2), op0, op1), rd, [out])
 
-    def tt(out, a, b, o):
-        op("v", lambda: g.vector.tensor_tensor(ap(out), ap(a), ap(b), o), [a, b], [out])
+    def tt(out, a, b, o, off=None):
+        x = ap(a) if off is None else ap(a).indirect(ap(off))
+        op("v", lambda: g.vector.tensor_tensor(ap(out), x, ap(b), o), [a, b] + ([off] if off else []), [out])
 
-    def red(out, a):
-        op("v", lambda: g.vector.tensor_reduce(ap(out), ap(a), AxisListType.X, A.add), [a], [out])
+    def red(out, a, o=A.add, neg=False):
+        op("v", lambda: g.vector.tensor_reduce(ap(out), ap(a), AxisListType.X, o, negate=neg), [a], [out])
 
     def cp(out, a):
         op("v", lambda: g.vector.tensor_copy(ap(out), ap(a)), [a], [out])
-
-    def tr(out, a):
-        op("v", lambda: g.vector.transpose(ap(out), ap(a)), [a], [out])
 
     def ms(out, c):
         op("v", lambda: g.vector.memset(ap(out), c), [], [out])
 
     def act(out, a, fn=F.Copy, **kw):
         k2 = {k: sc(x) for k, x in kw.items()}
-        op("a", lambda: g.scalar.activation(ap(out), ap(a), fn, **k2), [a] + [x for x in kw.values() if isinstance(x, tuple)], [out])
+        op("a", lambda: g.scalar.activation(ap(out), ap(a), fn, **k2),
+           [a] + [x for k, x in kw.items() if isinstance(x, tuple) and k != "accum_out"], [out] + [x for k, x in kw.items() if k == "accum_out"])
+
+    def pl(x):
+        return (x[0] + "s", x[1], x[2], 1)
 
     def quant(out, in_):
-        o2 = v(out[0] + "s", out[1], out[2])
-        op("v", lambda: g.vector.quantize_mx(ap(out), ap(o2), ap(in_)), [in_], [out, o2])
+        op("v", lambda: g.vector.quantize_mx(ap(out), ap(pl(out)), ap(in_)), [in_], [out, pl(out)])
 
     def mm(out, w, x, start=True, stop=True):
-        ws, xs = v(w[0] + "s", w[1], w[2]), v(x[0] + "s", x[1], x[2])
-        op("t", lambda: g.tensor.matmul_mx(ap(out), ap(w), ap(ws), ap(x), ap(xs), start, stop), [w, ws, x, xs], [out])
+        op("t", lambda: g.tensor.matmul_mx(ap(out), ap(w), ap(pl(w)), ap(x), ap(pl(x)), start, stop), [w, pl(w), x, pl(x)], [out])
 
     def scatter(out, in_, off):
         op("v", lambda: g.vector.tensor_copy(ap(out).indirect(ap(off)), ap(in_)), [in_, off], [out])
@@ -176,15 +166,9 @@ def rank_program(g, core, T, topo):
     def gather(out, win, off):
         op("v", lambda: g.vector.tensor_copy(ap(out), ap(win).indirect(ap(off))), [win, off], [out])
 
-    def gather_add(out, win, off, col):
-        op("v", lambda: g.vector.tensor_scalar(ap(out), ap(win).indirect(ap(off)), ap(col), None, A.add), [win, off, col], [out])
-
-    def pick_c(out, win, off):
+    def pick(out, win, off):
+        op("a", lambda: g.scalar.activation(ap(pl(out)), ap(pl(win)).indirect(ap(off)), F.Copy), [pl(win), off], [pl(out)])
         op("v", lambda: g.vector.tensor_copy(ap(out).bitcast(dt.uint32), ap(win).bitcast(dt.uint32).indirect(ap(off))), [win, off], [out])
-
-    def pick_s(out, win, off):
-        out, win = v(out[0] + "s", out[1], out[2]), v(win[0] + "s", win[1], win[2])
-        op("a", lambda: g.scalar.activation(ap(out), ap(win).indirect(ap(off)), F.Copy), [win, off], [out])
 
     def dma(q, out, in_, oap=None, iap=None):
         waits(q, [in_], [out], True)
@@ -199,10 +183,10 @@ def rank_program(g, core, T, topo):
 
     def landed(n, lo, hi, tok):
         if hi > lo:
-            for m in (n, n + "s"):
-                note("-", [], [v(m, lo, hi)], tok, True)
+            note("-", [], [v(n, lo, hi), v(n + "s", lo, hi)], tok, True)
 
     def send(x, transfers):
+        transfers = [t if x else (t[0], pl(t[1]), pl(t[2]), t[3], t[4]) for t in transfers]
         waits("g", [t[2] for t in transfers], [], True)
         s, n = "l%d" % nl[0], 0
         nl[0] += 1
@@ -216,25 +200,31 @@ def rank_program(g, core, T, topo):
         note("g", [t[2] for t in transfers], [], (s, n), True)
         ends.append((s, n))
 
-    others = [(me + i) % NR for i in range(1, NR)]
-    oc_ = [T.cores[d] for d in others]
+    oc_ = [T.cores[(me + i) % NR] for i in range(1, NR)]
     helper = _helper_of(topo, core)
     engs = topo.engines(core, oc_[0])
+    ne = len(engs)
     m_all = topo.mask(core, oc_[0])
     m_help = topo.mask(core, helper)
     m_far = m_help & ~m_all
-    bcast = 2 * len(engs) * (NR - 1)
+    bcast = 2 * ne * (NR - 1)
+    par, k4 = me % 2, me // 2
 
-    smn = [0]
+    top = {"SM": 0, "CK": 0, "OF": 0}
+
+    def new(n, w, al):
+        lo = (top[n] + al - 1) // al * al
+        top[n] = lo + w
+        return (n, lo, lo + w, 1)
 
     def sm(n=1):
-        smn[0] += n
-        return ("SM", smn[0] - n, smn[0], 1)
+        return new("SM", n, 8 if n >= 8 else 1)
 
-    dma("s", v("TB"), v("TB"), None, T.tb[:, :])
-    dma("a", v("UC"), v("UC"), None, T.u[:, 0:4])
-    dma("a", v("NZ"), v("NZ"), None, T.nz[:, :])
-    dma("s", v("WT"), v("WT"), None, T.w[:, :])
+    def ck(n=1):
+        return new("CK", n, 8 if n >= 8 else 1)
+
+    def of(n=1):
+        return new("OF", n, 2)
 
     def iota(out, pattern, mult, small=True, base=0):
         if small:
@@ -242,283 +232,310 @@ def rank_program(g, core, T, topo):
         else:
             op("g", lambda: g.iota(ap(out), pattern, base, mult), [], [out])
 
+    dma("s", v("TB"), v("TB"), None, T.tb[:, :])
+    dma("a", v("UC"), v("UC"), None, T.u[:, 0:4])
+    dma("a", v("NZ"), v("NZ"), None, T.nz[:, :])
+    dma("s", v("WT"), v("WT"), None, T.w[:, :])
     iota(v("CI", 0, 1), [[0, 1]], 1, False)
-    iota(v("KI"), [[1, 128]], 0)
     iota(v("OH2"), [[0, 8], [1, 16], [16, 2]], 0)
+    iota(v("KI"), [[1, 128]], 0)
     iota(v("J32"), [[1, 32]], 0)
     iota(v("IREF"), [[0, 8], [1, 16]], 0)
 
-    ms(v("ZB"), 0.0)
-    act(v("MVC"), v("ZB", 0, 512))
-    ci, cf, ck = (lambda i: v("CI", i, i + 1)), (lambda i: v("CF", i, i + 1)), (lambda i: v("CK", i, i + 1))
+    ci, cf = (lambda i: v("CI", i, i + 1)), (lambda i: v("CF", i, i + 1))
     J8, J16 = v("J32", 0, 8), v("J32", 0, 16)
+    ms(v("ZB"), 0.0)
     ts(ci(1), ci(0), 15, A.bitwise_and)
     ts(ci(2), ci(0), 4, A.logical_shift_right)
-    ts(ci(4), ci(0), 3, A.bitwise_and)
-    ts(ci(5), ci(0), 2, A.logical_shift_right)
-    ts(ci(3), ci(0), 31, A.bitwise_and)
-    cp(v("CF", 0, 6), v("CI", 0, 6))
-    P, I16, S16, Q4, P4 = cf(0), cf(1), cf(2), cf(4), cf(5)
+    ts(ci(3), ci(0), 3, A.bitwise_and)
+    ts(ci(4), ci(0), 2, A.logical_shift_right)
+    ts(ci(5), ci(0), 1, A.bitwise_and)
+    ts(ci(6), ci(0), 1, A.logical_shift_right)
+    ms(v("MVC"), 0.0)
+    ts(ci(7), ci(6), k4 + 1, A.add)
+    cp(v("CF", 0, 7), v("CI", 0, 7))
+    P, I16, S16, Q4, P4, Q2 = cf(0), cf(1), cf(2), cf(3), cf(4), cf(5)
+    ms(v("INFO"), 0.0)
+    H16, P32, ia, ib = ck(), ck(), ck(), ck()
+    ts(H16, S16, 16.0, A.mult)
+    ts(P32, P, 32.0, A.add)
+    ts(ia, P, float(me), A.is_equal, MK, A.mult)
+    ts(ib, P, float(me + 16), A.is_equal, -0.125, A.mult)
     ts(v("TIE"), v("KI"), P, A.is_lt, TINY, A.mult)
+    tt(v("INFO", 3, 4), ia, ib, A.add)
     for h in range(2):
         act(v("OHREF", h, 512, 2), v("OH2"))
-    ts(ck(1), S16, 16.0, A.mult)
-    for e, x in ((0, ck(1)), (1, I16), (10, ck(1)), (11, I16), (16, S16), (21, I16), (26, S16), (31, I16)):
-        act(v("MVC", e, e + 1), x)
-
-    ts(v("NUC"), v("UC"), -1.0, A.mult)
     for b in range(4):
+        ts(v("NU", b, 512, 4), v("ZB", 0, 128), v("UC", b, b + 1), A.subtract)
+    for b in range(2):
         ts(v("UT", b, 512, 4), v("ZB", 0, 128), v("UC", b, b + 1), A.add)
-        act(v("NU", b, 512, 4), v("ZB", 0, 128), F.Identity, bias=v("NUC", b, b + 1))
-    act(v("INFO"), v("ZB", 0, 512))
+        act(v("UT", b + 2, 512, 4), v("ZB", 0, 128), F.Identity, bias=v("UC", b + 2, b + 3))
+    for e, st, x in ((0, 10, H16), (1, 10, I16), (16, 6, H16), (25, 6, I16)):
+        act(v("MVC", e, e + st + 1, st), v("ZB", 0, 2), F.Identity, bias=x)
     act(v("ZE"), v("ZB", 0, 520))
+    for t in (1, 0):
+        n = "NT%d" % t
+        for b in range(8):
+            act(v(n, 64 + b, 576, 72), v("ZB", 0, 8))
+        for a in range(NR):
+            act(v(n, 72 * a, 72 * a + 64), v("NZ", 64 * t, 64 * t + 64))
+        if t == 1:
+            break
 
     TQ = v("TQ")
+    quant(v("NUQ"), v("NU"))
     quant(TQ, v("TB"))
     send(True, [([helper], v("HT"), TQ, m_help, "arrh")])
     quant(v("UQ"), v("UT"))
-    quant(v("NUQ"), v("NU"))
     PX, PS, PL, PF = v("PA", 0, 128), v("PB", 0, 128), v("PC", 0, 128), v("PD", 0, 144)
-    mm(PX, v("UQ"), TQ, True, False)
-    mm(PX, TQ, v("NUQ"), False, True)
+    mm(PX, TQ, v("NUQ"), True, False)
+    mm(PX, v("UQ"), TQ, False, True)
     mm(PS, TQ, v("UQ"))
     quant(v("MVQ"), v("MVC"))
-    rk = sm()
+    rk, va, vb, OFF1 = sm(), sm(), sm(), of(4)
     tt(v("CMP"), PX, v("TIE"), A.is_lt)
+    ts(v("INFO", 0, 1), v("PB", 0, 1), 0.0, A.is_gt)
     red(rk, v("CMP"))
     ts(v("OHT"), v("OHREF"), rk, A.is_equal)
+    ts(va, rk, 31.5, A.is_ge, 1000.0, A.mult)
     quant(v("OHQ"), v("OHT"))
-    ts(v("INFO", 0, 1), v("PB", 0, 1), 0.0, A.is_gt)
+    ts(vb, va, rk, A.add, P32, A.min)
     mm(PL, v("OHQ"), v("MVQ"))
-    cp(v("OFF1"), v("PC", 0, 4))
+    ts(v("INFO", 1, 2), vb, RND, A.add, RND, A.subtract)
+    tt(v("INFO", 2, 3), vb, v("INFO", 1, 2), A.subtract)
+    cp(OFF1, v("PC", 0, 4))
     cp(v("INFO", 4, 8), v("PC", 4, 8))
-    pick_s(v("L1S", 0, 16), TQ, v("OFF1", 0, 1))
-    pick_c(v("L1S", 0, 16), TQ, v("OFF1", 0, 1))
+    pick(v("L1S", 0, 16), TQ, v(OFF1, 0, 1))
     quant(v("L1S", 16, 144), v("INFO"))
-    own = v("LD1", SL * me, SL * me + SL)
-    send(True, [(oc_, own, v("L1S", 0, SL), m_all, "arr1")])
-    send(False, [(oc_, v("LD1s", own[1], own[2]), v("L1Ss", 0, SL), m_all, "arr1")])
-    send(False, [([helper], v("HTs"), v("TQs"), m_far, "arrg")])
-    dma("s", own, v("L1S", 0, SL), codes(own), codes(v("L1S", 0, SL)))
-    dma("s", v("LD1s", own[1], own[2]), v("L1Ss", 0, SL))
-    pown = v("PH1", 16 * me, 16 * me + 16)
-    town = v("TQ", 16 * me, 16 * me + 16)
+    own, mine = v("LD1", SL * me, SL * me + SL), v("L1S", 0, SL)
+    for x in (True, False):
+        send(x, [(oc_, own, mine, m_all, "arr1")])
+    send(False, [([helper], v("HT"), TQ, m_far, "arrg")])
+    dma("s", own, mine, codes(own), codes(mine))
+    dma("s", pl(own), pl(mine))
+    pown, town = v("PH1", 16 * me, 16 * me + 16), v("TQ", 16 * me, 16 * me + 16)
     dma("s", pown, town, codes(pown), codes(town))
-    dma("s", v("PH1s", pown[1], pown[2]), v("TQs", town[1], town[2]))
-    pick_s(v("NB", 144, 160), TQ, v("OFF1", 2, 3))
-    pick_c(v("NB", 144, 160), TQ, v("OFF1", 2, 3))
+    dma("s", pl(pown), pl(town))
 
-    for n in ("KR", "KR1"):
-        iota(v(n), [[0, 2], [-1, 16]], 0, True, 7)
     iota(v("QR"), [[0, 8], [1, 4], [0, 4]], 0)
+    iota(v("C256"), [[0, 8], [1, 8], [0, 4]], 0)
+    iota(v("OXI"), [[72, 8], [0, 2]], 0, True, 64)
     ts(v("ZE", 4, 516, 4), v("KI"), P, A.is_equal, 0.5, A.mult)
-    ts(v("TIE8"), J8, -0.125, A.mult, 0.875, A.add)
-    for b in range(4):
-        quant(v("EQ", 128 * b, 128 * b + 128), v("ZE", 4 - b, 516 - b))
+    quant(v("N1Q"), v("NT1"))
+    for b in range(8):
+        act(v("NT0", 64 + b, 576, 72), v("ZB", 0, 8))
+    for a in range(NR):
+        act(v("NT0", 72 * a, 72 * a + 64), v("NZ", 0, 64))
     E = [v("EQ", 128 * b, 128 * b + 128) for b in range(4)]
-    for t in (0, 1):
-        n = "NT%d" % t
-        act(v(n), v("ZB"))
-        for a in range(NR):
-            act(v(n, 72 * a, 72 * a + 64), v("NZ", 64 * t, 64 * t + 64))
-        quant(v("N%dQ" % t), v(n))
-        if t == 0:
-            act(v("ONE"), v("ZB", 0, 512))
-            ms(v("ONE", 0, 512, 4), 1.0)
-            ts(v("J18"), J16, float(SL), A.mult)
-            ms(v("WN", 16, 32), float(SL * NR))
-            quant(v("ONQ"), v("ONE"))
     PVb = [v("PV", 512 * b, 512 * b + 144) for b in range(4)]
     for b in range(4):
+        quant(E[b], v("ZE", 4 - b, 516 - b))
         mm(PVb[b], E[b], v("N1Q"))
+    ct, TIE8, TM0, TM1, TMP, c8, CB, C2, C3, EP, Q22, Q8, THM = ck(), ck(8), ck(8), ck(8), ck(8), ck(), ck(), ck(2), ck(), ck(), ck(), ck(), ck(8)
+    ms(v("S1"), 0.0)
+    ts(ct, P, -16.0, A.add, 0.0, A.max)
     ms(v("NZ1", 64, 80), 0.0)
+    ms(v("S1", 0, 512, 4), 1.0)
+    ts(v("S1", 3, 512, 4), v("IREF"), P, A.is_equal, ct, A.add)
     for b in range(4):
         act(v("NZ1", b, 64, 4), v("PV", 512 * b, 512 * b + 16))
+    quant(v("N0Q"), v("NT0"))
     for b in range(4):
         mm(PVb[b], E[b], v("N0Q"), True, False)
-    ms(v("F16"), 0.0)
-    ts(v("OFT"), J8, 0.0, A.add)
+    WN, J18, F16, JB, FLW = sm(96), sm(16), sm(16), sm(32), sm(32)
+    ts(c8, I16, 8.0, A.mult, -48.0, A.add)
+    ts(J18, J16, float(SL), A.mult)
+    ms(v(WN, 8, 16), float(SL * NR))
+    quant(v("S1Q"), v("S1"))
+    ts(CB, I16, 7.5, A.is_gt, c8, A.mult)
+    pick(v("NB", 144, 160), TQ, v(OFF1, 2, 3))
+    pick(v("W2", 400, 416), TQ, v(OFF1, 0, 1))
+    ts(TIE8, J8, -0.125, A.mult)
+    ts(ci(7), ci(7), 3, A.bitwise_and)
+    ts(TM0, J8, I16, A.is_equal, MK, A.mult)
+    ms(F16, 0.0)
+    ts(v(C2, 0, 1), CB, 2.0, A.mult, 7.0, A.add)
+    ts(v(C2, 1, 2), CB, 2.0, A.mult, 167.0, A.add)
+    ts(EP, ci(7), 2.0, A.mult, float(par), A.add)
+    ts(C3, I16, 7.5, A.is_gt, Q2, A.mult)
+    tt(TM0, TM0, TIE8, A.add)
+    ts(TMP, TIE8, MK, A.add)
+    ts(EP, EP, I16, A.subtract)
+    ts(C3, C3, 80.0, A.mult, 3.5, A.add)
+    ts(Q22, Q2, 2.0, A.mult)
+    ts(EP, I16, 7.5, A.is_gt, EP, A.mult)
     ts(v("RM"), v("IREF"), 0.0, A.is_gt)
-    ts(v("MS"), J8, S16, A.is_equal)
-    ms(v("ZW"), 0.0)
+    ts(TM1, J8, EP, A.subtract, I16, A.is_equal)
+    ms(v("ZW"), 1.0)
+    ts(TM1, TM1, MK, A.mult)
     ts(v("DIAG"), v("KI"), P, A.is_equal)
-    for b, x in ((0, 16.0), (1, 1.0)):
-        ms(v("ZW", b, 512, 4), x)
+    tt(TM1, TM1, TIE8, A.add)
     quant(v("ZWQ"), v("ZW"))
+    act(v("SC"), v("ZB", 0, 512))
+    act(v("ZT"), v("ZB", 0, 512))
+    act(v("XT", 256, 512), v("ZB", 0, 256))
+    act(v("MT"), v("ZB", 0, 512))
+    OFT, OFG, OFX = of(8), of(), of(16)
+    ts(OFT, J8, 0.0, A.add)
+    ts(OFG, S16, 0.0, A.add)
+    ts(OFX, v("OXI"), Q4, A.add)
+    cp(v(JB, 0, 16), J16)
+    ts(v("MASK"), v("C256"), S16, A.is_equal)
+    ts(v("SC", 0, 512, 4), v("QR"), Q4, A.is_equal, 4.0, A.mult)
+    for b in (1, 2):
+        ts(v("SC", b, 512, 4), v("IREF"), I16, A.is_equal, 2.0, A.mult)
+    ms(v("MASK", 0, 256, 4), 0.0)
+    quant(v("SCQ"), v("SC"))
 
     landed("LD1", 0, own[1], ("arr1", bcast))
     landed("LD1", own[2], 144, ("arr1", bcast))
-    mm(PF, v("ONQ"), v("LD1"))
+    mm(PF, v("S1Q"), v("LD1"))
     for b in range(4):
         mm(PVb[b], E[b], v("LD1"), False, True)
     for b in range(4):
         act(v("V0", b, 576, 4), PVb[b])
     FIT = v("PD", 16, 144, SL)
-
-    def places(kr, kt, off):
-        pl, c16 = sm(), sm(16)
-        tr(v(kt), v(kr))
-        ts(c16, v(kr, 0, 16), v(kt, 0, 1), A.is_gt)
-        red(pl, c16)
-        ts(v(off, 0, 1), pl, 0.0, A.add)
-        return pl
-
-    for o in (0, 16):
-        tt(v("KR", o, o + 8), FIT, v("TIE8"), A.add)
-    pl0 = places("KR", "KT", "OP0")
-    gv = sm()
-    ts(gv, pl0, 3.5, A.is_lt, 16.0, A.mult)
-    scatter(v("WN", 0, 16), v("J18"), v("OP0", 0, 1))
-    ts(v("OX0", 0, 1), gv, pl0, A.subtract, 7.0, A.add)
-    sh = me % 2
-    gather_add(v("OFFH", sh, sh + 16), v("WN"), v("OX0", 0, 1), I16)
-    oh = v("OFFH", me + sh, me + sh + 1)
+    mx, cm, p1, gv, t1, O0 = sm(), sm(8), sm(), sm(), sm(), sm(96)
+    OP0, OX0, TG0, OFFH = of(), of(), of(), of(18)
+    red(mx, FIT, A.max)
+    tt(v(F16, 0, 8), FIT, TM0, A.subtract)
+    ts(cm, FIT, MK, A.add, mx, A.is_gt)
+    red(p1, cm)
+    ts(OP0, p1, CB, A.add, -1.0, A.add)
+    ts(gv, p1, 4.5, A.is_lt, 8.0, A.mult)
+    ts(t1, p1, -1.0, A.mult, 9.0, A.add)
+    scatter(WN, J18, OP0)
+    ts(OX0, gv, p1, A.subtract, 8.0, A.add)
+    scatter(O0, J16, OP0)
+    ts(v(OFFH, par, par + 16), WN, I16, A.add, off=OX0)
+    ts(TG0, p1, t1, A.min, -1.0, A.add)
     quant(v("NB", 0, 144), v("V0"))
-    hown = v("W2", 128 + 16 * me, 144 + 16 * me)
-    pick_c(hown, v("NB"), oh)
-    pick_s(hown, v("NB"), oh)
-    hos = v("W2s", hown[1], hown[2])
-    send(True, [(oc_, hown, hown, m_all, "arr2")])
-    send(False, [(oc_, hos, hos, m_all, "arr2")])
+    OFE = of(4)
+    ts(OFE, v(O0, 0, 4), 16.0, A.mult, I16, A.add)
+    hown = v("W2", 16 * me, 16 * me + 16)
+    pick(hown, v("NB"), v(OFFH, me + par, me + par + 1))
+    for x in (True, False):
+        send(x, [(oc_, hown, hown, m_all, "arr2")])
 
+    landed("PH1", 0, pown[1], ("arrp", 2 * (NR - 1)))
+    landed("PH1", pown[2], 128, ("arrp", 2 * (NR - 1)))
+    gown = v("PG", 64 * par, 64 * par + 64)
+    BR16, FS, FB, TP, B32 = v(JB, 16, 32), sm(96), sm(16), sm(16), sm(32)
+    BR = v(JB, 16, 24)
+    gather(BR16, O0, TG0)
+    pick(gown, v("PH1"), OFE)
+    for x in (True, False):
+        send(x, [([T.cores[me ^ 1]], gown, gown, m_all, "arrx")])
     for b in range(4):
         mm(PVb[b], E[b], v("N1Q"), True, False)
         mm(PVb[b], E[b], v("LD1"), False, True)
+    dma("s", ("od", 0, 1, 1), O0, T.od[0:1, :], T.SM[0:1, O0[1]:O0[1] + 8])
+    G, z1, ZR, DG, BSp, Zp, cc, m1, f2, KB, KBm, KBp, FLA = sm(8), sm(8), sm(8), sm(16), sm(16), sm(), sm(8), sm(8), sm(8), sm(8), sm(8), sm(8), sm(64)
+    LZ = of(16)
+    scatter(FS, F16, OP0)
+    tt(G, BR, J8, A.is_equal)
+    ts(z1, BR, 72.0, A.mult, 68.0, A.add)
+    gather(BSp, BR, OFG)
+    gather(FB, FS, TG0)
+    tt(ZR, z1, G, A.add)
+    ts(cc, G, -16.0, A.mult, 112.0, A.add)
+    gather(TP, J16, TG0)
+    ts(LZ, ZR, Q22, A.add, off=OFG)
+    ts(f2, v(FB, 0, 8), -16.0, A.add)
+    tt(m1, v(FB, 0, 8), cc, A.min)
+    gather(DG, v("V0"), v(LZ, 0, 1))
+    ts(v("TA"), BR, v(BSp, 0, 1), A.not_equal, -BIG, A.mult, off=OFT)
+    for b in range(2):
+        act(v("ZT", b, 512, 4), v("DIAG"), F.Identity, scale=v(DG, b, b + 1))
     for b in range(4):
         act(v("V1", b, 576, 4), PVb[b])
-    TK, t1, CAP, KB = sm(8), sm(), sm(8), sm(8)
-    ts(t1, pl0, -1.0, A.mult, 7.0, A.add)
-    cp(v("F16", 0, 8), FIT)
-    scatter(v("O0"), J16, v("OP0", 0, 1))
-    ts(v("TG0", 0, 1), t1, pl0, A.min)
-    scatter(v("FS"), v("F16"), v("OP0", 0, 1))
-    gather(v("BR"), v("O0"), v("TG0", 0, 1))
-    gather(v("FBR"), v("FS"), v("TG0", 0, 1))
-    BR = v("BR", 0, 8)
-    dma("s", ("od", 0, 1, 1), v("O0"), T.od[0:1, :], T.O0[0:1, 0:8])
-    TKp, BSp, HIp, LOp, Zp, xa, xb = sm(), sm(), sm(), sm(), sm(), sm(8), sm(8)
-    tt(TK, BR, J8, A.not_equal)
-    tt(xb, BR, v("MS"), A.mult)
-    ts(v("B16"), v("BR"), 16.0, A.mult)
-    ts(v("TH8"), TK, -BIG, A.mult, BIG, A.add)
-    ts(CAP, TK, -1000.0, A.mult, 1112.0, A.add)
-    tt(xa, TK, v("MS"), A.mult)
-    red(BSp, xb)
-    gather(v("THR"), v("TH8"), v("OFT"))
-    tt(CAP, v("FBR", 0, 8), CAP, A.min)
-    red(TKp, xa)
-    sl, s0, s1 = sm(8), sm(8), sm(8)
-    ts(sl, J8, BSp, A.is_equal, 2.0, A.mult)
-    tt(KB, CAP, v("TIE8"), A.add)
-    ts(v("M32"), v("J32"), P4, A.is_equal)
-    ts(s0, sl, TKp, A.mult)
-    gather(v("TA"), BR, v("OFT"))
-    tt(s1, sl, s0, A.subtract)
-    xs = [(sm(16), out, e) for out, e in ((HIp, 68), (LOp, 69))]
-    for x16, out, e in xs:
-        tt(("SM", x16[1], x16[1] + 8, 1), s0, v("V0", e, 576, 72), A.mult)
-    for x16, out, e in xs:
-        tt(("SM", x16[1] + 8, x16[1] + 16, 1), s1, v("V0", e + 2, 576, 72), A.mult)
-    ms(v("ST4"), 0.0)
-    for x16, out, e in xs:
-        red(out, x16)
-    act(v("ZT"), v("ZB", 0, 512))
-    act(v("MT"), v("ZB", 0, 512))
-    for b, x in ((0, HIp), (1, LOp)):
-        act(v("ZT", b, 512, 4), v("DIAG"), F.Identity, scale=x)
-    ts(v("TA"), v("TA"), BSp, A.not_equal, -BIG, A.mult)
-    ts(v("OHL"), v("IREF"), LOp, A.is_equal)
-    ts(Zp, HIp, 16.0, A.mult, LOp, A.add)
-    quant(v("W2", 384, 528), v("V1"))
+    tt(KB, m1, f2, A.max)
+    tt(Zp, v(DG, 0, 1), v(DG, 1, 2), A.add)
+    tt(v("XT", 0, 256), v("V0"), v("MASK"), A.mult, off=OFX)
     quant(v("ZQ"), v("ZT"))
     mm(PL, v("ZWQ"), v("ZQ"))
-    for b, x in ((0, 16.0), (1, 1.0), (2, 128.0), (3, 1.0)):
-        act(v("STT", b, 512, 4), v("OHL"), F.Identity, scale=x)
-    act(v("NT"), v("ZB", 0, 512))
-    D0, D1, X0, X3, TK2 = sm(), sm(), sm(), sm(), sm()
-    ts(D0, S16, HIp, A.subtract, 8.0, A.add)
-    tt(D1, I16, LOp, A.subtract)
-    ts(X0, BSp, S16, A.subtract, TKp, A.mult)
-    ts(X3, BSp, 2.0, A.mult, TKp, A.mult)
-    ts(TK2, TKp, 2.0, A.mult)
+    tt(KBm, KB, TM1, A.add)
+    tt(KBp, KB, TMP, A.add)
+    quant(v("XQ"), v("XT"))
+    mm(v("PD", 0, 128), v("SCQ"), v("XQ"))
+    act(FLA, v("PD", 0, 64))
+    ts(v(B32, 0, 16), TP, 16.0, A.mult)
+    ts(v(B32, 16, 32), TP, 16.0, A.mult, 64.0, A.add)
     ts(v("TI1"), PL, Zp, A.is_lt, TINY, A.mult)
-    ts(v("ST4", 0, 512, 4), v("QR"), Q4, A.is_equal, 4.0, A.mult)
-    ts(v("JC"), J8, 16.0, A.mult, I16, A.add)
+    ts(v("M32"), v("J32"), P4, A.is_equal)
+    ts(THM, J8, S16, A.is_equal, 16.5, A.mult)
     tt(v("TI1"), v("TI1"), v("TA"), A.add)
-    quant(v("S4Q"), v("ST4"))
+    ts(THM, THM, -1.0, A.add)
+    quant(v("W2", 256, 400), v("V1"))
+    ms(v(FLW, 0, 8), 400.0)
+    ts(v(FLW, 8, 16), J8, float(SL), A.mult, 256.0, A.add)
+    ts(v(FLW, 16, 24), J8, 16.0, A.mult)
+    ts(Q8, I16, 7.0, A.min)
+    quant(v("WQ"), v("WT"))
 
-    landed("W2", 128, hown[1], ("arr2", bcast))
-    landed("W2", hown[2], 256, ("arr2", bcast))
-    H = v("W2", 128, 256)
+    landed("W2", 0, hown[1], ("arr2", bcast))
+    landed("W2", hown[2], 128, ("arr2", bcast))
+    landed("PG", 64 - 64 * par, 128 - 64 * par, ("arrx", 2 * ne))
+    H = v("W2", 0, 128)
     mm(PS, v("UQ"), H)
     mm(PX, v("UQ"), H, True, False)
     mm(PX, H, v("NUQ"), False, True)
     for b in range(4):
         mm(v("PV", 512 * b, 512 * b + 128), E[b], H)
+    Km, Kp, nx, sj, sg, ab, Mp, BS, O1, A1 = sm(8), sm(8), sm(), sm(8), sm(), sm(), sm(), sm(160), sm(160), sm(16)
+    OP1, TG1, OFF3, OFFG = of(2), of(), of(16), of(32)
+    ts(v("IND"), PS, 0.0, A.is_gt)
+    op("v", lambda: g.vector.tensor_tensor_scan(ap(v("CS")), ap(v("RM")), ap(v("IND")), 0.0, A.mult, A.add), [v("RM"), v("IND")], [v("CS")])
+    tt(v("CM1"), PX, v("TI1"), A.is_lt)
+    tt(Km, v("CS", 15, 128, 16), KBm, A.add)
+    tt(Kp, v("CS", 15, 128, 16), KBp, A.add)
+    red(Mp, v("CM1"))
+    red(nx, Km, A.max, True)
+    act(sj, Kp, F.Sign, bias=nx, accum_out=sg)
     for b in range(4):
         act(v("D5", b, 512, 4), v("PV", 512 * b, 512 * b + 128))
-    tt(v("IND"), PS, v("THR"), A.is_gt)
-    op("v", lambda: g.vector.tensor_tensor_scan(ap(v("CS")), ap(v("RM")), ap(v("IND")), 0.0, A.mult, A.add), [v("RM"), v("IND")], [v("CS")])
-    for o in (0, 16):
-        tt(v("KR1", o, o + 8), v("CS", 15, 128, 16), KB, A.add)
-    pl1 = places("KR1", "KT1", "OP1")
-    t2 = sm()
-    ts(t2, pl1, -1.0, A.mult, 7.0, A.add)
-    scatter(v("BS"), v("B16"), v("OP1", 0, 1))
-    ts(v("TG1", 0, 1), t2, pl1, A.min)
-    gather_add(v("OFF3"), v("BS"), v("TG1", 0, 1), I16)
-    landed("PH1", 0, pown[1], ("arrp", 2 * (NR - 1)))
-    landed("PH1", pown[2], 128, ("arrp", 2 * (NR - 1)))
-    pick_s(v("S3"), v("PH1"), v("OFF3", 0, 8))
-    pick_c(v("S3"), v("PH1"), v("OFF3", 0, 8))
-    bown = v("W2", 16 * me, 16 * me + 16)
-    send(True, [([c], bown, v("S3", 16 * d, 16 * d + 16), 1 << engs[i], "arr3") for i, (d, c) in enumerate(zip(others, oc_))])
-    send(False, [([c], v("W2s", bown[1], bown[2]), v("S3s", 16 * d, 16 * d + 16), 1 << engs[i], "arr3") for i, (d, c) in enumerate(zip(others, oc_))])
-
-    Mp, T1, PTm, fm = sm(), sm(), sm(), sm()
-    c1, c2, nw, nk, sel, G, r1, D2, Y0, D3, fl = sm(), sm(), sm(), sm(), sm(), sm(8), sm(), sm(), sm(), sm(), sm(8)
-    am = v("A1", me, me + 1)
-    tt(v("CM1"), PX, v("TI1"), A.is_lt)
-    scatter(v("O1"), J16, v("OP1", 0, 1))
-    ts(v("OFFO", 0, 1), v("OFF3", me, me + 1), 0.0, A.add)
-    red(Mp, v("CM1"))
-    ts(fm, v("OFF3", me, me + 1), I16, A.subtract, 0.0625, A.mult)
-    gather(v("A1"), v("O1"), v("TG1", 0, 1))
-    dma("s", ("od", 0, 1, 1), v("O1"), T.od[1:2, :], T.O1[0:1, 0:8])
     ts(v("MT", 0, 128, 4), v("M32"), Mp, A.mult, 16.0, A.min)
-    ts(T1, am, float(me), A.not_equal)
-    tt(PTm, am, fm, A.not_equal)
+    ts(v("MT", 129, 160, 4), THM, Mp, A.is_gt, 64.0, A.mult)
+    ts(OP1, C2, sg, A.add, 0.5, A.mult)
+    ts(ab, sg, -1.0, A.mult, sg, A.max)
     quant(v("MQ"), v("MT"))
-    mm(PL, v("S4Q"), v("MQ"))
-    tt(c1, T1, PTm, A.mult)
-    pick_c(bown, v("PH1"), v("OFFO", 0, 1))
-    pick_s(bown, v("PH1"), v("OFFO", 0, 1))
-    tt(c2, T1, c1, A.subtract)
-    ts(r1, Mp, 15.5, A.is_lt, c1, A.mult)
-    ts(v("OFFG"), v("PC", 0, 32), Q4, A.add)
-    ts(nw, c2, PTm, A.add, -1.0, A.add)
-    ts(Y0, X0, c2, A.mult, D0, A.add)
-    op("v", lambda: g.vector.tensor_tensor(ap(v("VT")), ap(v("NZ1", 0, 72)).indirect(ap(v("OFFG"))), ap(v("D5")), A.add),
-       [v("NZ1", 0, 72), v("OFFG"), v("D5")], [v("VT")])
-    ts(nk, TKp, nw, A.mult, 1.0, A.add)
-    ts(D3, X3, c2, A.mult)
-    ts(D2, TK2, c2, A.mult, r1, A.add)
-    ts(sel, BSp, fm, A.is_equal, nk, A.mult)
-    quant(v("W2", 256, 384), v("VT"))
-    ts(G, J8, HIp, A.is_equal, sel, A.mult)
-    quant(v("STQ"), v("STT"))
-    for b, x in enumerate((Y0, D1, D2, D3)):
-        ts(v("NT", b, 32, 4), G, x, A.mult)
-    quant(v("NTQ"), v("NT"))
-    mm(v("PD", 0, 128), v("STQ"), v("NTQ"))
-    quant(v("WQ"), v("WT"))
-    tt(fl, v("PD", 0, 8), v("JC"), A.add)
-    cp(v("OFFF"), fl)
+    mm(PL, v("SCQ"), v("MQ"))
+    scatter(BS, B32, OP1)
+    ts(TG1, ab, -0.5, A.mult, C3, A.add)
+    scatter(O1, JB, OP1)
+    ts(OFF3, BS, I16, A.add, off=TG1)
+    ts(OFFG, v("PC", 0, 32), Q4, A.add)
+    pick(v("S3"), v("PG"), v(OFF3, 8, 14))
+    bown = v("W3", 32 + 32 * k4, 64 + 32 * k4)
+    grp = [T.cores[par + 2 * ((k4 + i) % 4)] for i in (1, 2, 3)]
+    h, q = ne // 2, ne // 4
+    for x, cuts in ((True, (0, h, h + q, ne)), (False, (0, q, h, ne))):
+        send(x, [([c], bown, v("S3", 32 * i, 32 * i + 32), sum(1 << e for e in engs[cuts[i]:cuts[i + 1]]), "arr3") for i, c in enumerate(grp)])
 
-    landed("W2", 0, bown[1], ("arr3", 2 * (NR - 1)))
-    landed("W2", bown[2], 128, ("arr3", 2 * (NR - 1)))
-    pick_c(v("FT"), v("W2"), v("OFFF"))
-    pick_s(v("FT"), v("W2"), v("OFFF"))
+    xa, xb, xc = sm(), sm(), sm()
+    E0, E1, E2, HL0, HL1, OFFF = of(), of(), of(), of(16), of(16), of(16)
+    X, O = v(A1, 14, 15), v(A1, 15, 16)
+    tt(v("VT"), v("NZ1", 0, 72), v("D5"), A.add, off=OFFG)
+    gather(A1, O1, TG1)
+    dma("s", ("od", 0, 1, 1), O1, T.od[1:2, :], T.SM[0:1, O1[1]:O1[1] + 8])
+    tt(v(FLW, 24, 32), v("PC", 32, 40), v(FLW, 16, 24), A.add)
+    quant(v("W2", 128, 256), v("VT"))
+    ts(xa, X, float(me), A.not_equal, 8.0, A.mult)
+    ts(xb, X, O, A.not_equal, 16.0, A.mult)
+    ts(xc, X, O, A.not_equal)
+    ts(E2, O, 8.0, A.mult, Q8, A.add)
+    ts(E0, xa, xb, A.add, X, A.add)
+    ts(E1, xa, xc, A.mult, O, A.add)
+    pick(bown, v("PG"), v(OFF3, 14, 16))
+    ts(HL0, FLW, I16, A.add, off=E0)
+    ts(HL1, v(FLW, 16, 32), I16, A.add, off=E1)
+    ts(OFFF, FLA, 0.0, A.add, off=E2)
+    pick(v("W3", 0, 16), v("W2"), v(HL0, 0, 1))
+    pick(v("W3", 16, 32), v("W2"), v(HL1, 0, 1))
+
+    landed("W3", 32, bown[1], ("arr3", 2 * ne))
+    landed("W3", bown[2], 160, ("arr3", 2 * ne))
+    pick(v("FT"), v("W3"), v(OFFF, 0, 8))
     dma("s", ("oc", 0, 1, 1), v("FT"), T.oc[:, :], codes(v("FT")))
     mm(PS, v("WQ"), v("FT"))
     for k in range(4):

@@ -3,36 +3,41 @@ from concourse.mybir import dt, AluOpType, AxisListType, ActivationFunctionType
 
 A = AluOpType
 F = ActivationFunctionType
-NR, SL = 8, 18
+NR, SL, DIRECT = 8, 18, 3
+SHARED = ("R2",)
 TINY, BIG, MK, RND = 2.0 ** -100, 1e29, 256.0, 2.0 ** 27
 
 _f, _b, _u = "float32", "bfloat16", "uint16"
 SCRATCH = {}
 for _n, _w, _t in (
-        ("TB", 512, _b), ("UC", 4, _b), ("NZ", 128, _b), ("WT", 512, _b), ("ZB", 576, _b), ("UT", 512, _b), ("NU", 512, _b),
-        ("CI", 8, "int32"), ("CF", 8, _f), ("CK", 96, _f), ("J32", 32, _f), ("KI", 128, _b), ("IREF", 128, _b), ("OH2", 256, _b),
-        ("OHREF", 512, _b), ("QR", 128, _b), ("ZE", 520, _b), ("TIE", 128, _f), ("DIAG", 128, _b), ("RM", 128, _f),
-        ("M32", 32, _f), ("C256", 256, _b), ("MASK", 256, _b), ("OXI", 16, _f),
+        ("TB", 512, _b), ("UC", 4, _b), ("NZ", 144, _b), ("WT", 512, _b), ("ZB", 576, _b), ("UT", 512, _b), ("NU", 512, _b),
+        ("CI", 8, "int32"), ("CF", 8, _f), ("CK", 128, _f), ("J32", 32, _f), ("KI", 128, _b), ("IREF", 128, _b), ("OH2", 256, _b),
+        ("OHREF", 512, _b), ("QR", 128, _b), ("ZE", 520, _b), ("TIE", 128, _f), ("RM", 128, _f),
+        ("M32", 32, _f), ("C64", 64, _f), ("MASK", 64, _f),
         ("MVC", 512, _b), ("S1", 512, _b), ("ZW", 512, _b), ("SC", 512, _b), ("NT0", 576, _b), ("NT1", 576, _b),
-        ("INFO", 512, _b), ("OHT", 512, _b), ("CMP", 128, _f), ("SM", 1280, _f),
-        ("V0", 576, _b), ("V1", 576, _b), ("NZ1", 80, _f), ("ZT", 512, _b), ("XT", 512, _b),
-        ("TI1", 128, _f), ("TA", 128, _f), ("IND", 128, _f), ("CS", 128, _f),
-        ("D5", 512, _f), ("MT", 512, _b), ("VT", 512, _b), ("Y", 128, _f), ("CM1", 128, _f), ("OF", 256, _u)):
+        ("INFO", 512, _b), ("OHT", 512, _b), ("CMP", 128, _f), ("SM", 1536, _f),
+        ("V0", 576, _b), ("V1", 576, _b), ("NZ1", 80, _f), ("ZT", 512, _b),
+        ("TI1", 128, _f), ("TI0", 128, _f), ("IND", 128, _f), ("CS", 128, _f),
+        ("D5", 512, _f), ("VT", 512, _b), ("Y", 128, _f), ("CM1", 128, _f), ("OF", 256, _u)):
     SCRATCH[_n] = ("sbuf", [128, _w], _t)
 for _n, _w in (("UQ", 128), ("NUQ", 128), ("TQ", 128), ("MVQ", 128), ("OHQ", 128), ("S1Q", 128), ("EQ", 512), ("N0Q", 144), ("N1Q", 144),
                ("WQ", 128), ("ZWQ", 128), ("SCQ", 128), ("L1S", 144), ("LD1", 144), ("NB", 160), ("W2", 416), ("PH1", 128), ("PG", 128),
-               ("S3", 96), ("W3", 160), ("ZQ", 128), ("MQ", 128), ("XQ", 128), ("FT", 128), ("HT", 128)):
+               ("S3", 96), ("W3", 160), ("ZQ", 128), ("MQ", 128), ("XQ", 128), ("FT", 128), ("HT", 32), ("R1", 18), ("R2", 16)):
     SCRATCH[_n] = ("sbuf", [128, _w], "float8_e4m3fn_x4")
     SCRATCH[_n + "s"] = ("sbuf", [128, _w], "uint8")
 for _n, _w in (("PV", 2048), ("PA", 512), ("PB", 512), ("PC", 512), ("PD", 512)):
     SCRATCH[_n] = ("psum", [128, _w], _f)
 
-SEMAPHORES = ["sv", "sa", "st", "sg", "arrh", "arrg", "arr1", "arr2", "arr3", "arrp", "arrx"]
+SEMAPHORES = ["sv", "sa", "st", "sg", "arrh", "arrg", "arr1", "arr2", "arr3", "arrp", "arrx", "r1c", "r1s", "r2c", "r2s"]
 SEMAPHORES += ["d%d" % i for i in range(24)] + ["l%d" % i for i in range(12)]
 
 
-def _helper_of(topo, core):
-    return [c for c in topo.cores_of(core) if topo.die(c) != topo.die(core)][0]
+def _helpers(topo, core):
+    return [c for c in topo.cores_of(core) if topo.die(c) != topo.die(core)]
+
+
+def _bits(es):
+    return sum(1 << e for e in es)
 
 
 def _dst(topo, d, s):
@@ -40,30 +45,53 @@ def _dst(topo, d, s):
     return DstId(rid=rid, pnc=pid)
 
 
-def _hand_on(g, core, T, topo, owner):
+def _hand_on(g, core, T, topo, owner, j):
     me = T.rank_of(owner)
-    near, far = topo.engines(owner, core), len(topo.engines(owner, T.cores[me - 1]))
-    for k, (src, dst, sem, n) in enumerate((("HT", "PH1", "arrh", len(near)), ("HTs", "PH1s", "arrg", len(near) - far))):
+    engs = topo.engines(core, T.cores[me - 1])
+    near, far = len(topo.engines(owner, core)), len(topo.engines(owner, core)) - len(engs)
+    role = (j - me // 2) % 4
+    done = []
+
+    def call(sem, n, tr):
         g.wait_ge(T.sem[sem], n)
-        tr = []
-        for i, d in enumerate((me + x) % NR for x in range(1, NR)):
-            c = T.cores[d]
-            s, t = T[src][:, 16 * d:16 * d + 16], T[dst][:, 16 * me:16 * me + 16]
-            if k == 0:
-                s, t = s.bitcast(dt.uint8), t.bitcast(dt.uint8)
-            tr.append(RemoteDMATransfer(dst_ids=[_dst(topo, c, core)], dma_engine_mask=1 << topo.engines(core, c)[i],
-                                        remote_sem=T.sem.arrp, srcs=[s], dsts=[t]))
-        g.remote_dma_fused(tr, local_sem=T.sem["l%d" % k])
-    for k in range(2):
-        g.wait_ge(T.sem["l%d" % k], NR - 1)
+        s = "l%d" % len(done)
+        g.remote_dma_fused(tr, local_sem=T.sem[s])
+        done.append((s, len(engs)))
+
+    def view(n, lo, hi, x):
+        return T[n][:, lo:hi].bitcast(dt.uint8) if x else T[n + "s"][:, lo:hi]
+
+    def pieces(x):
+        ds = [d for d in (2 * j, 2 * j + 1) if d != me]
+        k = len(engs) // len(ds)
+        call("arrh" if x else "arrg", (near if x else far) // 4,
+             [RemoteDMATransfer(dst_ids=[_dst(topo, T.cores[d], core)], dma_engine_mask=_bits(engs[k * i:k * i + k]), remote_sem=T.sem.arrp,
+                                srcs=[view("HT", 16 * (d % 2), 16 * (d % 2) + 16, x)], dsts=[view("PH1", 16 * me, 16 * me + 16, x)])
+              for i, d in enumerate(ds)])
+
+    def relay(src, dst, w, sem):
+        if role >= 2 or src not in SHARED:
+            return
+        cs = [T.cores[(me + DIRECT + 1 + 2 * role + i) % NR] for i in range(2)]
+        for x in (True, False):
+            call(src.lower() + ("c" if x else "s"), far // 2,
+                 [RemoteDMATransfer(dst_ids=[_dst(topo, c, core) for c in cs], dma_engine_mask=_bits(engs), remote_sem=T.sem[sem],
+                                    srcs=[view(src, 0, w, x)], dsts=[view(dst, w * me, w * me + w, x) for c in cs])])
+
+    pieces(True)
+    relay("R1", "LD1", SL, "arr1")
+    pieces(False)
+    relay("R2", "W2", 16, "arr2")
+    for s, n in done:
+        g.wait_ge(T.sem[s], n)
 
 
 def rank_program(g, core, T, topo):
     me = T.rank_of(core)
     if me is None:
         for c in T.cores:
-            if _helper_of(topo, c) == core:
-                _hand_on(g, core, T, topo, c)
+            if core in _helpers(topo, c):
+                _hand_on(g, core, T, topo, c, _helpers(topo, c).index(core))
         return
     ENG = {"v": g.vector, "a": g.scalar, "t": g.tensor, "g": g, "s": g.sync}
     SEM = {"v": "sv", "a": "sa", "t": "st", "g": "sg"}
@@ -151,6 +179,9 @@ def rank_program(g, core, T, topo):
         op("a", lambda: g.scalar.activation(ap(out), ap(a), fn, **k2),
            [a] + [x for k, x in kw.items() if isinstance(x, tuple) and k != "accum_out"], [out] + [x for k, x in kw.items() if k == "accum_out"])
 
+    def lin(out, x, a, b):
+        act(out, x, F.Identity, scale=a, bias=b)
+
     def pl(x):
         return (x[0] + "s", x[1], x[2], 1)
 
@@ -201,14 +232,28 @@ def rank_program(g, core, T, topo):
         ends.append((s, n))
 
     oc_ = [T.cores[(me + i) % NR] for i in range(1, NR)]
-    helper = _helper_of(topo, core)
+    hs = _helpers(topo, core)
     engs = topo.engines(core, oc_[0])
     ne = len(engs)
     m_all = topo.mask(core, oc_[0])
-    m_help = topo.mask(core, helper)
-    m_far = m_help & ~m_all
+    e16 = topo.engines(core, hs[0])
+    far = [e for e in e16 if e not in engs]
     bcast = 2 * ne * (NR - 1)
     par, k4 = me % 2, me // 2
+    HBM = ("hbm", 0, 1, 1)
+
+    def broadcast(dst, src, via, sem):
+        k = len(far) // 2
+        for x in (True, False):
+            if via not in SHARED:
+                send(x, [(oc_, dst, src, m_all, sem)])
+                continue
+            send(x, [(oc_[:DIRECT], dst, src, m_all, sem)] +
+                 [([hs[(k4 + i) % 4]], v(via), src, _bits(far[k * i:k * i + k]), via.lower() + ("c" if x else "s")) for i in range(2)])
+
+    def to_helpers(x, es, sem):
+        k = len(es) // 4
+        send(x, [([c], v("HT"), v("TQ", 32 * j, 32 * j + 32), _bits(es[k * j:k * j + k]), sem) for j, c in enumerate(hs)])
 
     top = {"SM": 0, "CK": 0, "OF": 0}
 
@@ -232,246 +277,251 @@ def rank_program(g, core, T, topo):
         else:
             op("g", lambda: g.iota(ap(out), pattern, base, mult), [], [out])
 
-    dma("s", v("TB"), v("TB"), None, T.tb[:, :])
-    dma("a", v("UC"), v("UC"), None, T.u[:, 0:4])
-    dma("a", v("NZ"), v("NZ"), None, T.nz[:, :])
-    dma("s", v("WT"), v("WT"), None, T.w[:, :])
-    iota(v("CI", 0, 1), [[0, 1]], 1, False)
-    iota(v("OH2"), [[0, 8], [1, 16], [16, 2]], 0)
+    ci, cf = (lambda i: v("CI", i, i + 1)), (lambda i: v("CF", i, i + 1))
+    P, I16, S16, Q4, P4, Q2 = cf(0), cf(1), cf(2), cf(3), cf(4), cf(5)
+    dma("s", v("TB"), HBM, None, T.tb[:, :])
+    dma("a", v("UC"), HBM, None, T.u[:, 0:4])
+    for t in range(2):
+        dma("a", v("NZ", 72 * t, 72 * t + 64), HBM, None, T.nz[:, 64 * t:64 * t + 64])
+    iota(P, [[0, 1]], 1)
     iota(v("KI"), [[1, 128]], 0)
+    iota(ci(0), [[0, 1]], 1, False)
+    iota(v("OH2"), [[0, 8], [1, 16], [16, 2]], 0)
     iota(v("J32"), [[1, 32]], 0)
     iota(v("IREF"), [[0, 8], [1, 16]], 0)
 
-    ci, cf = (lambda i: v("CI", i, i + 1)), (lambda i: v("CF", i, i + 1))
-    J8, J16 = v("J32", 0, 8), v("J32", 0, 16)
+    J8, J16, Z128, HD = v("J32", 0, 8), v("J32", 0, 16), v("ZB", 0, 128), v("ZE", 4, 516, 4)
     ms(v("ZB"), 0.0)
+    ms(v("ZE"), 0.0)
+    ts(HD, v("KI"), P, A.is_equal, 0.5, A.mult)
     ts(ci(1), ci(0), 15, A.bitwise_and)
     ts(ci(2), ci(0), 4, A.logical_shift_right)
     ts(ci(3), ci(0), 3, A.bitwise_and)
     ts(ci(4), ci(0), 2, A.logical_shift_right)
     ts(ci(5), ci(0), 1, A.bitwise_and)
     ts(ci(6), ci(0), 1, A.logical_shift_right)
-    ms(v("MVC"), 0.0)
-    ts(ci(7), ci(6), k4 + 1, A.add)
-    cp(v("CF", 0, 7), v("CI", 0, 7))
-    P, I16, S16, Q4, P4, Q2 = cf(0), cf(1), cf(2), cf(3), cf(4), cf(5)
-    ms(v("INFO"), 0.0)
     H16, P32, ia, ib = ck(), ck(), ck(), ck()
-    ts(H16, S16, 16.0, A.mult)
-    ts(P32, P, 32.0, A.add)
-    ts(ia, P, float(me), A.is_equal, MK, A.mult)
-    ts(ib, P, float(me + 16), A.is_equal, -0.125, A.mult)
-    ts(v("TIE"), v("KI"), P, A.is_lt, TINY, A.mult)
-    tt(v("INFO", 3, 4), ia, ib, A.add)
+    act(v("MVC"), v("ZB", 0, 512))
+    act(v("INFO"), v("ZB", 0, 512))
+    E = [v("EQ", 128 * b, 128 * b + 128) for b in range(4)]
+    PVb = [v("PV", 512 * b, 512 * b + 144) for b in range(4)]
+
+    def unit(b):
+        quant(E[b], v("ZE", 4 - b, 516 - b))
+
+    unit(0)
+    cp(v("CF", 1, 7), v("CI", 1, 7))
+    for b in range(4):
+        ts(v("NU", b, 512, 4), Z128, v("UC", b, b + 1), A.subtract)
+    for b in range(2):
+        ts(v("UT", b, 512, 4), Z128, v("UC", b, b + 1), A.add)
+        lin(v("UT", b + 2, 512, 4), Z128, 1.0, v("UC", b + 2, b + 3))
+    lin(H16, S16, 16.0, 0.0)
+    lin(P32, P, 1.0, 32.0)
+    for e, st, x in ((1, 10, I16), (25, 6, I16), (0, 10, H16), (16, 6, H16)):
+        lin(v("MVC", e, e + st + 1, st), v("ZB", 0, 2), 1.0, x)
     for h in range(2):
         act(v("OHREF", h, 512, 2), v("OH2"))
-    for b in range(4):
-        ts(v("NU", b, 512, 4), v("ZB", 0, 128), v("UC", b, b + 1), A.subtract)
-    for b in range(2):
-        ts(v("UT", b, 512, 4), v("ZB", 0, 128), v("UC", b, b + 1), A.add)
-        act(v("UT", b + 2, 512, 4), v("ZB", 0, 128), F.Identity, bias=v("UC", b + 2, b + 3))
-    for e, st, x in ((0, 10, H16), (1, 10, I16), (16, 6, H16), (25, 6, I16)):
-        act(v("MVC", e, e + st + 1, st), v("ZB", 0, 2), F.Identity, bias=x)
-    act(v("ZE"), v("ZB", 0, 520))
-    for t in (1, 0):
-        n = "NT%d" % t
-        for b in range(8):
-            act(v(n, 64 + b, 576, 72), v("ZB", 0, 8))
+    for t in range(2):
+        act(v("NZ", 72 * t + 64, 72 * t + 72), v("ZB", 0, 8))
+
+    def noise(t):
         for a in range(NR):
-            act(v(n, 72 * a, 72 * a + 64), v("NZ", 64 * t, 64 * t + 64))
-        if t == 1:
-            break
+            act(v("NT%d" % t, 72 * a, 72 * a + 72), v("NZ", 72 * t, 72 * t + 72))
+
+    noise(0)
+    for b, x in ((1, 0.0), (2, 0.0), (0, 1.0)):
+        lin(v("S1", b, 512, 4), Z128, 1.0, x)
+    act(v("SC", 3, 512, 4), Z128)
+    for b in (2, 3):
+        act(v("ZT", b, 512, 4), Z128)
+    lin(v("ZW"), v("ZB", 0, 512), 1.0, 2.0)
 
     TQ = v("TQ")
     quant(v("NUQ"), v("NU"))
     quant(TQ, v("TB"))
-    send(True, [([helper], v("HT"), TQ, m_help, "arrh")])
+    to_helpers(True, e16, "arrh")
+    dma("s", v("WT"), HBM, None, T.w[:, :])
     quant(v("UQ"), v("UT"))
     PX, PS, PL, PF = v("PA", 0, 128), v("PB", 0, 128), v("PC", 0, 128), v("PD", 0, 144)
     mm(PX, TQ, v("NUQ"), True, False)
     mm(PX, v("UQ"), TQ, False, True)
     mm(PS, TQ, v("UQ"))
-    quant(v("MVQ"), v("MVC"))
-    rk, va, vb, OFF1 = sm(), sm(), sm(), of(4)
+    ts(v("TIE"), v("KI"), P, A.is_lt, TINY, A.mult)
+    unit(1)
+    rk, va, vb, OFF1, ct = sm(), sm(), sm(), of(4), ck()
     tt(v("CMP"), PX, v("TIE"), A.is_lt)
-    ts(v("INFO", 0, 1), v("PB", 0, 1), 0.0, A.is_gt)
+    ts(ia, P, float(me), A.is_equal, MK, A.mult)
+    ts(ib, P, float(me + 16), A.is_equal, -0.125, A.mult)
     red(rk, v("CMP"))
+    quant(v("MVQ"), v("MVC"))
     ts(v("OHT"), v("OHREF"), rk, A.is_equal)
     ts(va, rk, 31.5, A.is_ge, 1000.0, A.mult)
+    ts(v("INFO", 0, 1), v("PB", 0, 1), 0.0, A.is_gt)
     quant(v("OHQ"), v("OHT"))
-    ts(vb, va, rk, A.add, P32, A.min)
     mm(PL, v("OHQ"), v("MVQ"))
+    ts(vb, va, rk, A.add, P32, A.min)
+    tt(v("INFO", 3, 4), ia, ib, A.add)
     ts(v("INFO", 1, 2), vb, RND, A.add, RND, A.subtract)
+    ts(ct, P, -16.0, A.add, 0.0, A.max)
     tt(v("INFO", 2, 3), vb, v("INFO", 1, 2), A.subtract)
-    cp(OFF1, v("PC", 0, 4))
     cp(v("INFO", 4, 8), v("PC", 4, 8))
-    pick(v("L1S", 0, 16), TQ, v(OFF1, 0, 1))
+    cp(OFF1, v("PC", 0, 4))
     quant(v("L1S", 16, 144), v("INFO"))
+    pick(v("L1S", 0, 16), TQ, v(OFF1, 0, 1))
     own, mine = v("LD1", SL * me, SL * me + SL), v("L1S", 0, SL)
-    for x in (True, False):
-        send(x, [(oc_, own, mine, m_all, "arr1")])
-    send(False, [([helper], v("HT"), TQ, m_far, "arrg")])
+    broadcast(own, mine, "R1", "arr1")
+    to_helpers(False, far, "arrg")
     dma("s", own, mine, codes(own), codes(mine))
     dma("s", pl(own), pl(mine))
     pown, town = v("PH1", 16 * me, 16 * me + 16), v("TQ", 16 * me, 16 * me + 16)
     dma("s", pown, town, codes(pown), codes(town))
     dma("s", pl(pown), pl(town))
 
+    WN, J18, F16, JB, FLW = sm(160), sm(16), sm(16), sm(32), sm(32)
+    iota(J18, [[SL, 16]], 0)
+    iota(v(WN, 16, 24), [[0, 8]], 0, True, SL * NR)
     iota(v("QR"), [[0, 8], [1, 4], [0, 4]], 0)
-    iota(v("C256"), [[0, 8], [1, 8], [0, 4]], 0)
-    iota(v("OXI"), [[72, 8], [0, 2]], 0, True, 64)
-    ts(v("ZE", 4, 516, 4), v("KI"), P, A.is_equal, 0.5, A.mult)
-    quant(v("N1Q"), v("NT1"))
-    for b in range(8):
-        act(v("NT0", 64 + b, 576, 72), v("ZB", 0, 8))
-    for a in range(NR):
-        act(v("NT0", 72 * a, 72 * a + 64), v("NZ", 0, 64))
-    E = [v("EQ", 128 * b, 128 * b + 128) for b in range(4)]
-    PVb = [v("PV", 512 * b, 512 * b + 144) for b in range(4)]
-    for b in range(4):
-        quant(E[b], v("ZE", 4 - b, 516 - b))
-        mm(PVb[b], E[b], v("N1Q"))
-    ct, TIE8, TM0, TM1, TMP, c8, CB, C2, C3, EP, Q22, Q8, THM = ck(), ck(8), ck(8), ck(8), ck(8), ck(), ck(), ck(2), ck(), ck(), ck(), ck(), ck(8)
-    ms(v("S1"), 0.0)
-    ts(ct, P, -16.0, A.add, 0.0, A.max)
-    ms(v("NZ1", 64, 80), 0.0)
-    ms(v("S1", 0, 512, 4), 1.0)
+    iota(v("C64"), [[0, 8], [1, 8]], 0)
+    iota(v(JB, 0, 16), [[1, 16]], 0)
+    iota(v("RM"), [[0, 8], [1000, 16]], 0)
+    iota(v(FLW, 0, 8), [[0, 8]], 0, True, 400)
+    iota(v(FLW, 8, 16), [[SL, 8]], 0, True, 256)
+    iota(v(FLW, 16, 24), [[16, 8]], 0)
+    TIE8, TM0, TMB, TM1, TMP, c8, CB, C2, C3, EP, Q22, Q8, THM, G8, cx = (
+        ck(8), ck(8), ck(8), ck(8), ck(8), ck(), ck(), ck(2), ck(), ck(), ck(), ck(), ck(8), ck(), ck())
+    lin(c8, I16, 8.0, -48.0)
+    lin(TIE8, J8, -0.125, 0.0)
+    lin(F16, J16, 0.0, 0.0)
     ts(v("S1", 3, 512, 4), v("IREF"), P, A.is_equal, ct, A.add)
-    for b in range(4):
-        act(v("NZ1", b, 64, 4), v("PV", 512 * b, 512 * b + 16))
     quant(v("N0Q"), v("NT0"))
+    unit(2)
+    unit(3)
     for b in range(4):
         mm(PVb[b], E[b], v("N0Q"), True, False)
-    WN, J18, F16, JB, FLW = sm(96), sm(16), sm(16), sm(32), sm(32)
-    ts(c8, I16, 8.0, A.mult, -48.0, A.add)
-    ts(J18, J16, float(SL), A.mult)
-    ms(v(WN, 8, 16), float(SL * NR))
     quant(v("S1Q"), v("S1"))
-    ts(CB, I16, 7.5, A.is_gt, c8, A.mult)
-    pick(v("NB", 144, 160), TQ, v(OFF1, 2, 3))
-    pick(v("W2", 400, 416), TQ, v(OFF1, 0, 1))
-    ts(TIE8, J8, -0.125, A.mult)
-    ts(ci(7), ci(7), 3, A.bitwise_and)
+    ts(G8, I16, 7.5, A.is_gt)
     ts(TM0, J8, I16, A.is_equal, MK, A.mult)
-    ms(F16, 0.0)
-    ts(v(C2, 0, 1), CB, 2.0, A.mult, 7.0, A.add)
-    ts(v(C2, 1, 2), CB, 2.0, A.mult, 167.0, A.add)
-    ts(EP, ci(7), 2.0, A.mult, float(par), A.add)
-    ts(C3, I16, 7.5, A.is_gt, Q2, A.mult)
-    tt(TM0, TM0, TIE8, A.add)
-    ts(TMP, TIE8, MK, A.add)
-    ts(EP, EP, I16, A.subtract)
-    ts(C3, C3, 80.0, A.mult, 3.5, A.add)
-    ts(Q22, Q2, 2.0, A.mult)
-    ts(EP, I16, 7.5, A.is_gt, EP, A.mult)
-    ts(v("RM"), v("IREF"), 0.0, A.is_gt)
-    ts(TM1, J8, EP, A.subtract, I16, A.is_equal)
-    ms(v("ZW"), 1.0)
-    ts(TM1, TM1, MK, A.mult)
-    ts(v("DIAG"), v("KI"), P, A.is_equal)
-    tt(TM1, TM1, TIE8, A.add)
-    quant(v("ZWQ"), v("ZW"))
-    act(v("SC"), v("ZB", 0, 512))
-    act(v("ZT"), v("ZB", 0, 512))
-    act(v("XT", 256, 512), v("ZB", 0, 256))
-    act(v("MT"), v("ZB", 0, 512))
-    OFT, OFG, OFX = of(8), of(), of(16)
+    pick(v("NB", 144, 160), TQ, v(OFF1, 2, 3))
+    lin(CB, G8, c8, 0.0)
+    lin(TMB, TM0, 1.0, -MK)
+    lin(v(C2, 0, 1), CB, 2.0, 7.0)
+    pick(v("W2", 400, 416), TQ, v(OFF1, 0, 1))
+    noise(1)
+    lin(v(C2, 1, 2), CB, 2.0, 167.0)
+    lin(TMP, TIE8, 1.0, MK)
+    lin(Q22, Q2, 2.0, 0.0)
+    lin(cx, G8, 72.0, 65.0)
+    lin(v("NZ1", 64, 80), J16, 0.0, 0.0)
+    OFT, OFG0, OX1, OX2 = of(8), of(), of(4), of(4)
+    ts(ci(7), ci(6), float(k4 + 1), A.add)
+    ts(C3, G8, Q2, A.mult, 80.0, A.mult)
     ts(OFT, J8, 0.0, A.add)
-    ts(OFG, S16, 0.0, A.add)
-    ts(OFX, v("OXI"), Q4, A.add)
-    cp(v(JB, 0, 16), J16)
-    ts(v("MASK"), v("C256"), S16, A.is_equal)
+    ts(ci(7), ci(7), 3, A.bitwise_and)
+    ts(OFG0, S16, 0.0, A.add)
+    ts(v("M32"), v("J32"), P4, A.is_equal)
+    ts(EP, ci(7), 2.0, A.mult, float(par), A.add)
+    ts(THM, J8, S16, A.is_equal, 16.5, A.mult)
+    ts(Q8, I16, 7.0, A.min)
+    ts(EP, EP, I16, A.subtract, G8, A.mult)
+    ts(v("MASK"), v("C64"), S16, A.is_equal)
     ts(v("SC", 0, 512, 4), v("QR"), Q4, A.is_equal, 4.0, A.mult)
+    ts(TM1, J8, EP, A.subtract, I16, A.is_equal)
     for b in (1, 2):
         ts(v("SC", b, 512, 4), v("IREF"), I16, A.is_equal, 2.0, A.mult)
-    ms(v("MASK", 0, 256, 4), 0.0)
-    quant(v("SCQ"), v("SC"))
+    ts(TM1, TM1, MK, A.mult)
+    quant(v("N1Q"), v("NT1"))
 
     landed("LD1", 0, own[1], ("arr1", bcast))
     landed("LD1", own[2], 144, ("arr1", bcast))
     mm(PF, v("S1Q"), v("LD1"))
     for b in range(4):
         mm(PVb[b], E[b], v("LD1"), False, True)
-    for b in range(4):
-        act(v("V0", b, 576, 4), PVb[b])
     FIT = v("PD", 16, 144, SL)
-    mx, cm, p1, gv, t1, O0 = sm(), sm(8), sm(), sm(), sm(), sm(96)
-    OP0, OX0, TG0, OFFH = of(), of(), of(), of(18)
-    red(mx, FIT, A.max)
-    tt(v(F16, 0, 8), FIT, TM0, A.subtract)
-    ts(cm, FIT, MK, A.add, mx, A.is_gt)
-    red(p1, cm)
-    ts(OP0, p1, CB, A.add, -1.0, A.add)
-    ts(gv, p1, 4.5, A.is_lt, 8.0, A.mult)
-    ts(t1, p1, -1.0, A.mult, 9.0, A.add)
+    mx, K0, cm, s0, gv, t1, O0, OD0 = sm(), sm(8), sm(8), sm(), sm(), sm(), sm(160), sm(8)
+    OP0, OX0, TG0, OFFH, OFE = of(), of(), of(), of(18), of(4)
+    quant(v("ZWQ"), v("ZW"))
+    red(mx, FIT, A.max, True)
+    tt(K0, FIT, TMB, A.subtract)
+    act(v("V0", 0, 576, 4), PVb[0])
+    act(cm, K0, F.Sign, bias=mx, accum_out=s0)
+    for b in range(1, 4):
+        act(v("V0", b, 576, 4), PVb[b])
+    quant(v("SCQ"), v("SC"))
+    ts(OX1, v("J32", 0, 4), 144.0, A.mult, cx, A.add)
+    ts(OP0, s0, v(C2, 0, 1), A.add)
+    ts(gv, s0, 0.0, A.is_lt, 8.0, A.mult)
+    ts(t1, s0, -1.0, A.mult, s0, A.max)
     scatter(WN, J18, OP0)
-    ts(OX0, gv, p1, A.subtract, 8.0, A.add)
-    scatter(O0, J16, OP0)
-    ts(v(OFFH, par, par + 16), WN, I16, A.add, off=OX0)
-    ts(TG0, p1, t1, A.min, -1.0, A.add)
+    ts(OX0, gv, s0, A.subtract, 7.0, A.add)
+    ts(TG0, t1, -1.0, A.mult, 7.0, A.add)
     quant(v("NB", 0, 144), v("V0"))
-    OFE = of(4)
-    ts(OFE, v(O0, 0, 4), 16.0, A.mult, I16, A.add)
+    ts(v(OFFH, par, par + 16), WN, I16, A.add, off=OX0)
+    scatter(O0, J16, OP0)
     hown = v("W2", 16 * me, 16 * me + 16)
     pick(hown, v("NB"), v(OFFH, me + par, me + par + 1))
-    for x in (True, False):
-        send(x, [(oc_, hown, hown, m_all, "arr2")])
+    broadcast(hown, hown, "R2", "arr2")
 
-    landed("PH1", 0, pown[1], ("arrp", 2 * (NR - 1)))
-    landed("PH1", pown[2], 128, ("arrp", 2 * (NR - 1)))
+    landed("PH1", 0, pown[1], ("arrp", ne * NR))
+    landed("PH1", pown[2], 128, ("arrp", ne * NR))
     gown = v("PG", 64 * par, 64 * par + 64)
-    BR16, FS, FB, TP, B32 = v(JB, 16, 32), sm(96), sm(16), sm(16), sm(32)
+    BR16, FS, FB, TP, B32 = v(JB, 16, 32), sm(160), sm(16), sm(16), sm(32)
     BR = v(JB, 16, 24)
-    gather(BR16, O0, TG0)
-    pick(gown, v("PH1"), OFE)
-    for x in (True, False):
-        send(x, [([T.cores[me ^ 1]], gown, gown, m_all, "arrx")])
+    G, z1, ZR, DG, BSp, Zp, cc, m1, f2, KB, KBm, KBp, FLA, TA = (
+        sm(8), sm(8), sm(8), sm(16), sm(16), sm(), sm(8), sm(8), sm(8), sm(8), sm(8), sm(8), sm(64), sm(8))
+    LZ = of(16)
+    for b in range(4):
+        mm(PVb[b], E[b], v("N1Q"))
+    for b in range(4):
+        act(v("NZ1", b, 64, 4), v("PV", 512 * b, 512 * b + 16))
     for b in range(4):
         mm(PVb[b], E[b], v("N1Q"), True, False)
         mm(PVb[b], E[b], v("LD1"), False, True)
-    dma("s", ("od", 0, 1, 1), O0, T.od[0:1, :], T.SM[0:1, O0[1]:O0[1] + 8])
-    G, z1, ZR, DG, BSp, Zp, cc, m1, f2, KB, KBm, KBp, FLA = sm(8), sm(8), sm(8), sm(16), sm(16), sm(), sm(8), sm(8), sm(8), sm(8), sm(8), sm(8), sm(64)
-    LZ = of(16)
-    scatter(FS, F16, OP0)
+    gather(BR16, O0, TG0)
+    ts(OFE, v(O0, 0, 8, 2), 16.0, A.mult, I16, A.add)
+    tt(v(F16, 0, 8), K0, TMP, A.subtract)
     tt(G, BR, J8, A.is_equal)
     ts(z1, BR, 72.0, A.mult, 68.0, A.add)
-    gather(BSp, BR, OFG)
-    gather(FB, FS, TG0)
+    scatter(FS, F16, OP0)
     tt(ZR, z1, G, A.add)
-    ts(cc, G, -16.0, A.mult, 112.0, A.add)
-    gather(TP, J16, TG0)
-    ts(LZ, ZR, Q22, A.add, off=OFG)
-    ts(f2, v(FB, 0, 8), -16.0, A.add)
-    tt(m1, v(FB, 0, 8), cc, A.min)
+    pick(gown, v("PH1"), OFE)
+    for x in (True, False):
+        send(x, [([T.cores[me ^ 1]], gown, gown, m_all, "arrx")])
+    act(OD0, v(O0, 0, 16, 2))
+    dma("s", HBM, OD0, T.od[0:1, :], T.SM[0:1, OD0[1]:OD0[1] + 8])
+    ts(LZ, ZR, Q22, A.add, off=OFG0)
+    gather(FB, FS, TG0)
+    ts(OX2, OX1, 1.0, A.add)
+    tt(TM1, TM1, TIE8, A.add)
+    lin(cc, G, -16.0, 112.0)
+    lin(f2, v(FB, 0, 8), 1.0, -16.0)
     gather(DG, v("V0"), v(LZ, 0, 1))
-    ts(v("TA"), BR, v(BSp, 0, 1), A.not_equal, -BIG, A.mult, off=OFT)
+    gather(BSp, BR, OFG0)
+    gather(TP, J16, TG0)
+    tt(v("INFO", 9, 264, 4), v("V0"), v("MASK"), A.mult, off=OX1)
+    tt(v("INFO", 10, 264, 4), v("V0"), v("MASK"), A.mult, off=OX2)
     for b in range(2):
-        act(v("ZT", b, 512, 4), v("DIAG"), F.Identity, scale=v(DG, b, b + 1))
+        lin(v("ZT", b, 512, 4), HD, v(DG, b, b + 1), 0.0)
+    lin(Zp, v(DG, 0, 1), 1.0, v(DG, 1, 2))
     for b in range(4):
         act(v("V1", b, 576, 4), PVb[b])
-    tt(KB, m1, f2, A.max)
-    tt(Zp, v(DG, 0, 1), v(DG, 1, 2), A.add)
-    tt(v("XT", 0, 256), v("V0"), v("MASK"), A.mult, off=OFX)
+    lin(v(B32, 0, 16), TP, 8.0, 0.0)
+    lin(v(B32, 16, 32), TP, 8.0, 64.0)
+    lin(C3, C3, 1.0, 3.5)
+    lin(THM, THM, 1.0, -1.0)
+    tt(m1, v(FB, 0, 8), cc, A.min)
+    ts(TA, BR, v(BSp, 0, 1), A.not_equal, -BIG, A.mult)
     quant(v("ZQ"), v("ZT"))
     mm(PL, v("ZWQ"), v("ZQ"))
+    tt(KB, m1, f2, A.max)
+    quant(v("XQ"), v("INFO"))
+    mm(v("PD", 0, 128), v("SCQ"), v("XQ"))
+    act(FLA, v("PD", 2, 66))
     tt(KBm, KB, TM1, A.add)
     tt(KBp, KB, TMP, A.add)
-    quant(v("XQ"), v("XT"))
-    mm(v("PD", 0, 128), v("SCQ"), v("XQ"))
-    act(FLA, v("PD", 0, 64))
-    ts(v(B32, 0, 16), TP, 16.0, A.mult)
-    ts(v(B32, 16, 32), TP, 16.0, A.mult, 64.0, A.add)
-    ts(v("TI1"), PL, Zp, A.is_lt, TINY, A.mult)
-    ts(v("M32"), v("J32"), P4, A.is_equal)
-    ts(THM, J8, S16, A.is_equal, 16.5, A.mult)
-    tt(v("TI1"), v("TI1"), v("TA"), A.add)
-    ts(THM, THM, -1.0, A.add)
-    quant(v("W2", 256, 400), v("V1"))
-    ms(v(FLW, 0, 8), 400.0)
-    ts(v(FLW, 8, 16), J8, float(SL), A.mult, 256.0, A.add)
-    ts(v(FLW, 16, 24), J8, 16.0, A.mult)
-    ts(Q8, I16, 7.0, A.min)
+    ts(v("TI0"), PL, Zp, A.is_lt, TINY, A.mult)
     quant(v("WQ"), v("WT"))
+    tt(v("TI1"), TA, v("TI0"), A.add, off=OFT)
 
     landed("W2", 0, hown[1], ("arr2", bcast))
     landed("W2", hown[2], 128, ("arr2", bcast))
@@ -484,51 +534,52 @@ def rank_program(g, core, T, topo):
         mm(v("PV", 512 * b, 512 * b + 128), E[b], H)
     Km, Kp, nx, sj, sg, ab, Mp, BS, O1, A1 = sm(8), sm(8), sm(), sm(8), sm(), sm(), sm(), sm(160), sm(160), sm(16)
     OP1, TG1, OFF3, OFFG = of(2), of(), of(16), of(32)
+    quant(v("W2", 256, 400), v("V1"))
     ts(v("IND"), PS, 0.0, A.is_gt)
-    op("v", lambda: g.vector.tensor_tensor_scan(ap(v("CS")), ap(v("RM")), ap(v("IND")), 0.0, A.mult, A.add), [v("RM"), v("IND")], [v("CS")])
+    op("v", lambda: g.vector.tensor_tensor_scan(ap(v("CS")), ap(v("RM")), ap(v("IND")), 0.0, A.min, A.add), [v("RM"), v("IND")], [v("CS")])
     tt(v("CM1"), PX, v("TI1"), A.is_lt)
     tt(Km, v("CS", 15, 128, 16), KBm, A.add)
     tt(Kp, v("CS", 15, 128, 16), KBp, A.add)
-    red(Mp, v("CM1"))
     red(nx, Km, A.max, True)
     act(sj, Kp, F.Sign, bias=nx, accum_out=sg)
     for b in range(4):
         act(v("D5", b, 512, 4), v("PV", 512 * b, 512 * b + 128))
-    ts(v("MT", 0, 128, 4), v("M32"), Mp, A.mult, 16.0, A.min)
-    ts(v("MT", 129, 160, 4), THM, Mp, A.is_gt, 64.0, A.mult)
+    red(Mp, v("CM1"))
+    ts(v("INFO", 272, 400, 4), v("M32"), Mp, A.mult, 16.0, A.min)
+    ts(v("INFO", 401, 432, 4), THM, Mp, A.is_gt, 64.0, A.mult)
     ts(OP1, C2, sg, A.add, 0.5, A.mult)
     ts(ab, sg, -1.0, A.mult, sg, A.max)
-    quant(v("MQ"), v("MT"))
+    quant(v("MQ"), v("INFO"))
     mm(PL, v("SCQ"), v("MQ"))
     scatter(BS, B32, OP1)
     ts(TG1, ab, -0.5, A.mult, C3, A.add)
     scatter(O1, JB, OP1)
     ts(OFF3, BS, I16, A.add, off=TG1)
-    ts(OFFG, v("PC", 0, 32), Q4, A.add)
+    gather(A1, O1, TG1)
+    ts(OFFG, v("PC", 68, 100), Q4, A.add)
     pick(v("S3"), v("PG"), v(OFF3, 8, 14))
     bown = v("W3", 32 + 32 * k4, 64 + 32 * k4)
     grp = [T.cores[par + 2 * ((k4 + i) % 4)] for i in (1, 2, 3)]
     h, q = ne // 2, ne // 4
     for x, cuts in ((True, (0, h, h + q, ne)), (False, (0, q, h, ne))):
-        send(x, [([c], bown, v("S3", 32 * i, 32 * i + 32), sum(1 << e for e in engs[cuts[i]:cuts[i + 1]]), "arr3") for i, c in enumerate(grp)])
+        send(x, [([c], bown, v("S3", 32 * i, 32 * i + 32), _bits(engs[cuts[i]:cuts[i + 1]]), "arr3") for i, c in enumerate(grp)])
 
     xa, xb, xc = sm(), sm(), sm()
     E0, E1, E2, HL0, HL1, OFFF = of(), of(), of(), of(16), of(16), of(16)
     X, O = v(A1, 14, 15), v(A1, 15, 16)
-    tt(v("VT"), v("NZ1", 0, 72), v("D5"), A.add, off=OFFG)
-    gather(A1, O1, TG1)
-    dma("s", ("od", 0, 1, 1), O1, T.od[1:2, :], T.SM[0:1, O1[1]:O1[1] + 8])
-    tt(v(FLW, 24, 32), v("PC", 32, 40), v(FLW, 16, 24), A.add)
-    quant(v("W2", 128, 256), v("VT"))
+    dma("s", HBM, O1, T.od[1:2, :], T.SM[0:1, O1[1]:O1[1] + 8])
     ts(xa, X, float(me), A.not_equal, 8.0, A.mult)
     ts(xb, X, O, A.not_equal, 16.0, A.mult)
     ts(xc, X, O, A.not_equal)
-    ts(E2, O, 8.0, A.mult, Q8, A.add)
+    tt(v("VT"), v("NZ1", 0, 72), v("D5"), A.add, off=OFFG)
     ts(E0, xa, xb, A.add, X, A.add)
     ts(E1, xa, xc, A.mult, O, A.add)
-    pick(bown, v("PG"), v(OFF3, 14, 16))
+    tt(v(FLW, 24, 32), v("PC", 100, 108), v(FLW, 16, 24), A.add)
+    quant(v("W2", 128, 256), v("VT"))
+    ts(E2, O, 8.0, A.mult, Q8, A.add)
     ts(HL0, FLW, I16, A.add, off=E0)
     ts(HL1, v(FLW, 16, 32), I16, A.add, off=E1)
+    pick(bown, v("PG"), v(OFF3, 14, 16))
     ts(OFFF, FLA, 0.0, A.add, off=E2)
     pick(v("W3", 0, 16), v("W2"), v(HL0, 0, 1))
     pick(v("W3", 16, 32), v("W2"), v(HL1, 0, 1))
@@ -536,12 +587,12 @@ def rank_program(g, core, T, topo):
     landed("W3", 32, bown[1], ("arr3", 2 * ne))
     landed("W3", bown[2], 160, ("arr3", 2 * ne))
     pick(v("FT"), v("W3"), v(OFFF, 0, 8))
-    dma("s", ("oc", 0, 1, 1), v("FT"), T.oc[:, :], codes(v("FT")))
+    dma("s", HBM, v("FT"), T.oc[:, :], codes(v("FT")))
     mm(PS, v("WQ"), v("FT"))
     for k in range(4):
-        dma("a", ("osc", 0, 1, 1), v("FTs"), T.osc[4 * k:4 * k + 4, :], T.FTs[32 * k:32 * k + 4, 0:128])
+        dma("a", HBM, v("FTs"), T.osc[4 * k:4 * k + 4, :], T.FTs[32 * k:32 * k + 4, 0:128])
     cp(v("Y"), PS)
-    dma("s", ("y", 0, 1, 1), v("Y"), T.y[:, :])
+    dma("s", HBM, v("Y"), T.y[:, :])
 
     for q in ("v", "a", "t", "g"):
         g.wait_ge(T.sem[SEM[q]], cnt[q])

@@ -10,26 +10,26 @@ TINY, BIG, MK, RND = 2.0 ** -100, 1e29, 256.0, 2.0 ** 27
 _f, _b, _u = "float32", "bfloat16", "uint16"
 SCRATCH = {}
 for _n, _w, _t in (
-        ("TB", 512, _b), ("UC", 4, _b), ("NZ", 144, _b), ("WT", 512, _b), ("ZB", 576, _b), ("UT", 512, _b), ("NU", 512, _b),
-        ("CI", 8, "int32"), ("CF", 8, _f), ("CK", 128, _f), ("J32", 32, _f), ("KI", 128, _b), ("IREF", 128, _b), ("OH2", 256, _b),
-        ("OHREF", 512, _b), ("QR", 128, _b), ("ZE", 520, _b), ("TIE", 128, _f), ("RM", 128, _f),
+        ("TB", 512, _b), ("UC", 4, _b), ("NZ", 144, _b), ("WT", 512, _b), ("ZB", 128, _b), ("UT", 512, _b), ("NU", 512, _b),
+        ("CI", 8, "int32"), ("CF", 8, _f), ("CK", 128, _f), ("J32", 32, _f), ("KI", 128, _b), ("IREF", 128, _b),
+        ("QR", 128, _b), ("ZE", 520, _b), ("TIE", 128, _f), ("RM", 128, _f),
         ("M32", 32, _f), ("C64", 64, _f), ("MASK", 64, _f),
-        ("MVC", 512, _b), ("S1", 512, _b), ("ZW", 512, _b), ("SC", 512, _b), ("NT0", 576, _b), ("NT1", 576, _b),
-        ("INFO", 512, _b), ("OHT", 512, _b), ("CMP", 128, _f), ("SM", 1536, _f),
-        ("V0", 576, _b), ("V1", 576, _b), ("NZ1", 80, _f), ("ZT", 512, _b),
-        ("TI1", 128, _f), ("TI0", 128, _f), ("IND", 128, _f), ("CS", 128, _f),
+        ("MVC", 512, _b), ("S1", 512, _b), ("SC", 512, _b), ("NT0", 576, _b), ("NT1", 576, _b),
+        ("INFO", 512, _b), ("OHT", 512, _b), ("CMP", 128, _f), ("SM", 1792, _f),
+        ("V0", 576, _b), ("V1", 576, _b), ("NZ1", 136, _f), ("ZT", 512, _b),
+        ("TI1", 128, _f), ("THP", 128, _f), ("INP", 128, _f), ("G128", 128, _b), ("TI0", 128, _f), ("IND", 128, _f), ("CS", 128, _f),
         ("D5", 512, _f), ("VT", 512, _b), ("Y", 128, _f), ("CM1", 128, _f), ("OF", 256, _u)):
     SCRATCH[_n] = ("sbuf", [128, _w], _t)
 for _n, _w in (("UQ", 128), ("NUQ", 128), ("TQ", 128), ("MVQ", 128), ("OHQ", 128), ("S1Q", 128), ("EQ", 512), ("N0Q", 144), ("N1Q", 144),
                ("WQ", 128), ("ZWQ", 128), ("SCQ", 128), ("L1S", 144), ("LD1", 144), ("NB", 160), ("W2", 416), ("PH1", 128), ("PG", 128),
-               ("S3", 96), ("W3", 160), ("ZQ", 128), ("MQ", 128), ("XQ", 128), ("FT", 128), ("HT", 32), ("R1", 18), ("R2", 16)):
+               ("S3", 96), ("W3", 160), ("ZQ", 128), ("MQ", 128), ("FT", 128), ("HT", 32), ("R1", 18), ("R2", 16)):
     SCRATCH[_n] = ("sbuf", [128, _w], "float8_e4m3fn_x4")
     SCRATCH[_n + "s"] = ("sbuf", [128, _w], "uint8")
 for _n, _w in (("PV", 2048), ("PA", 512), ("PB", 512), ("PC", 512), ("PD", 512)):
     SCRATCH[_n] = ("psum", [128, _w], _f)
 
-SEMAPHORES = ["sv", "sa", "st", "sg", "arrh", "arrg", "arr1", "arr2", "arr3", "arrp", "arrx", "r1c", "r1s", "r2c", "r2s"]
-SEMAPHORES += ["d%d" % i for i in range(24)] + ["l%d" % i for i in range(12)]
+SEMAPHORES = ["sv", "sa", "st", "sg", "arrh", "arrg", "arr1", "arr2", "arr3", "arr4", "arrp", "arrx", "r1", "r2"]
+SEMAPHORES += ["d%d" % i for i in range(24)] + ["l%d" % i for i in range(16)]
 
 
 def _helpers(topo, core):
@@ -48,7 +48,8 @@ def _dst(topo, d, s):
 def _hand_on(g, core, T, topo, owner, j):
     me = T.rank_of(owner)
     engs = topo.engines(core, T.cores[me - 1])
-    near, far = len(topo.engines(owner, core)), len(topo.engines(owner, core)) - len(engs)
+    near = len(topo.engines(owner, core))
+    far = near - len(engs)
     role = (j - me // 2) % 4
     done = []
 
@@ -64,19 +65,19 @@ def _hand_on(g, core, T, topo, owner, j):
     def pieces(x):
         ds = [d for d in (2 * j, 2 * j + 1) if d != me]
         k = len(engs) // len(ds)
-        call("arrh" if x else "arrg", (near if x else far) // 4,
+        call("arrh" if x else "arrg", far // 4,
              [RemoteDMATransfer(dst_ids=[_dst(topo, T.cores[d], core)], dma_engine_mask=_bits(engs[k * i:k * i + k]), remote_sem=T.sem.arrp,
                                 srcs=[view("HT", 16 * (d % 2), 16 * (d % 2) + 16, x)], dsts=[view("PH1", 16 * me, 16 * me + 16, x)])
               for i, d in enumerate(ds)])
 
     def relay(src, dst, w, sem):
-        if role >= 2 or src not in SHARED:
+        if src not in SHARED:
             return
-        cs = [T.cores[(me + DIRECT + 1 + 2 * role + i) % NR] for i in range(2)]
-        for x in (True, False):
-            call(src.lower() + ("c" if x else "s"), far // 2,
-                 [RemoteDMATransfer(dst_ids=[_dst(topo, c, core) for c in cs], dma_engine_mask=_bits(engs), remote_sem=T.sem[sem],
-                                    srcs=[view(src, 0, w, x)], dsts=[view(dst, w * me, w * me + w, x) for c in cs])])
+        cs = [T.cores[(me + DIRECT + 1 + 2 * (role % 2) + i) % NR] for i in range(2)]
+        x = role < 2
+        call(src.lower(), near // 2,
+             [RemoteDMATransfer(dst_ids=[_dst(topo, c, core) for c in cs], dma_engine_mask=_bits(engs), remote_sem=T.sem[sem],
+                                srcs=[view(src, 0, w, x)], dsts=[view(dst, w * me, w * me + w, x) for c in cs])])
 
     pieces(True)
     relay("R1", "LD1", SL, "arr1")
@@ -119,7 +120,7 @@ def rank_program(g, core, T, topo):
                     if not clash(a, lo, hi, st):
                         continue
                     same = a[4] == q and not dma and not a[6]
-                    if same and (q == "t" or not a[3]):
+                    if same and q == "t":
                         continue
                     if not (w or a[3]) and (same or not ps):
                         continue
@@ -212,9 +213,10 @@ def rank_program(g, core, T, topo):
     def codes(x):
         return ap(x).bitcast(dt.uint8)
 
-    def landed(n, lo, hi, tok):
+    def landed(n, lo, hi, tok, tok2=None):
         if hi > lo:
-            note("-", [], [v(n, lo, hi), v(n + "s", lo, hi)], tok, True)
+            note("-", [], [v(n, lo, hi)], tok, True)
+            note("-", [], [v(n + "s", lo, hi)], tok2 or tok, True)
 
     def send(x, transfers):
         transfers = [t if x else (t[0], pl(t[1]), pl(t[2]), t[3], t[4]) for t in transfers]
@@ -236,20 +238,17 @@ def rank_program(g, core, T, topo):
     engs = topo.engines(core, oc_[0])
     ne = len(engs)
     m_all = topo.mask(core, oc_[0])
-    e16 = topo.engines(core, hs[0])
-    far = [e for e in e16 if e not in engs]
+    far = [e for e in topo.engines(core, hs[0]) if e not in engs]
     bcast = 2 * ne * (NR - 1)
     par, k4 = me % 2, me // 2
     HBM = ("hbm", 0, 1, 1)
 
     def broadcast(dst, src, via, sem):
-        k = len(far) // 2
+        if via in SHARED:
+            for x in (True, False):
+                send(x, [([hs[(k4 + i + (0 if x else 2)) % 4]], v(via), src, _bits(es), via.lower()) for i, es in enumerate((engs, far))])
         for x in (True, False):
-            if via not in SHARED:
-                send(x, [(oc_, dst, src, m_all, sem)])
-                continue
-            send(x, [(oc_[:DIRECT], dst, src, m_all, sem)] +
-                 [([hs[(k4 + i) % 4]], v(via), src, _bits(far[k * i:k * i + k]), via.lower() + ("c" if x else "s")) for i in range(2)])
+            send(x, [(oc_[:DIRECT] if via in SHARED else oc_, dst, src, m_all, sem)])
 
     def to_helpers(x, es, sem):
         k = len(es) // 4
@@ -279,120 +278,121 @@ def rank_program(g, core, T, topo):
 
     ci, cf = (lambda i: v("CI", i, i + 1)), (lambda i: v("CF", i, i + 1))
     P, I16, S16, Q4, P4, Q2 = cf(0), cf(1), cf(2), cf(3), cf(4), cf(5)
+    dma("s", v("UC"), HBM, None, T.u[:, 0:4])
     dma("s", v("TB"), HBM, None, T.tb[:, :])
-    dma("a", v("UC"), HBM, None, T.u[:, 0:4])
     for t in range(2):
-        dma("a", v("NZ", 72 * t, 72 * t + 64), HBM, None, T.nz[:, 64 * t:64 * t + 64])
+        dma("s", v("NZ", 72 * t, 72 * t + 64), HBM, None, T.nz[:, 64 * t:64 * t + 64])
+    dma("s", v("WT"), v("TB"), None, T.w[:, :])
+    iota(ci(0), [[0, 1]], 1, False)
     iota(P, [[0, 1]], 1)
     iota(v("KI"), [[1, 128]], 0)
-    iota(ci(0), [[0, 1]], 1, False)
-    iota(v("OH2"), [[0, 8], [1, 16], [16, 2]], 0)
-    iota(v("J32"), [[1, 32]], 0)
     iota(v("IREF"), [[0, 8], [1, 16]], 0)
+    iota(v("J32"), [[1, 32]], 0)
+    iota(v("QR"), [[0, 8], [1, 4], [0, 4]], 0)
 
     J8, J16, Z128, HD = v("J32", 0, 8), v("J32", 0, 16), v("ZB", 0, 128), v("ZE", 4, 516, 4)
-    ms(v("ZB"), 0.0)
-    ms(v("ZE"), 0.0)
-    ts(HD, v("KI"), P, A.is_equal, 0.5, A.mult)
-    ts(ci(1), ci(0), 15, A.bitwise_and)
-    ts(ci(2), ci(0), 4, A.logical_shift_right)
-    ts(ci(3), ci(0), 3, A.bitwise_and)
-    ts(ci(4), ci(0), 2, A.logical_shift_right)
-    ts(ci(5), ci(0), 1, A.bitwise_and)
-    ts(ci(6), ci(0), 1, A.logical_shift_right)
-    H16, P32, ia, ib = ck(), ck(), ck(), ck()
-    act(v("MVC"), v("ZB", 0, 512))
-    act(v("INFO"), v("ZB", 0, 512))
+    H16, P32, ia, ib, ct = ck(), ck(), ck(), ck(), ck()
     E = [v("EQ", 128 * b, 128 * b + 128) for b in range(4)]
     PVb = [v("PV", 512 * b, 512 * b + 144) for b in range(4)]
 
     def unit(b):
         quant(E[b], v("ZE", 4 - b, 516 - b))
 
-    unit(0)
-    cp(v("CF", 1, 7), v("CI", 1, 7))
-    for b in range(4):
-        ts(v("NU", b, 512, 4), Z128, v("UC", b, b + 1), A.subtract)
-    for b in range(2):
-        ts(v("UT", b, 512, 4), Z128, v("UC", b, b + 1), A.add)
-        lin(v("UT", b + 2, 512, 4), Z128, 1.0, v("UC", b + 2, b + 3))
-    lin(H16, S16, 16.0, 0.0)
-    lin(P32, P, 1.0, 32.0)
-    for e, st, x in ((1, 10, I16), (25, 6, I16), (0, 10, H16), (16, 6, H16)):
-        lin(v("MVC", e, e + st + 1, st), v("ZB", 0, 2), 1.0, x)
-    for h in range(2):
-        act(v("OHREF", h, 512, 2), v("OH2"))
-    for t in range(2):
-        act(v("NZ", 72 * t + 64, 72 * t + 72), v("ZB", 0, 8))
-
     def noise(t):
         for a in range(NR):
             act(v("NT%d" % t, 72 * a, 72 * a + 72), v("NZ", 72 * t, 72 * t + 72))
 
-    noise(0)
+    ms(Z128, 0.0)
+    ms(v("ZE"), 0.0)
+    ms(v("MVC"), 0.0)
+    ts(ci(1), ci(0), 15, A.bitwise_and)
+    ts(ci(2), ci(0), 4, A.logical_shift_right)
+    ts(ci(3), ci(0), 3, A.bitwise_and)
+    ts(ci(4), ci(0), 2, A.logical_shift_right)
+    ts(ci(5), ci(0), 1, A.bitwise_and)
+    ts(ci(6), ci(0), 1, A.logical_shift_right)
+    ts(HD, v("KI"), P, A.is_equal, 0.5, A.mult)
+    cp(v("CF", 1, 6), v("CI", 1, 6))
+    for n, b in (("OHT", 2), ("OHT", 3), ("ZT", 2), ("ZT", 3), ("SC", 3)):
+        act(v(n, b, 512, 4), Z128)
+    for b in range(4):
+        ts(v("NU", b, 512, 4), Z128, v("UC", b, b + 1), A.subtract)
+        lin(v("UT", b, 512, 4), Z128, 1.0, v("UC", b, b + 1))
+    lin(H16, S16, 16.0, 0.0)
+    for e, x in ((8, I16), (0, H16)):
+        lin(v("MVC", e, e + 6, 5), v("ZB", 0, 2), 1.0, x)
+    lin(P32, P, 1.0, 32.0)
+    for b in range(4):
+        act(v("INFO", 128 * b, 128 * b + 128), Z128)
+    for t in range(2):
+        act(v("NZ", 72 * t + 64, 72 * t + 72), v("ZB", 0, 8))
+    act(ct, P, F.Relu, bias=-16.0)
     for b, x in ((1, 0.0), (2, 0.0), (0, 1.0)):
         lin(v("S1", b, 512, 4), Z128, 1.0, x)
-    act(v("SC", 3, 512, 4), Z128)
-    for b in (2, 3):
-        act(v("ZT", b, 512, 4), Z128)
-    lin(v("ZW"), v("ZB", 0, 512), 1.0, 2.0)
+    noise(0)
 
     TQ = v("TQ")
+    unit(0)
     quant(v("NUQ"), v("NU"))
     quant(TQ, v("TB"))
-    to_helpers(True, e16, "arrh")
-    dma("s", v("WT"), HBM, None, T.w[:, :])
+    to_helpers(True, far, "arrh")
+    to_helpers(False, engs, "arrg")
+    pown, town = v("PH1", 16 * me, 16 * me + 16), v("TQ", 16 * me, 16 * me + 16)
+    dma("s", pown, town, codes(pown), codes(town))
+    dma("s", pl(pown), pl(town))
     quant(v("UQ"), v("UT"))
-    PX, PS, PL, PF = v("PA", 0, 128), v("PB", 0, 128), v("PC", 0, 128), v("PD", 0, 144)
+    PX, PS, PL, PF = v("PA", 0, 128), v("PB", 0, 128), v("PC", 0, 128), v("PD", 0, 128)
     mm(PX, TQ, v("NUQ"), True, False)
     mm(PX, v("UQ"), TQ, False, True)
     mm(PS, TQ, v("UQ"))
     ts(v("TIE"), v("KI"), P, A.is_lt, TINY, A.mult)
     unit(1)
-    rk, va, vb, OFF1, ct = sm(), sm(), sm(), of(4), ck()
+    rk, va, vb, OFF1 = sm(), sm(), sm(), of(4)
     tt(v("CMP"), PX, v("TIE"), A.is_lt)
     ts(ia, P, float(me), A.is_equal, MK, A.mult)
-    ts(ib, P, float(me + 16), A.is_equal, -0.125, A.mult)
     red(rk, v("CMP"))
     quant(v("MVQ"), v("MVC"))
-    ts(v("OHT"), v("OHREF"), rk, A.is_equal)
+    ts(v("OHT", 0, 512, 4), v("IREF"), rk, A.is_equal)
+    ts(v("OHT", 1, 512, 4), v("IREF"), 16.0, A.add, rk, A.is_equal)
     ts(va, rk, 31.5, A.is_ge, 1000.0, A.mult)
-    ts(v("INFO", 0, 1), v("PB", 0, 1), 0.0, A.is_gt)
+    ts(ib, P, float(me + 16), A.is_equal, -0.125, A.mult)
     quant(v("OHQ"), v("OHT"))
     mm(PL, v("OHQ"), v("MVQ"))
     ts(vb, va, rk, A.add, P32, A.min)
+    ts(v("INFO", 0, 1), v("PB", 0, 1), 0.0, A.is_gt)
     tt(v("INFO", 3, 4), ia, ib, A.add)
     ts(v("INFO", 1, 2), vb, RND, A.add, RND, A.subtract)
-    ts(ct, P, -16.0, A.add, 0.0, A.max)
     tt(v("INFO", 2, 3), vb, v("INFO", 1, 2), A.subtract)
-    cp(v("INFO", 4, 8), v("PC", 4, 8))
-    cp(OFF1, v("PC", 0, 4))
+    cp(v("INFO", 4, 8), v("PC", 0, 4))
+    ts(v(OFF1, 0, 1), v("PC", 0, 1), v("PC", 2, 3), A.add)
+    for b in range(2):
+        lin(v("OHT", b, 512, 4), Z128, 1.0, 2.0)
     quant(v("L1S", 16, 144), v("INFO"))
     pick(v("L1S", 0, 16), TQ, v(OFF1, 0, 1))
     own, mine = v("LD1", SL * me, SL * me + SL), v("L1S", 0, SL)
     broadcast(own, mine, "R1", "arr1")
-    to_helpers(False, far, "arrg")
     dma("s", own, mine, codes(own), codes(mine))
     dma("s", pl(own), pl(mine))
-    pown, town = v("PH1", 16 * me, 16 * me + 16), v("TQ", 16 * me, 16 * me + 16)
-    dma("s", pown, town, codes(pown), codes(town))
-    dma("s", pl(pown), pl(town))
 
     WN, J18, F16, JB, FLW = sm(160), sm(16), sm(16), sm(32), sm(32)
+    JZ, WZ, CZ, CCW = sm(32), sm(168), ck(2), sm(16)
     iota(J18, [[SL, 16]], 0)
     iota(v(WN, 16, 24), [[0, 8]], 0, True, SL * NR)
-    iota(v("QR"), [[0, 8], [1, 4], [0, 4]], 0)
+    iota(v("G128"), [[1, 8], [0, 16]], 0)
     iota(v("C64"), [[0, 8], [1, 8]], 0)
+    iota(JZ, [[1, 2], [72, 16]], 0, True, 68)
     iota(v(JB, 0, 16), [[1, 16]], 0)
+    iota(CCW, [[0, 8], [-16, 2]], 0, True, 112)
     iota(v("RM"), [[0, 8], [1000, 16]], 0)
-    iota(v(FLW, 0, 8), [[0, 8]], 0, True, 400)
-    iota(v(FLW, 8, 16), [[SL, 8]], 0, True, 256)
-    iota(v(FLW, 16, 24), [[16, 8]], 0)
-    TIE8, TM0, TMB, TM1, TMP, c8, CB, C2, C3, EP, Q22, Q8, THM, G8, cx = (
-        ck(8), ck(8), ck(8), ck(8), ck(8), ck(), ck(), ck(2), ck(), ck(), ck(), ck(), ck(8), ck(), ck())
+    iota(v(FLW, 0, 8), [[-16, 8]], 0, True, 400)
+    iota(v(FLW, 8, 16), [[SL - 16, 8]], 0, True, 256)
+    iota(v(FLW, 16, 24), [[0, 8]], 0)
+    TIE8, TM0, TMB, TM1, TMP, c8, CB, C2, C3, EP, EQ1, Q22, Q8, THM, G8, cx = (
+        ck(8), ck(8), ck(8), ck(8), ck(8), ck(), ck(), ck(2), ck(), ck(), ck(), ck(), ck(), ck(8), ck(), ck())
     lin(c8, I16, 8.0, -48.0)
     lin(TIE8, J8, -0.125, 0.0)
     lin(F16, J16, 0.0, 0.0)
+    ts(v(OFF1, 2, 3), v("PC", 1, 2), v("PC", 3, 4), A.add)
     ts(v("S1", 3, 512, 4), v("IREF"), P, A.is_equal, ct, A.add)
     quant(v("N0Q"), v("NT0"))
     unit(2)
@@ -405,42 +405,48 @@ def rank_program(g, core, T, topo):
     pick(v("NB", 144, 160), TQ, v(OFF1, 2, 3))
     lin(CB, G8, c8, 0.0)
     lin(TMB, TM0, 1.0, -MK)
-    lin(v(C2, 0, 1), CB, 2.0, 7.0)
+    lin(v(CZ, 0, 1), CB, 2.0, 7.0)
+    lin(v(CZ, 1, 2), CB, 2.0, 8.0)
     pick(v("W2", 400, 416), TQ, v(OFF1, 0, 1))
+    lin(cx, G8, 72.0, 65.0)
     noise(1)
+    lin(v(C2, 0, 1), CB, 2.0, 7.0)
     lin(v(C2, 1, 2), CB, 2.0, 167.0)
     lin(TMP, TIE8, 1.0, MK)
     lin(Q22, Q2, 2.0, 0.0)
-    lin(cx, G8, 72.0, 65.0)
-    lin(v("NZ1", 64, 80), J16, 0.0, 0.0)
+    act(v("NZ1", 64, 136), v("ZB", 0, 72))
     OFT, OFG0, OX1, OX2 = of(8), of(), of(4), of(4)
     ts(ci(7), ci(6), float(k4 + 1), A.add)
-    ts(C3, G8, Q2, A.mult, 80.0, A.mult)
     ts(OFT, J8, 0.0, A.add)
+    ts(C3, G8, Q2, A.mult, 80.0, A.mult)
     ts(ci(7), ci(7), 3, A.bitwise_and)
     ts(OFG0, S16, 0.0, A.add)
     ts(v("M32"), v("J32"), P4, A.is_equal)
     ts(EP, ci(7), 2.0, A.mult, float(par), A.add)
-    ts(THM, J8, S16, A.is_equal, 16.5, A.mult)
+    ts(THM, J8, S16, A.is_equal)
     ts(Q8, I16, 7.0, A.min)
     ts(EP, EP, I16, A.subtract, G8, A.mult)
-    ts(v("MASK"), v("C64"), S16, A.is_equal)
+    ts(OX1, v("J32", 0, 4), 144.0, A.mult, cx, A.add)
     ts(v("SC", 0, 512, 4), v("QR"), Q4, A.is_equal, 4.0, A.mult)
     ts(TM1, J8, EP, A.subtract, I16, A.is_equal)
     for b in (1, 2):
         ts(v("SC", b, 512, 4), v("IREF"), I16, A.is_equal, 2.0, A.mult)
-    ts(TM1, TM1, MK, A.mult)
+    lin(C3, C3, 1.0, 3.5)
+    lin(EQ1, EP, 1.0, I16)
+    lin(TM1, TM1, MK, 0.0)
     quant(v("N1Q"), v("NT1"))
 
     landed("LD1", 0, own[1], ("arr1", bcast))
     landed("LD1", own[2], 144, ("arr1", bcast))
-    mm(PF, v("S1Q"), v("LD1"))
+    mm(PF, v("S1Q"), v("LD1", 16, 144))
     for b in range(4):
         mm(PVb[b], E[b], v("LD1"), False, True)
-    FIT = v("PD", 16, 144, SL)
+    FIT = v("PD", 0, 128, SL)
     mx, K0, cm, s0, gv, t1, O0, OD0 = sm(), sm(8), sm(8), sm(), sm(), sm(), sm(160), sm(8)
-    OP0, OX0, TG0, OFFH, OFE = of(), of(), of(), of(18), of(4)
-    quant(v("ZWQ"), v("ZW"))
+    OPZ, OX0, TG0, OFFH, OFE, TGZ, g7 = of(2), of(), of(), of(18), of(4), of(), sm()
+    OP0 = v(OPZ, 0, 1)
+    quant(v("ZWQ"), v("OHT"))
+    quant(v("WQ"), v("WT"))
     red(mx, FIT, A.max, True)
     tt(K0, FIT, TMB, A.subtract)
     act(v("V0", 0, 576, 4), PVb[0])
@@ -448,16 +454,19 @@ def rank_program(g, core, T, topo):
     for b in range(1, 4):
         act(v("V0", b, 576, 4), PVb[b])
     quant(v("SCQ"), v("SC"))
-    ts(OX1, v("J32", 0, 4), 144.0, A.mult, cx, A.add)
-    ts(OP0, s0, v(C2, 0, 1), A.add)
+    ts(v("THP"), v("G128"), EQ1, A.not_equal, BIG, A.mult)
+    tt(v(F16, 0, 8), K0, TMP, A.subtract)
+    ts(OPZ, CZ, s0, A.add)
     ts(gv, s0, 0.0, A.is_lt, 8.0, A.mult)
     ts(t1, s0, -1.0, A.mult, s0, A.max)
+    ts(g7, s0, 0.0, A.is_lt, 7.0, A.add)
     scatter(WN, J18, OP0)
     ts(OX0, gv, s0, A.subtract, 7.0, A.add)
-    ts(TG0, t1, -1.0, A.mult, 7.0, A.add)
+    ts(TGZ, g7, t1, A.subtract)
+    tt(TM1, TM1, TIE8, A.add)
     quant(v("NB", 0, 144), v("V0"))
     ts(v(OFFH, par, par + 16), WN, I16, A.add, off=OX0)
-    scatter(O0, J16, OP0)
+    scatter(WZ, JZ, OPZ)
     hown = v("W2", 16 * me, 16 * me + 16)
     pick(hown, v("NB"), v(OFFH, me + par, me + par + 1))
     broadcast(hown, hown, "R2", "arr2")
@@ -467,9 +476,9 @@ def rank_program(g, core, T, topo):
     gown = v("PG", 64 * par, 64 * par + 64)
     BR16, FS, FB, TP, B32 = v(JB, 16, 32), sm(160), sm(16), sm(16), sm(32)
     BR = v(JB, 16, 24)
-    G, z1, ZR, DG, BSp, Zp, cc, m1, f2, KB, KBm, KBp, FLA, TA = (
-        sm(8), sm(8), sm(8), sm(16), sm(16), sm(), sm(8), sm(8), sm(8), sm(8), sm(8), sm(8), sm(64), sm(8))
-    LZ = of(16)
+    ZR, DG, BSp, Zp, cc, m1, f2, KB, KBm, KBp, FLA, TA = (
+        sm(16), sm(16), sm(16), sm(), sm(16), sm(8), sm(8), sm(8), sm(8), sm(8), sm(64), sm(8))
+    LZ, kb = of(16), sm()
     for b in range(4):
         mm(PVb[b], E[b], v("N1Q"))
     for b in range(4):
@@ -477,50 +486,43 @@ def rank_program(g, core, T, topo):
     for b in range(4):
         mm(PVb[b], E[b], v("N1Q"), True, False)
         mm(PVb[b], E[b], v("LD1"), False, True)
-    gather(BR16, O0, TG0)
-    ts(OFE, v(O0, 0, 8, 2), 16.0, A.mult, I16, A.add)
-    tt(v(F16, 0, 8), K0, TMP, A.subtract)
-    tt(G, BR, J8, A.is_equal)
-    ts(z1, BR, 72.0, A.mult, 68.0, A.add)
     scatter(FS, F16, OP0)
-    tt(ZR, z1, G, A.add)
+    ts(TG0, t1, -1.0, A.mult, 7.0, A.add)
+    gather(ZR, WZ, TGZ)
+    scatter(O0, J16, OP0)
+    gather(cc, CCW, TGZ)
+    gather(FB, FS, TG0)
+    ts(LZ, ZR, Q22, A.add, off=OFG0)
+    ts(OFE, v(O0, 0, 8, 2), 16.0, A.mult, I16, A.add)
+    gather(BR16, O0, TG0)
+    lin(f2, v(FB, 0, 8), 1.0, -16.0)
+    tt(m1, v(FB, 0, 8), v(cc, 0, 8), A.min)
+    gather(DG, v("V0"), v(LZ, 0, 1))
     pick(gown, v("PH1"), OFE)
     for x in (True, False):
         send(x, [([T.cores[me ^ 1]], gown, gown, m_all, "arrx")])
-    act(OD0, v(O0, 0, 16, 2))
-    dma("s", HBM, OD0, T.od[0:1, :], T.SM[0:1, OD0[1]:OD0[1] + 8])
-    ts(LZ, ZR, Q22, A.add, off=OFG0)
-    gather(FB, FS, TG0)
-    ts(OX2, OX1, 1.0, A.add)
-    tt(TM1, TM1, TIE8, A.add)
-    lin(cc, G, -16.0, 112.0)
-    lin(f2, v(FB, 0, 8), 1.0, -16.0)
-    gather(DG, v("V0"), v(LZ, 0, 1))
-    gather(BSp, BR, OFG0)
-    gather(TP, J16, TG0)
-    tt(v("INFO", 9, 264, 4), v("V0"), v("MASK"), A.mult, off=OX1)
-    tt(v("INFO", 10, 264, 4), v("V0"), v("MASK"), A.mult, off=OX2)
-    for b in range(2):
-        lin(v("ZT", b, 512, 4), HD, v(DG, b, b + 1), 0.0)
-    lin(Zp, v(DG, 0, 1), 1.0, v(DG, 1, 2))
-    for b in range(4):
-        act(v("V1", b, 576, 4), PVb[b])
-    lin(v(B32, 0, 16), TP, 8.0, 0.0)
-    lin(v(B32, 16, 32), TP, 8.0, 64.0)
-    lin(C3, C3, 1.0, 3.5)
-    lin(THM, THM, 1.0, -1.0)
-    tt(m1, v(FB, 0, 8), cc, A.min)
-    ts(TA, BR, v(BSp, 0, 1), A.not_equal, -BIG, A.mult)
-    quant(v("ZQ"), v("ZT"))
-    mm(PL, v("ZWQ"), v("ZQ"))
     tt(KB, m1, f2, A.max)
-    quant(v("XQ"), v("INFO"))
-    mm(v("PD", 0, 128), v("SCQ"), v("XQ"))
-    act(FLA, v("PD", 2, 66))
+    for b in range(2):
+        ts(v("ZT", b, 512, 4), HD, v(DG, b, b + 1), A.mult)
+    lin(Zp, v(DG, 0, 1), 1.0, v(DG, 1, 2))
+    act(OD0, v(O0, 0, 16, 2))
+    gather(BSp, BR, OFG0)
     tt(KBm, KB, TM1, A.add)
     tt(KBp, KB, TMP, A.add)
+    quant(v("ZQ"), v("ZT"))
+    mm(PL, v("ZWQ"), v("ZQ"))
+    gather(TP, J16, TG0)
+    red(kb, KBm, A.max, True)
+    for b in range(4):
+        act(v("V1", b, 576, 4), PVb[b])
+    lin(KBp, KBp, 1.0, kb)
+    lin(v(B32, 0, 16), TP, 8.0, 0.0)
+    lin(v(B32, 16, 32), TP, 8.0, 64.0)
+    ts(v("MASK"), v("C64"), S16, A.is_equal)
+    ts(TA, BR, v(BSp, 0, 1), A.not_equal, -BIG, A.mult)
+    ts(OX2, OX1, 1.0, A.add)
     ts(v("TI0"), PL, Zp, A.is_lt, TINY, A.mult)
-    quant(v("WQ"), v("WT"))
+    tt(v("INFO", 9, 264, 4), v("V0"), v("MASK"), A.mult, off=OX1)
     tt(v("TI1"), TA, v("TI0"), A.add, off=OFT)
 
     landed("W2", 0, hown[1], ("arr2", bcast))
@@ -532,65 +534,73 @@ def rank_program(g, core, T, topo):
     mm(PX, H, v("NUQ"), False, True)
     for b in range(4):
         mm(v("PV", 512 * b, 512 * b + 128), E[b], H)
-    Km, Kp, nx, sj, sg, ab, Mp, BS, O1, A1 = sm(8), sm(8), sm(), sm(8), sm(), sm(), sm(), sm(160), sm(160), sm(16)
+    Kp, nx, sj, sg, ab, Mp, BS, O1, A1 = sm(8), sm(), sm(8), sm(), sm(), sm(), sm(160), sm(160), sm(16)
     OP1, TG1, OFF3, OFFG = of(2), of(), of(16), of(32)
-    quant(v("W2", 256, 400), v("V1"))
     ts(v("IND"), PS, 0.0, A.is_gt)
+    tt(v("INP"), PS, v("THP"), A.is_gt)
     op("v", lambda: g.vector.tensor_tensor_scan(ap(v("CS")), ap(v("RM")), ap(v("IND")), 0.0, A.min, A.add), [v("RM"), v("IND")], [v("CS")])
+    act(v("CMP"), v("INP"), F.Identity, scale=-1.0, accum_out=nx)
     tt(v("CM1"), PX, v("TI1"), A.is_lt)
-    tt(Km, v("CS", 15, 128, 16), KBm, A.add)
     tt(Kp, v("CS", 15, 128, 16), KBp, A.add)
-    red(nx, Km, A.max, True)
     act(sj, Kp, F.Sign, bias=nx, accum_out=sg)
+    act(ab, sg, F.Abs)
     for b in range(4):
         act(v("D5", b, 512, 4), v("PV", 512 * b, 512 * b + 128))
     red(Mp, v("CM1"))
-    ts(v("INFO", 272, 400, 4), v("M32"), Mp, A.mult, 16.0, A.min)
-    ts(v("INFO", 401, 432, 4), THM, Mp, A.is_gt, 64.0, A.mult)
+    tt(v("INFO", 10, 264, 4), v("V0"), v("MASK"), A.mult, off=OX2)
     ts(OP1, C2, sg, A.add, 0.5, A.mult)
-    ts(ab, sg, -1.0, A.mult, sg, A.max)
-    quant(v("MQ"), v("INFO"))
-    mm(PL, v("SCQ"), v("MQ"))
+    ts(v("INFO", 272, 400, 4), v("M32"), Mp, A.mult)
+    ts(v("INFO", 401, 432, 4), THM, Mp, A.mult)
     scatter(BS, B32, OP1)
     ts(TG1, ab, -0.5, A.mult, C3, A.add)
-    scatter(O1, JB, OP1)
+    quant(v("MQ"), v("INFO"))
+    mm(PL, v("SCQ"), v("MQ"))
     ts(OFF3, BS, I16, A.add, off=TG1)
-    gather(A1, O1, TG1)
-    ts(OFFG, v("PC", 68, 100), Q4, A.add)
+    scatter(O1, JB, OP1)
     pick(v("S3"), v("PG"), v(OFF3, 8, 14))
     bown = v("W3", 32 + 32 * k4, 64 + 32 * k4)
     grp = [T.cores[par + 2 * ((k4 + i) % 4)] for i in (1, 2, 3)]
     h, q = ne // 2, ne // 4
     for x, cuts in ((True, (0, h, h + q, ne)), (False, (0, q, h, ne))):
-        send(x, [([c], bown, v("S3", 32 * i, 32 * i + 32), _bits(engs[cuts[i]:cuts[i + 1]]), "arr3") for i, c in enumerate(grp)])
+        send(x, [([c], bown, v("S3", 32 * i, 32 * i + 32), _bits(engs[cuts[i]:cuts[i + 1]]), "arr3" if x else "arr4") for i, c in enumerate(grp)])
 
-    xa, xb, xc = sm(), sm(), sm()
+    xa, xb, xc, d1, d2, hx, ho, fs = sm(), sm(), sm(), sm(), sm(), sm(), sm(), sm(8)
     E0, E1, E2, HL0, HL1, OFFF = of(), of(), of(), of(16), of(16), of(16)
     X, O = v(A1, 14, 15), v(A1, 15, 16)
-    dma("s", HBM, O1, T.od[1:2, :], T.SM[0:1, O1[1]:O1[1] + 8])
-    ts(xa, X, float(me), A.not_equal, 8.0, A.mult)
-    ts(xb, X, O, A.not_equal, 16.0, A.mult)
-    ts(xc, X, O, A.not_equal)
-    tt(v("VT"), v("NZ1", 0, 72), v("D5"), A.add, off=OFFG)
+    ts(OFFG, v("PC", 68, 100), Q4, A.add)
+    gather(A1, O1, TG1)
+    quant(v("W2", 256, 400), v("V1"))
+    act(d1, X, F.Sign, bias=float(-me))
+    act(d2, O, F.Sign, scale=-1.0, bias=X)
+    act(fs, v("PC", 100, 108), F.Sign, scale=-1.0, bias=31.0)
+    act(FLA, v("PC", 2, 66))
+    act(xa, d1, F.Abs, scale=8.0)
+    act(xb, d2, F.Abs, scale=16.0)
+    act(xc, d2, F.Abs)
+    lin(v(FLW, 24, 32), fs, 64.0, 64.0)
+    lin(hx, X, 16.0, I16)
+    lin(ho, O, 16.0, I16)
+    tt(v("VT"), v("NZ1"), v("D5"), A.add, off=OFFG)
     ts(E0, xa, xb, A.add, X, A.add)
     ts(E1, xa, xc, A.mult, O, A.add)
-    tt(v(FLW, 24, 32), v("PC", 100, 108), v(FLW, 16, 24), A.add)
-    quant(v("W2", 128, 256), v("VT"))
     ts(E2, O, 8.0, A.mult, Q8, A.add)
-    ts(HL0, FLW, I16, A.add, off=E0)
-    ts(HL1, v(FLW, 16, 32), I16, A.add, off=E1)
+    quant(v("W2", 128, 256), v("VT"))
+    ts(HL0, FLW, hx, A.add, off=E0)
+    ts(HL1, v(FLW, 16, 32), ho, A.add, off=E1)
     pick(bown, v("PG"), v(OFF3, 14, 16))
     ts(OFFF, FLA, 0.0, A.add, off=E2)
     pick(v("W3", 0, 16), v("W2"), v(HL0, 0, 1))
     pick(v("W3", 16, 32), v("W2"), v(HL1, 0, 1))
 
-    landed("W3", 32, bown[1], ("arr3", 2 * ne))
-    landed("W3", bown[2], 160, ("arr3", 2 * ne))
+    landed("W3", 32, bown[1], ("arr3", ne), ("arr4", ne))
+    landed("W3", bown[2], 160, ("arr3", ne), ("arr4", ne))
     pick(v("FT"), v("W3"), v(OFFF, 0, 8))
     dma("s", HBM, v("FT"), T.oc[:, :], codes(v("FT")))
     mm(PS, v("WQ"), v("FT"))
     for k in range(4):
         dma("a", HBM, v("FTs"), T.osc[4 * k:4 * k + 4, :], T.FTs[32 * k:32 * k + 4, 0:128])
+    for t, x in enumerate((OD0, O1)):
+        dma("a", HBM, x, T.od[t:t + 1, :], T.SM[0:1, x[1]:x[1] + 8])
     cp(v("Y"), PS)
     dma("s", HBM, v("Y"), T.y[:, :])
 

@@ -3,37 +3,45 @@ from concourse.mybir import dt, AluOpType, AxisListType, ActivationFunctionType
 
 A = AluOpType
 F = ActivationFunctionType
-NR, SL, DIRECT = 8, 18, 3
-SHARED = ("R2",)
-TINY, BIG, MK, RND = 2.0 ** -100, 1e29, 256.0, 2.0 ** 27
+NR, SL, NI = 8, 17, 3
+NL1, DP = NR * SL, 288
+TINY, MK, RND = 2.0 ** -100, 256.0, 2.0 ** 27
+
+ORDER = [0,9,6,5,8,17,10,16,51,11,15,7,18,19,78,32,23,27,21,25,22,28,24,26,1,2,3,34,29,45,20,62,46,47,31,30,35,36,4,40,41,48,49,33,53,54,55,56,57,13,12,85,37,14,58,68,38,59,39,87,76,52,84,61,103,64,86,82,105,102,83,92,91,90,107,80,50,63,108,89,116,79,119,69,70,43,42,44,60,88,65,66,73,67,120,121,77,75,74,72,71,145,147,106,81,101,144,125,104,118,133,141,124,140,111,95,96,100,93,94,97,99,98,137,132,110,109,114,122,123,157,117,163,162,115,139,112,135,165,160,158,159,161,136,113,169,164,167,170,168,138,129,166,171,172,134,173,174,188,177,176,175,185,210,180,189,200,184,178,203,202,142,181,192,193,179,186,187,128,195,194,130,196,209,206,207,190,205,277,197,182,183,191,198,199,149,152,151,148,146,155,154,153,150,156,211,201,127,214,143,204,208,215,213,218,217,228,224,131,229,216,126,230,231,212,223,220,222,232,219,233,234,221,245,242,243,244,235,236,225,239,249,237,246,226,247,240,238,258,251,241,250,252,248,256,257,254,255,227,259,261,260,262,263,264,253,268,269,265,266,270,271,272,273,274,275,276,267,278,280,279,281,284,283,290,282,289,288,291,285,287,286]
 
 _f, _b, _u = "float32", "bfloat16", "uint16"
 SCRATCH = {}
 for _n, _w, _t in (
-        ("TB", 512, _b), ("UC", 4, _b), ("NZ", 144, _b), ("WT", 512, _b), ("ZB", 128, _b), ("UT", 512, _b), ("NU", 512, _b),
+        ("TB", 512, _b), ("UC", 4, _b), ("WT", 512, _b), ("ZB", 148, _b), ("UT", 512, _b), ("NU", 512, _b),
         ("CI", 8, "int32"), ("CF", 8, _f), ("CK", 128, _f), ("J32", 32, _f), ("KI", 128, _b), ("IREF", 128, _b),
-        ("QR", 128, _b), ("ZE", 520, _b), ("TIE", 128, _f), ("RM", 128, _f),
-        ("M32", 32, _f), ("C64", 64, _f), ("MASK", 64, _f),
-        ("MVC", 512, _b), ("S1", 512, _b), ("SC", 512, _b), ("NT0", 576, _b), ("NT1", 576, _b),
-        ("INFO", 512, _b), ("OHT", 512, _b), ("CMP", 128, _f), ("SM", 1792, _f),
-        ("V0", 576, _b), ("V1", 576, _b), ("NZ1", 136, _f), ("ZT", 512, _b),
-        ("TI1", 128, _f), ("THP", 128, _f), ("INP", 128, _f), ("G128", 128, _b), ("TI0", 128, _f), ("IND", 128, _f), ("CS", 128, _f),
-        ("D5", 512, _f), ("VT", 512, _b), ("Y", 128, _f), ("CM1", 128, _f), ("OF", 256, _u)):
+        ("QREF", 128, _b), ("G128", 128, _b), ("ZE", 520, _b), ("TIE", 128, _b),
+        ("ZW", 512, _b), ("CM", 512, _b), ("INF", 580, _b), ("S1", 512, _b), ("SC", 512, _b), ("NT", 608, _b),
+        ("SM", 1024, _f), ("V0", 4 * NL1, _b), ("DW", 16 + 4 * DP, _b), ("NZ1", 192, _f), ("DS", 128, _f), ("Z2", 128, _f),
+        ("CMT", 256, _f), ("MW", 256, _b), ("TAB", 256, _f), ("FLA", 80, _f), ("SG", NL1 + 16, _f),
+        ("Y", 128, _f), ("OF", 256, _u), ("KY", 64, _b), ("KS", 64, _f), ("OK", 8, _u)):
     SCRATCH[_n] = ("sbuf", [128, _w], _t)
-for _n, _w in (("UQ", 128), ("NUQ", 128), ("TQ", 128), ("MVQ", 128), ("OHQ", 128), ("S1Q", 128), ("EQ", 512), ("N0Q", 144), ("N1Q", 144),
-               ("WQ", 128), ("ZWQ", 128), ("SCQ", 128), ("L1S", 144), ("LD1", 144), ("NB", 160), ("W2", 416), ("PH1", 128), ("PG", 128),
-               ("S3", 96), ("W3", 160), ("ZQ", 128), ("MQ", 128), ("FT", 128), ("HT", 32), ("R1", 18), ("R2", 16)):
+for _n, _w in (("UQ", 128), ("NUQ", 128), ("TQ", 128), ("ZWQ", 128), ("CQ", 128), ("S1Q", 128), ("EQ", 512), ("NQ", 152),
+               ("WQ", 128), ("SCQ", 128), ("L1S", 144), ("L0", 128), ("LD1", 160), ("NB", 152), ("HS", 144), ("W2", 272), ("PH1", 128), ("PG", 128),
+               ("S3", 128), ("W3", 160), ("ZQ", 128), ("FT", 128), ("HT", 32), ("RI", NI), ("R2", 16), ("R3", 32)):
     SCRATCH[_n] = ("sbuf", [128, _w], "float8_e4m3fn_x4")
     SCRATCH[_n + "s"] = ("sbuf", [128, _w], "uint8")
 for _n, _w in (("PV", 2048), ("PA", 512), ("PB", 512), ("PC", 512), ("PD", 512)):
     SCRATCH[_n] = ("psum", [128, _w], _f)
 
-SEMAPHORES = ["sv", "sa", "st", "sg", "arrh", "arrg", "arr1", "arr2", "arr3", "arr4", "arrp", "arrx", "r1", "r2"]
-SEMAPHORES += ["d%d" % i for i in range(24)] + ["l%d" % i for i in range(16)]
+SEMAPHORES = ["sv", "sa", "st", "sg", "arrh", "arrg", "arr1", "arr2", "arr3", "arr4", "arrp", "arrx", "arri", "arrk", "ri", "rj", "r2", "r3"]
+SEMAPHORES += ["d%d" % i for i in range(32)] + ["l%d" % i for i in range(20)]
+
+
+def _slot(r):
+    return r % 2 * (NR // 2) + r // 2
 
 
 def _helpers(topo, core):
     return [c for c in topo.cores_of(core) if topo.die(c) != topo.die(core)]
+
+
+def _neighbours(topo, core):
+    return [c for c in topo.cores_of(core) if topo.die(c) == topo.die(core) and c != core]
 
 
 def _bits(es):
@@ -47,6 +55,7 @@ def _dst(topo, d, s):
 
 def _hand_on(g, core, T, topo, owner, j):
     me = T.rank_of(owner)
+    q = _slot(me)
     engs = topo.engines(core, T.cores[me - 1])
     near = len(topo.engines(owner, core))
     far = near - len(engs)
@@ -65,26 +74,49 @@ def _hand_on(g, core, T, topo, owner, j):
     def pieces(x):
         ds = [d for d in (2 * j, 2 * j + 1) if d != me]
         k = len(engs) // len(ds)
-        call("arrh" if x else "arrg", far // 4,
+        call("arrh" if x else "arrg", far // 4 if x or j in (1, 2) else (len(engs) if j == 0 else far // 2),
              [RemoteDMATransfer(dst_ids=[_dst(topo, T.cores[d], core)], dma_engine_mask=_bits(engs[k * i:k * i + k]), remote_sem=T.sem.arrp,
-                                srcs=[view("HT", 16 * (d % 2), 16 * (d % 2) + 16, x)], dsts=[view("PH1", 16 * me, 16 * me + 16, x)])
+                                srcs=[view("HT", 16 * (d % 2), 16 * (d % 2) + 16, x)], dsts=[view("PH1", 16 * q, 16 * q + 16, x)])
               for i, d in enumerate(ds)])
 
-    def relay(src, dst, w, sem):
-        if src not in SHARED:
-            return
-        cs = [T.cores[(me + DIRECT + 1 + 2 * (role % 2) + i) % NR] for i in range(2)]
+    def relay(src, n, dst, lo, w, sem, first):
         x = role < 2
-        call(src.lower(), near // 2,
+        cs = [T.cores[(me + i) % NR] for i in range(first, NR)]
+        k = (len(cs) + 1) // 2
+        cs = (cs[:k], cs[k:], cs[-k:], cs[:-k])[role]
+        call(src.lower(), n,
              [RemoteDMATransfer(dst_ids=[_dst(topo, c, core) for c in cs], dma_engine_mask=_bits(engs), remote_sem=T.sem[sem],
-                                srcs=[view(src, 0, w, x)], dsts=[view(dst, w * me, w * me + w, x) for c in cs])])
+                                srcs=[view(src, 0, w, x)], dsts=[view(dst, lo + w * q, lo + w * q + w, x) for c in cs])])
 
     pieces(True)
-    relay("R1", "LD1", SL, "arr1")
     pieces(False)
-    relay("R2", "W2", 16, "arr2")
+    relay("R2", far // 2, "W2", 0, 16, "arr2", 3)
     for s, n in done:
         g.wait_ge(T.sem[s], n)
+
+
+def _hand_info(g, core, T, topo, owner, j):
+    me = T.rank_of(owner)
+    lo = NL1 + NI * _slot(me)
+    engs = topo.engines(core, T.cores[me - 1])
+    far = len(topo.engines(owner, core)) - len(engs)
+    cs = [T.cores[(me + i) % NR] for i in ((1, 2, 3, 4, 5), (3, 4, 5, 6, 7), (6, 7), (1, 2))[j]], [T.cores[(me + i) % NR] for i in (1, 2)]
+    jobs = ((True,), (False,), (True, False))[j]
+    for k, x in enumerate(jobs):
+        g.wait_ge(T.sem["ri" if x else "rj"], far // 2)
+        src = T.RI[:, 0:NI].bitcast(dt.uint8) if x else T.RIs[:, 0:NI]
+        dst = T.LD1[:, lo:lo + NI].bitcast(dt.uint8) if x else T.LD1s[:, lo:lo + NI]
+        g.remote_dma_fused([RemoteDMATransfer(dst_ids=[_dst(topo, c, core) for c in cs[k]], dma_engine_mask=_bits(engs), remote_sem=T.sem.arri,
+                                              srcs=[src], dsts=[dst for c in cs[k]])], local_sem=T.sem["l%d" % k])
+    if j < 2:
+        lo, two = 16 * _slot(me), [T.cores[(me + i) % NR] for i in (1, 2)]
+        g.wait_ge(T.sem.r2, len(engs))
+        src = T.R2s[:, 0:16] if j else T.R2[:, 0:16].bitcast(dt.uint8)
+        dst = T.W2s[:, lo:lo + 16] if j else T.W2[:, lo:lo + 16].bitcast(dt.uint8)
+        g.remote_dma_fused([RemoteDMATransfer(dst_ids=[_dst(topo, c, core) for c in two], dma_engine_mask=_bits(engs), remote_sem=T.sem.arr2,
+                                              srcs=[src], dsts=[dst for c in two])], local_sem=T.sem.l1)
+    for k in range(2):
+        g.wait_ge(T.sem["l%d" % k], len(engs))
 
 
 def rank_program(g, core, T, topo):
@@ -93,10 +125,12 @@ def rank_program(g, core, T, topo):
         for c in T.cores:
             if core in _helpers(topo, c):
                 _hand_on(g, core, T, topo, c, _helpers(topo, c).index(core))
+            if core in _neighbours(topo, c):
+                _hand_info(g, core, T, topo, c, _neighbours(topo, c).index(core))
         return
     ENG = {"v": g.vector, "a": g.scalar, "t": g.tensor, "g": g, "s": g.sync}
     SEM = {"v": "sv", "a": "sa", "t": "st", "g": "sg"}
-    cnt, seen, acc, nd, nl, ends = {}, {q: {} for q in ENG}, {}, [0], [0], []
+    cnt, seen, acc, nd, nl, ends, items = {}, {q: {} for q in ENG}, {}, [0], [0], [], []
 
     def clash(a, lo, hi, st):
         if a[1] <= lo or hi <= a[0]:
@@ -137,6 +171,24 @@ def rank_program(g, core, T, topo):
                     n, lo, hi, st = span(x)
                     acc.setdefault(n, []).append((lo, hi, st, w, q, tok, dma))
 
+    def issue(kind, q, fn, rd, wr):
+        waits(q, rd, wr, kind != "op")
+        if kind == "op":
+            cnt[q] = cnt.get(q, 0) + 1
+            tok = (SEM[q], cnt[q])
+            fn().then_inc(T.sem[tok[0]], 1)
+        elif kind == "dma":
+            tok = ("d%d" % nd[0], 16)
+            nd[0] += 1
+            fn().then_inc(T.sem[tok[0]], 16)
+        else:
+            tok = ("l%d" % nl[0], fn[1])
+            nl[0] += 1
+            g.remote_dma_fused(fn[0], local_sem=T.sem[tok[0]])
+        note(q, rd, wr, tok, kind != "op")
+        if kind != "op":
+            ends.append(tok)
+
     def v(n, lo=0, hi=None, st=1):
         if isinstance(n, tuple):
             return (n[0], n[1] + lo, n[2] if hi is None else n[1] + hi, st)
@@ -146,10 +198,7 @@ def rank_program(g, core, T, topo):
         return T[x[0]][:, x[1]:x[2]] if x[3] == 1 else T[x[0]][:, x[1]:x[2]:x[3]]
 
     def op(q, fn, rd, wr):
-        waits(q, rd, wr)
-        cnt[q] = cnt.get(q, 0) + 1
-        fn().then_inc(T.sem[SEM[q]], 1)
-        note(q, rd, wr, (SEM[q], cnt[q]))
+        items.append(("op", q, fn, rd, wr))
 
     def sc(x):
         return ap(x) if isinstance(x, tuple) else x
@@ -169,16 +218,21 @@ def rank_program(g, core, T, topo):
     def red(out, a, o=A.add, neg=False):
         op("v", lambda: g.vector.tensor_reduce(ap(out), ap(a), AxisListType.X, o, negate=neg), [a], [out])
 
+    def least(out, a):
+        op("v", lambda: g.vector.tensor_reduce(ap(out), ap(a), AxisListType.X, A.min, apply_absolute_value=True), [a], [out])
+
     def cp(out, a):
         op("v", lambda: g.vector.tensor_copy(ap(out), ap(a)), [a], [out])
 
     def ms(out, c):
         op("v", lambda: g.vector.memset(ap(out), c), [], [out])
 
-    def act(out, a, fn=F.Copy, **kw):
+    def act(out, a, fn=F.Copy, off=None, **kw):
         k2 = {k: sc(x) for k, x in kw.items()}
-        op("a", lambda: g.scalar.activation(ap(out), ap(a), fn, **k2),
-           [a] + [x for k, x in kw.items() if isinstance(x, tuple) and k != "accum_out"], [out] + [x for k, x in kw.items() if k == "accum_out"])
+        x = ap(a) if off is None else ap(a).indirect(ap(off))
+        op("a", lambda: g.scalar.activation(ap(out), x, fn, **k2),
+           [a] + ([off] if off else []) + [y for k, y in kw.items() if isinstance(y, tuple) and k != "accum_out"],
+           [out] + [y for k, y in kw.items() if k == "accum_out"])
 
     def lin(out, x, a, b):
         act(out, x, F.Identity, scale=a, bias=b)
@@ -199,39 +253,31 @@ def rank_program(g, core, T, topo):
         op("v", lambda: g.vector.tensor_copy(ap(out), ap(win).indirect(ap(off))), [win, off], [out])
 
     def pick(out, win, off):
-        op("a", lambda: g.scalar.activation(ap(pl(out)), ap(pl(win)).indirect(ap(off)), F.Copy), [pl(win), off], [pl(out)])
+        act(pl(out), pl(win), off=off)
         op("v", lambda: g.vector.tensor_copy(ap(out).bitcast(dt.uint32), ap(win).bitcast(dt.uint32).indirect(ap(off))), [win, off], [out])
 
-    def dma(q, out, in_, oap=None, iap=None):
-        waits(q, [in_], [out], True)
-        s = "d%d" % nd[0]
-        nd[0] += 1
-        ENG[q].dma_start(ap(out) if oap is None else oap, ap(in_) if iap is None else iap).then_inc(T.sem[s], 16)
-        note(q, [in_], [out], (s, 16), True)
-        ends.append((s, 16))
+    def dma(q, out, in_, oap=None, iap=None, after=()):
+        items.append(("dma", q, lambda: ENG[q].dma_start(ap(out) if oap is None else oap, ap(in_) if iap is None else iap), [in_] + list(after), [out]))
 
     def codes(x):
         return ap(x).bitcast(dt.uint8)
 
-    def landed(n, lo, hi, tok, tok2=None):
-        if hi > lo:
-            note("-", [], [v(n, lo, hi)], tok, True)
-            note("-", [], [v(n + "s", lo, hi)], tok2 or tok, True)
+    def copy(out, in_, after=()):
+        dma("s", out, in_, codes(out), codes(in_), after)
+        dma("s", pl(out), pl(in_), None, None, after)
+
+    def landed(own, lo, hi, tok, tok2=None):
+        for a, b in ((lo, own[1]), (own[2], hi)):
+            if b > a:
+                note("-", [], [v(own[0], a, b)], tok, True)
+                note("-", [], [v(own[0] + "s", a, b)], tok2 or tok, True)
 
     def send(x, transfers):
-        transfers = [t if x else (t[0], pl(t[1]), pl(t[2]), t[3], t[4]) for t in transfers]
-        waits("g", [t[2] for t in transfers], [], True)
-        s, n = "l%d" % nl[0], 0
-        nl[0] += 1
-        out = []
-        for dc, y, z, mask, sem in transfers:
-            cast = codes if x else ap
-            out.append(RemoteDMATransfer(dst_ids=[_dst(topo, c, core) for c in dc], dma_engine_mask=mask, remote_sem=T.sem[sem],
-                                         srcs=[cast(z)], dsts=[cast(y) for c in dc]))
-            n += bin(mask).count("1")
-        g.remote_dma_fused(out, local_sem=T.sem[s])
-        note("g", [t[2] for t in transfers], [], (s, n), True)
-        ends.append((s, n))
+        transfers = [(t[0], pl(t[1]), pl(t[2]), t[3], t[4]) if x is False else t for t in transfers]
+        cast = codes if x else ap
+        out = [RemoteDMATransfer(dst_ids=[_dst(topo, c, core) for c in dc], dma_engine_mask=mask, remote_sem=T.sem[sem],
+                                 srcs=[cast(z)], dsts=[cast(y) for c in dc]) for dc, y, z, mask, sem in transfers]
+        items.append(("send", "g", (out, sum(bin(t[3]).count("1") for t in transfers)), [t[2] for t in transfers], []))
 
     oc_ = [T.cores[(me + i) % NR] for i in range(1, NR)]
     hs = _helpers(topo, core)
@@ -240,19 +286,20 @@ def rank_program(g, core, T, topo):
     m_all = topo.mask(core, oc_[0])
     far = [e for e in topo.engines(core, hs[0]) if e not in engs]
     bcast = 2 * ne * (NR - 1)
-    par, k4 = me % 2, me // 2
+    par, k4, q = me % 2, me // 2, _slot(me)
+    im = 2 * q
     HBM = ("hbm", 0, 1, 1)
 
-    def broadcast(dst, src, via, sem):
-        if via in SHARED:
-            for x in (True, False):
-                send(x, [([hs[(k4 + i + (0 if x else 2)) % 4]], v(via), src, _bits(es), via.lower()) for i, es in enumerate((engs, far))])
-        for x in (True, False):
-            send(x, [(oc_[:DIRECT] if via in SHARED else oc_, dst, src, m_all, sem)])
+    ns = _neighbours(topo, core)
+    h2, h4 = len(far) // 2, len(far) // 4
 
-    def to_helpers(x, es, sem):
-        k = len(es) // 4
-        send(x, [([c], v("HT"), v("TQ", 32 * j, 32 * j + 32), _bits(es[k * j:k * j + k]), sem) for j, c in enumerate(hs)])
+    def shared(via, src):
+        for x in (True, False):
+            to = [hs[(k4 + i + (0 if x else 2)) % 4] for i in range(2)] + [ns[0 if x else 1]]
+            send(x, [([c], v(via), src, _bits(es), via.lower()) for c, es in zip(to, (far[:h2], far[h2:], engs))])
+
+    def to_helpers(x, parts, sem):
+        send(x, [([hs[j]], v("HT"), v("TQ", 32 * j, 32 * j + 32), _bits(es), sem) for j, es in parts])
 
     top = {"SM": 0, "CK": 0, "OF": 0}
 
@@ -270,341 +317,337 @@ def rank_program(g, core, T, topo):
     def of(n=1):
         return new("OF", n, 2)
 
-    def iota(out, pattern, mult, small=True, base=0):
+    def col(x, i):
+        return v(x, i, i + 1)
+
+    def iota(out, pattern, mult=0, base=0, small=True):
         if small:
             op("g", lambda: g.iota(ap(out), pattern, base, mult, allow_small_or_imprecise_dtypes=True), [], [out])
         else:
             op("g", lambda: g.iota(ap(out), pattern, base, mult), [], [out])
 
+    def el(n, b, lo=0, hi=128, at=0):
+        return v(n, at + 4 * lo + b, at + 4 * hi, 4)
+
     ci, cf = (lambda i: v("CI", i, i + 1)), (lambda i: v("CF", i, i + 1))
-    P, I16, S16, Q4, P4, Q2 = cf(0), cf(1), cf(2), cf(3), cf(4), cf(5)
+    P, I16, S16, H2, QP, S2 = cf(0), cf(1), cf(2), cf(3), cf(4), cf(5)
+    KI, IREF, G128, Z128, HD = v("KI"), v("IREF"), v("G128"), v("ZB", 0, 128), v("ZE", 4, 516, 4)
+    J8, J16 = v("J32", 0, 8), v("J32", 0, 16)
     dma("s", v("UC"), HBM, None, T.u[:, 0:4])
     dma("s", v("TB"), HBM, None, T.tb[:, :])
-    for t in range(2):
-        dma("s", v("NZ", 72 * t, 72 * t + 64), HBM, None, T.nz[:, 64 * t:64 * t + 64])
+    dma("s", v("NT", 64, 64 + 4 * SL), HBM, None, T.nz[:, 0:4 * SL])
+    dma("s", v("NT", 0, 64), v("TB"), None, T.nz[:, 64:128])
     dma("s", v("WT"), v("TB"), None, T.w[:, :])
-    iota(ci(0), [[0, 1]], 1, False)
     iota(P, [[0, 1]], 1)
-    iota(v("KI"), [[1, 128]], 0)
-    iota(v("IREF"), [[0, 8], [1, 16]], 0)
-    iota(v("J32"), [[1, 32]], 0)
-    iota(v("QR"), [[0, 8], [1, 4], [0, 4]], 0)
+    iota(KI, [[1, 128]])
+    iota(IREF, [[0, 8], [1, 16]])
+    iota(ci(0), [[0, 1]], 1, 0, False)
 
-    J8, J16, Z128, HD = v("J32", 0, 8), v("J32", 0, 16), v("ZB", 0, 128), v("ZE", 4, 516, 4)
-    H16, P32, ia, ib, ct = ck(), ck(), ck(), ck(), ck()
     E = [v("EQ", 128 * b, 128 * b + 128) for b in range(4)]
-    PVb = [v("PV", 512 * b, 512 * b + 144) for b in range(4)]
 
-    def unit(b):
-        quant(E[b], v("ZE", 4 - b, 516 - b))
+    def PV(b, n):
+        return v("PV", 512 * b, 512 * b + n)
 
-    def noise(t):
-        for a in range(NR):
-            act(v("NT%d" % t, 72 * a, 72 * a + 72), v("NZ", 72 * t, 72 * t + 72))
-
-    ms(Z128, 0.0)
+    ms(v("ZB"), 0.0)
+    ms(v("CM"), 1.0)
+    for a in range(4):
+        act(v("INF", 145 * a, 145 * a + 145), v("ZB", 0, 145))
+    lin(el("ZW", 0), Z128, 1.0, MK)
+    lin(el("ZW", 1), Z128, 1.0, 1.0)
     ms(v("ZE"), 0.0)
-    ms(v("MVC"), 0.0)
-    ts(ci(1), ci(0), 15, A.bitwise_and)
-    ts(ci(2), ci(0), 4, A.logical_shift_right)
-    ts(ci(3), ci(0), 3, A.bitwise_and)
-    ts(ci(4), ci(0), 2, A.logical_shift_right)
-    ts(ci(5), ci(0), 1, A.bitwise_and)
-    ts(ci(6), ci(0), 1, A.logical_shift_right)
-    ts(HD, v("KI"), P, A.is_equal, 0.5, A.mult)
-    cp(v("CF", 1, 6), v("CI", 1, 6))
-    for n, b in (("OHT", 2), ("OHT", 3), ("ZT", 2), ("ZT", 3), ("SC", 3)):
-        act(v(n, b, 512, 4), Z128)
+    ts(v("TIE"), KI, P, A.is_gt, TINY, A.mult)
+    ts(el("CM", 1), KI, P, A.is_gt)
+    ts(HD, KI, P, A.is_equal, 0.5, A.mult)
     for b in range(4):
-        ts(v("NU", b, 512, 4), Z128, v("UC", b, b + 1), A.subtract)
-        lin(v("UT", b, 512, 4), Z128, 1.0, v("UC", b, b + 1))
-    lin(H16, S16, 16.0, 0.0)
-    for e, x in ((8, I16), (0, H16)):
-        lin(v("MVC", e, e + 6, 5), v("ZB", 0, 2), 1.0, x)
-    lin(P32, P, 1.0, 32.0)
-    for b in range(4):
-        act(v("INFO", 128 * b, 128 * b + 128), Z128)
-    for t in range(2):
-        act(v("NZ", 72 * t + 64, 72 * t + 72), v("ZB", 0, 8))
-    act(ct, P, F.Relu, bias=-16.0)
-    for b, x in ((1, 0.0), (2, 0.0), (0, 1.0)):
-        lin(v("S1", b, 512, 4), Z128, 1.0, x)
-    noise(0)
+        ts(el("NU", b), Z128, v("UC", b, b + 1), A.subtract)
+        lin(el("UT", b), Z128, 1.0, v("UC", b, b + 1))
+    quant(v("NUQ"), v("NU"))
+    for b in (2, 3):
+        lin(el("ZW", b), IREF, -1.0, 0.0)
+    op("v", lambda: g.vector.memset(T.INF[32:33, 65:66], -0.125 * me), [], [v("INF", 65, 66)])
+    ts(v("INF", 66, 67), P, float(q), A.is_equal, MK, A.mult)
 
     TQ = v("TQ")
-    unit(0)
-    quant(v("NUQ"), v("NU"))
     quant(TQ, v("TB"))
-    to_helpers(True, far, "arrh")
-    to_helpers(False, engs, "arrg")
-    pown, town = v("PH1", 16 * me, 16 * me + 16), v("TQ", 16 * me, 16 * me + 16)
-    dma("s", pown, town, codes(pown), codes(town))
-    dma("s", pl(pown), pl(town))
+    to_helpers(False, [(0, engs)], "arrg")
+    to_helpers(True, [(j, far[h4 * j:h4 * j + h4]) for j in range(4)], "arrh")
+    for a in (1, 2, 4):
+        act(v("NT", 64 + 4 * SL * a, 64 + 8 * SL * a), v("NT", 64, 64 + 4 * SL * a))
+    pown = v("PH1", 16 * q, 16 * q + 16)
+    copy(pown, v("TQ", 16 * me, 16 * me + 16))
+    iota(v("QREF"), [[0, 8], [1, 8], [0, 2]])
+    iota(v("J32"), [[1, 32]])
+    iota(G128, [[1, 8], [0, 16]])
     quant(v("UQ"), v("UT"))
     PX, PS, PL, PF = v("PA", 0, 128), v("PB", 0, 128), v("PC", 0, 128), v("PD", 0, 128)
-    mm(PX, TQ, v("NUQ"), True, False)
-    mm(PX, v("UQ"), TQ, False, True)
+    mm(PX, v("NUQ"), TQ, True, False)
+    mm(PX, TQ, v("UQ"), False, True)
     mm(PS, TQ, v("UQ"))
-    ts(v("TIE"), v("KI"), P, A.is_lt, TINY, A.mult)
-    unit(1)
-    rk, va, vb, OFF1 = sm(), sm(), sm(), of(4)
-    tt(v("CMP"), PX, v("TIE"), A.is_lt)
-    ts(ia, P, float(me), A.is_equal, MK, A.mult)
-    red(rk, v("CMP"))
-    quant(v("MVQ"), v("MVC"))
-    ts(v("OHT", 0, 512, 4), v("IREF"), rk, A.is_equal)
-    ts(v("OHT", 1, 512, 4), v("IREF"), 16.0, A.add, rk, A.is_equal)
-    ts(va, rk, 31.5, A.is_ge, 1000.0, A.mult)
-    ts(ib, P, float(me + 16), A.is_equal, -0.125, A.mult)
-    quant(v("OHQ"), v("OHT"))
-    mm(PL, v("OHQ"), v("MVQ"))
-    ts(vb, va, rk, A.add, P32, A.min)
-    ts(v("INFO", 0, 1), v("PB", 0, 1), 0.0, A.is_gt)
-    tt(v("INFO", 3, 4), ia, ib, A.add)
-    ts(v("INFO", 1, 2), vb, RND, A.add, RND, A.subtract)
-    tt(v("INFO", 2, 3), vb, v("INFO", 1, 2), A.subtract)
-    cp(v("INFO", 4, 8), v("PC", 0, 4))
-    ts(v(OFF1, 0, 1), v("PC", 0, 1), v("PC", 2, 3), A.add)
-    for b in range(2):
-        lin(v("OHT", b, 512, 4), Z128, 1.0, 2.0)
-    quant(v("L1S", 16, 144), v("INFO"))
-    pick(v("L1S", 0, 16), TQ, v(OFF1, 0, 1))
-    own, mine = v("LD1", SL * me, SL * me + SL), v("L1S", 0, SL)
-    broadcast(own, mine, "R1", "arr1")
-    dma("s", own, mine, codes(own), codes(mine))
-    dma("s", pl(own), pl(mine))
+    quant(v("ZWQ"), v("ZW"))
+    for b in (0, 1, 3):
+        lin(el("S1", b), Z128, 1.0, 1.0)
+    PO, OFF1, OFF2 = sm(3), of(), of()
+    tt(el("CM", 0), PX, v("TIE"), A.is_lt)
+    ts(v("INF", 64, 65), v("PB", 0, 1), 0.0, A.is_gt)
+    quant(v("CQ"), v("CM"))
+    mm(PL, v("ZWQ"), v("CQ"))
+    mm(PF, v("UQ"), TQ)
+    quant(v("L1S", 16, 144), v("INF", 64, 576))
+    least(col(PO, 0), PL)
+    ts(ci(1), ci(0), 15, A.bitwise_and)
+    cp(OFF1, col(PO, 0))
+    ts(ci(2), ci(0), 4, A.logical_shift_right)
+    pick(v("L1S", 0, 16), TQ, OFF1)
+    own, mine = v("LD1", SL * q, SL * q + SL), v("L1S", 0, SL)
+    for x in (True, False):
+        send(x, [(oc_, own, mine, m_all, "arr1")])
+    to_helpers(False, [(1, far[:h4]), (2, far[h4:h2]), (3, far[h2:])], "arrg")
+    quant(v("L0"), v("INF", 0, 512))
+    copy(own, v("L0", 0, SL))
 
-    WN, J18, F16, JB, FLW = sm(160), sm(16), sm(16), sm(32), sm(32)
-    JZ, WZ, CZ, CCW = sm(32), sm(168), ck(2), sm(16)
-    iota(J18, [[SL, 16]], 0)
-    iota(v(WN, 16, 24), [[0, 8]], 0, True, SL * NR)
-    iota(v("G128"), [[1, 8], [0, 16]], 0)
-    iota(v("C64"), [[0, 8], [1, 8]], 0)
-    iota(JZ, [[1, 2], [72, 16]], 0, True, 68)
-    iota(v(JB, 0, 16), [[1, 16]], 0)
-    iota(CCW, [[0, 8], [-16, 2]], 0, True, 112)
-    iota(v("RM"), [[0, 8], [1000, 16]], 0)
-    iota(v(FLW, 0, 8), [[-16, 8]], 0, True, 400)
-    iota(v(FLW, 8, 16), [[SL - 16, 8]], 0, True, 256)
-    iota(v(FLW, 16, 24), [[0, 8]], 0)
-    TIE8, TM0, TMB, TM1, TMP, c8, CB, C2, C3, EP, EQ1, Q22, Q8, THM, G8, cx = (
-        ck(8), ck(8), ck(8), ck(8), ck(8), ck(), ck(), ck(2), ck(), ck(), ck(), ck(), ck(), ck(8), ck(), ck())
-    lin(c8, I16, 8.0, -48.0)
-    lin(TIE8, J8, -0.125, 0.0)
-    lin(F16, J16, 0.0, 0.0)
-    ts(v(OFF1, 2, 3), v("PC", 1, 2), v("PC", 3, 4), A.add)
-    ts(v("S1", 3, 512, 4), v("IREF"), P, A.is_equal, ct, A.add)
-    quant(v("N0Q"), v("NT0"))
-    unit(2)
-    unit(3)
-    for b in range(4):
-        mm(PVb[b], E[b], v("N0Q"), True, False)
-    quant(v("S1Q"), v("S1"))
-    ts(G8, I16, 7.5, A.is_gt)
-    ts(TM0, J8, I16, A.is_equal, MK, A.mult)
-    pick(v("NB", 144, 160), TQ, v(OFF1, 2, 3))
-    lin(CB, G8, c8, 0.0)
-    lin(TMB, TM0, 1.0, -MK)
-    lin(v(CZ, 0, 1), CB, 2.0, 7.0)
-    lin(v(CZ, 1, 2), CB, 2.0, 8.0)
-    pick(v("W2", 400, 416), TQ, v(OFF1, 0, 1))
-    lin(cx, G8, 72.0, 65.0)
-    noise(1)
-    lin(v(C2, 0, 1), CB, 2.0, 7.0)
-    lin(v(C2, 1, 2), CB, 2.0, 167.0)
-    lin(TMP, TIE8, 1.0, MK)
-    lin(Q22, Q2, 2.0, 0.0)
-    act(v("NZ1", 64, 136), v("ZB", 0, 72))
-    OFT, OFG0, OX1, OX2 = of(8), of(), of(4), of(4)
-    ts(ci(7), ci(6), float(k4 + 1), A.add)
-    ts(OFT, J8, 0.0, A.add)
-    ts(C3, G8, Q2, A.mult, 80.0, A.mult)
-    ts(ci(7), ci(7), 3, A.bitwise_and)
-    ts(OFG0, S16, 0.0, A.add)
-    ts(v("M32"), v("J32"), P4, A.is_equal)
-    ts(EP, ci(7), 2.0, A.mult, float(par), A.add)
-    ts(THM, J8, S16, A.is_equal)
-    ts(Q8, I16, 7.0, A.min)
-    ts(EP, EP, I16, A.subtract, G8, A.mult)
-    ts(OX1, v("J32", 0, 4), 144.0, A.mult, cx, A.add)
-    ts(v("SC", 0, 512, 4), v("QR"), Q4, A.is_equal, 4.0, A.mult)
-    ts(TM1, J8, EP, A.subtract, I16, A.is_equal)
-    for b in (1, 2):
-        ts(v("SC", b, 512, 4), v("IREF"), I16, A.is_equal, 2.0, A.mult)
-    lin(C3, C3, 1.0, 3.5)
-    lin(EQ1, EP, 1.0, I16)
-    lin(TM1, TM1, MK, 0.0)
-    quant(v("N1Q"), v("NT1"))
-
-    landed("LD1", 0, own[1], ("arr1", bcast))
-    landed("LD1", own[2], 144, ("arr1", bcast))
-    mm(PF, v("S1Q"), v("LD1", 16, 144))
-    for b in range(4):
-        mm(PVb[b], E[b], v("LD1"), False, True)
-    FIT = v("PD", 0, 128, SL)
-    mx, K0, cm, s0, gv, t1, O0, OD0 = sm(), sm(8), sm(8), sm(), sm(), sm(), sm(160), sm(8)
-    OPZ, OX0, TG0, OFFH, OFE, TGZ, g7 = of(2), of(), of(), of(18), of(4), of(), sm()
-    OP0 = v(OPZ, 0, 1)
-    quant(v("ZWQ"), v("OHT"))
-    quant(v("WQ"), v("WT"))
-    red(mx, FIT, A.max, True)
-    tt(K0, FIT, TMB, A.subtract)
-    act(v("V0", 0, 576, 4), PVb[0])
-    act(cm, K0, F.Sign, bias=mx, accum_out=s0)
+    WN, WW, FS, FR, J17, JJ, QI, RM, JS = [sm(16) for i in range(9)]
+    TMP, TMB, TI8, CC = ck(8), ck(8), ck(8), ck(2)
+    nsg, fo, P32, CZ, G8, rq, rk, va, h8, mz = [ck() for i in range(10)]
+    C3, C7 = col(CC, 0), col(CC, 1)
+    K0, K1 = sm(16), v("KS", 8, 22)
+    LP, OFG, OX = of(2), of(2), of(8)
+    iota(v(J17, 0, 16, 2), [[SL, 8]])
+    iota(v(J17, 1, 16, 2), [[0, 8]], 0, NL1)
+    iota(RM, [[1, 2], [2, 4], [0, 2]])
+    iota(v(K0, 8, 16), [[0, 8]])
+    iota(WW, [[1, 2], [0, 8]], 0, -1)
+    lin(P32, P, 1.0, 32.0)
+    iota(QI, [[1, 8], [0, 2]])
+    ts(ci(3), ci(0), 1, A.bitwise_and)
+    ts(ci(4), ci(0), 1, A.logical_shift_right, 7, A.bitwise_and)
+    quant(E[0], v("ZE", 4, 516))
+    cp(v("CF", 1, 5), v("CI", 1, 5))
+    quant(v("NQ"), v("NT"))
     for b in range(1, 4):
-        act(v("V0", b, 576, 4), PVb[b])
+        quant(E[b], v("ZE", 4 - b, 516 - b))
+    act(v("Z2"), PL, F.Abs, bias=-16.0 * MK)
+    act(v("Y"), el("CM", 0), F.Identity, scale=-1.0, bias=127.0 / 128.0, accum_out=rk)
+    ts(el("S1", 2), v("QREF"), P, A.is_equal)
+    for b in range(4):
+        mm(PV(b, 128), E[b], v("NQ", 0, 128))
+    for b in range(4):
+        act(v("NZ1", 48 * b, 48 * b + 48), PV(b, 48))
+    for b in range(4):
+        mm(PV(b, NL1), E[b], v("NQ", 16, 16 + NL1), True, False)
+    quant(v("S1Q"), v("S1"))
+    red(col(PO, 1), v("Z2"), A.min)
+    ts(va, rk, 31.5, A.is_gt, 1000.0, A.mult)
+    ts(TMB, J8, QP, A.not_equal, -MK, A.mult)
+    ts(col(PO, 2), va, rk, A.add, P32, A.min)
+    cp(OFF2, col(PO, 1))
+    ts(v("INF", 72, 84, 4), PO, RND, A.add, RND, A.subtract)
+    act(v("DS"), PF, F.Sign, scale=-1.0, bias=TINY, accum_out=fo)
+    lin(h8, H2, 8.0, 0.0)
+    lin(S2, S16, 2.0, 0.0)
+    lin(TMP, v(RM, 0, 16, 2), -0.125, MK)
+    lin(CC, v("J32", 1, 3), 3.5, h8)
+    lin(v(FR, 1, 16, 2), v(WW, 0, 8), -112.0, fo)
+    pick(v("NB", NL1, NL1 + 16), TQ, OFF2)
+    tt(v("INF", 73, 84, 4), PO, v("INF", 72, 84, 4), A.subtract)
+    ts(OFG, v("J32", 0, 32, 16), S2, A.add)
+    cp(col(LP, 0), P)
+    quant(v("HS", 16, 144), v("INF", 64, 576))
+    for x in (True, False):
+        send(x, [([ns[j]], v("RI"), v("HS", 18, 18 + NI), _bits(es), "ri" if x else "rj")
+                 for j, es in ((0 if x else 1, far[:len(far) // 2]), (2, far[len(far) // 2:]))])
+    iown = v("LD1", NL1 + NI * q, NL1 + NI * q + NI)
+    copy(iown, v("HS", 18, 18 + NI), [v("LD1", 0, NL1)])
+    ts(nsg, QP, float(q), A.is_equal, 0.5, A.subtract)
+    ts(G8, I16, 7.5, A.is_gt)
+    pick(v("W2", 256, 272), TQ, OFF1)
+    lin(rq, QP, 0.125, 0.0)
+    lin(CZ, H2, float(DP), 280.0)
+    lin(rq, G8, -0.4375, rq)
+    lin(TI8, v(RM, 0, 16, 2), -0.0625, rq)
+    lin(JS, J16, 16.0, 0.0)
+    ts(mz, QP, S16, A.is_equal)
+    ts(v("MW", 0, 128), G128, S16, A.is_equal)
+    act(v("MW", 128, 256), Z128)
+    act(v("DW", 0, 16), v(Z128, 0, 16))
+    act(v("SG", NL1), v(Z128, 0, 16))
+    for b in (1, 3):
+        act(el("SC", b), Z128)
+    for b in (0, 2):
+        ts(el("SC", b), IREF, I16, A.is_equal, 2.0, A.mult)
+    ts(OX, v("J32", 2, 26, 3), CZ, A.add, mz, A.mult)
     quant(v("SCQ"), v("SC"))
-    ts(v("THP"), v("G128"), EQ1, A.not_equal, BIG, A.mult)
-    tt(v(F16, 0, 8), K0, TMP, A.subtract)
-    ts(OPZ, CZ, s0, A.add)
-    ts(gv, s0, 0.0, A.is_lt, 8.0, A.mult)
-    ts(t1, s0, -1.0, A.mult, s0, A.max)
-    ts(g7, s0, 0.0, A.is_lt, 7.0, A.add)
-    scatter(WN, J18, OP0)
-    ts(OX0, gv, s0, A.subtract, 7.0, A.add)
-    ts(TGZ, g7, t1, A.subtract)
-    tt(TM1, TM1, TIE8, A.add)
-    quant(v("NB", 0, 144), v("V0"))
-    ts(v(OFFH, par, par + 16), WN, I16, A.add, off=OX0)
-    scatter(WZ, JZ, OPZ)
-    hown = v("W2", 16 * me, 16 * me + 16)
-    pick(hown, v("NB"), v(OFFH, me + par, me + par + 1))
-    broadcast(hown, hown, "R2", "arr2")
+    quant(v("WQ"), v("WT"))
+    iota(JJ, [[64, 2], [16, 8]])
+    iota(v("KS", 16, 24), [[0, 8]])
 
-    landed("PH1", 0, pown[1], ("arrp", ne * NR))
-    landed("PH1", pown[2], 128, ("arrp", ne * NR))
+    def tab(j, lo=0, hi=16):
+        return v("TAB", 16 * lo + j, 16 * hi, 16)
+
+    iota(v("TAB"), [[16, 16], [0, 16]])
+    iota(tab(1), [[8, 16]])
+    iota(tab(2), [[-16, 16]], 0, 128)
+    iota(tab(3), [[-47, 2], [0, 8]], 0, 47)
+    iota(tab(4), [[1, 2], [0, 8]])
+    iota(tab(5, 8), [[0, 8]], 0, 128)
+    iota(tab(6), [[-16, 16]], 0, 144)
+    iota(tab(15, 8), [[SL, 8]], 0, 128)
+    iota(tab(5, 8 + q, 9 + q), [[0, 1]], 0, 256)
+    iota(tab(3, q, q + 1), [[0, 1]])
+
+    landed(own, 0, NL1, ("arr1", bcast))
+    mm(PF, v("S1Q"), v("LD1", 8, NL1))
+    for b in range(4):
+        mm(PV(b, NL1), E[b], v("LD1", 0, NL1), False, True)
+    FIT = v("PD", 8, 128, SL)
+    mx, cm, s0, gv, FM, bb, ww, ac, ab0, O0 = sm(), sm(16), sm(), sm(), sm(8), sm(16), sm(16), sm(), sm(), sm(16)
+    OP0, OX0, OFFH, OFE, TG0, XL = of(), of(), of(16), of(4), of(), of()
+    red(mx, FIT, A.max, True)
+    tt(v(K0, 0, 8), FIT, TMB, A.subtract)
+    act(v(cm, 0, 15), v(K0, 0, 15), F.Sign, bias=mx, accum_out=s0)
+    tt(FM, v(K0, 0, 8), TMP, A.subtract)
+    for b in range(4):
+        (cp if b == 0 else act)(v("V0", b, 4 * NL1, 4), PV(b, NL1))
+        if b == 1:
+            act(v(FR, 0, 16, 2), FM, F.Relu, scale=-2.0, bias=224.0)
+    ts(OP0, s0, 0.5, A.mult, C7, A.add)
+    ts(gv, s0, -7.0, A.is_lt, 8.0, A.mult)
+    scatter(WN, J17, OP0)
+    ts(OX0, s0, -0.5, A.mult, gv, A.add)
+    scatter(FS, FR, OP0)
+    ts(OFFH, WN, I16, A.add, off=OX0)
+    quant(v("NB", 0, NL1), v("V0"))
+    ts(ww, WW, nsg, A.mult, off=OX0)
+    hown = v("W2", 16 * q, 16 * q + 16)
+    pick(v("HS", 0, 16), v("NB"), col(OFFH, im))
+    mm(v("PB", 0, NL1), v("UQ"), v("NB", 0, NL1))
+    shared("R2", v("HS", 0, 16))
+    ts(bb, FS, -242.0, A.add, nsg, A.mult, off=OX0)
+    scatter(O0, QI, OP0)
+    act(v("SG", 0, NL1), v("PB", 0, NL1), F.Sign, bias=-TINY)
+    act(cm, v("SG"), F.Identity, off=col(OFFH, im), accum_out=ac)
+    act(ab0, s0, F.Abs, bias=7.0)
+    ts(OFE, v(O0, 0, 4), 16.0, A.mult, I16, A.add)
+    kown = v("KY", 8 * q, 8 * q + 1)
+    ts(kown, ac, col(ww, im), A.mult, col(bb, im), A.add)
+    send(None, [(oc_, kown, kown, m_all, "arrk")])
+
+    landed(pown, 0, 128, ("arrp", ne * NR))
+    landed(iown, NL1, NL1 + NI * NR, ("arri", bcast))
     gown = v("PG", 64 * par, 64 * par + 64)
-    BR16, FS, FB, TP, B32 = v(JB, 16, 32), sm(160), sm(16), sm(16), sm(32)
-    BR = v(JB, 16, 24)
-    ZR, DG, BSp, Zp, cc, m1, f2, KB, KBm, KBp, FLA, TA = (
-        sm(16), sm(16), sm(16), sm(), sm(16), sm(8), sm(8), sm(8), sm(8), sm(8), sm(64), sm(8))
-    LZ, kb = of(16), sm()
+    BP, B32, BSp, VS, DG, Zp, t1 = sm(32), sm(16), sm(32), sm(16), sm(16), sm(), sm()
+    BR = v(BP, 0, 16)
+    LZ = of()
+    CM1, TI0 = v("CMT", 0, 128), v("CMT", 128, 256)
+    DWb = [v("DW", 16 + DP * b, 16 + DP * (b + 1)) for b in range(4)]
     for b in range(4):
-        mm(PVb[b], E[b], v("N1Q"))
-    for b in range(4):
-        act(v("NZ1", b, 64, 4), v("PV", 512 * b, 512 * b + 16))
-    for b in range(4):
-        mm(PVb[b], E[b], v("N1Q"), True, False)
-        mm(PVb[b], E[b], v("LD1"), False, True)
-    scatter(FS, F16, OP0)
-    ts(TG0, t1, -1.0, A.mult, 7.0, A.add)
-    gather(ZR, WZ, TGZ)
-    scatter(O0, J16, OP0)
-    gather(cc, CCW, TGZ)
-    gather(FB, FS, TG0)
-    ts(LZ, ZR, Q22, A.add, off=OFG0)
-    ts(OFE, v(O0, 0, 8, 2), 16.0, A.mult, I16, A.add)
-    gather(BR16, O0, TG0)
-    lin(f2, v(FB, 0, 8), 1.0, -16.0)
-    tt(m1, v(FB, 0, 8), v(cc, 0, 8), A.min)
-    gather(DG, v("V0"), v(LZ, 0, 1))
+        mm(PV(b, 160), E[b], v("LD1"))
     pick(gown, v("PH1"), OFE)
     for x in (True, False):
         send(x, [([T.cores[me ^ 1]], gown, gown, m_all, "arrx")])
-    tt(KB, m1, f2, A.max)
+    ts(TG0, ab0, -0.5, A.mult, C3, A.add)
+    ts(XL, gv, QP, A.add)
+    gather(v(BP, 16, 32), O0, OX0)
+    gather(BR, O0, TG0)
+    gather(B32, JJ, TG0)
+    gather(BSp, BP, OFG)
     for b in range(2):
-        ts(v("ZT", b, 512, 4), HD, v(DG, b, b + 1), A.mult)
-    lin(Zp, v(DG, 0, 1), 1.0, v(DG, 1, 2))
-    act(OD0, v(O0, 0, 16, 2))
-    gather(BSp, BR, OFG0)
-    tt(KBm, KB, TM1, A.add)
-    tt(KBp, KB, TMP, A.add)
-    quant(v("ZQ"), v("ZT"))
-    mm(PL, v("ZWQ"), v("ZQ"))
-    gather(TP, J16, TG0)
-    red(kb, KBm, A.max, True)
-    for b in range(4):
-        act(v("V1", b, 576, 4), PVb[b])
-    lin(KBp, KBp, 1.0, kb)
-    lin(v(B32, 0, 16), TP, 8.0, 0.0)
-    lin(v(B32, 16, 32), TP, 8.0, 64.0)
-    ts(v("MASK"), v("C64"), S16, A.is_equal)
-    ts(TA, BR, v(BSp, 0, 1), A.not_equal, -BIG, A.mult)
-    ts(OX2, OX1, 1.0, A.add)
-    ts(v("TI0"), PL, Zp, A.is_lt, TINY, A.mult)
-    tt(v("INFO", 9, 264, 4), v("V0"), v("MASK"), A.mult, off=OX1)
-    tt(v("TI1"), TA, v("TI0"), A.add, off=OFT)
+        act(v(DWb[b], 128), PV(b, 160))
+    gather(VS, JS, XL)
+    pick(hown, v("NB"), col(OFFH, im))
+    ts(t1, col(BSp, 0), S16, A.is_equal, CZ, A.add)
+    lin(v(VS, 1, 16, 2), v(BR, 1, 16, 2), 16.0, 0.0)
+    ts(col(LP, 1), col(BSp, 16), 16.0, A.mult, I16, A.add)
+    ts(LZ, col(BSp, 0), float(NI), A.mult, t1, A.add)
+    gather(DG, v("DW", 0, 16 + 2 * DP), LZ)
+    act(v("CM", 192, 448, 2), v("DW", 0, 16 + 2 * DP), off=OX)
+    for b in range(2):
+        ts(el("INF", b, at=68), HD, col(DG, b), A.mult)
+    ts(Zp, col(DG, 0), col(DG, 1), A.add, 0.5, A.mult)
+    quant(v("ZQ"), v("INF", 68, 580))
+    mm(PL, v("S1Q"), v("ZQ"))
+    quant(v("CQ"), v("CM"))
+    for b in range(2, 4):
+        act(v(DWb[b], 128), PV(b, 160))
+    ts(TI0, PL, Zp, A.is_lt, TINY, A.mult)
+    mm(PF, v("SCQ"), v("CQ"))
+    act(v("FLA"), v(PF, 48))
 
-    landed("W2", 0, hown[1], ("arr2", bcast))
-    landed("W2", hown[2], 128, ("arr2", bcast))
-    landed("PG", 64 - 64 * par, 128 - 64 * par, ("arrx", 2 * ne))
+    for j in range(NR):
+        if j != q:
+            note("-", [], [v("KY", 8 * j, 8 * j + 1)], ("arrk", ne * (NR - 1)), True)
+    landed(gown, 0, 128, ("arrx", 2 * ne))
+    K = v("KY", 0, 64, 8)
+    nk, sg, ab, sj = v("KS", 0, 1), v("KS", 1, 2), v("KS", 2, 3), v("KS", 24, 38)
+    OP1, TG1 = v("OK", 0, 1), v("OK", 2, 3)
+    BS, VW, OFF3, TL = sm(16), sm(16), of(16), of(16)
+    red(nk, K, A.min)
+    tt(v(K1, 0, 8), K, TI8, A.add)
+    act(sj, K1, F.Sign, bias=nk, accum_out=sg)
+    act(ab, sg, F.Abs, bias=7.0)
+    ts(OP1, sg, 0.5, A.mult, C7, A.add)
+    scatter(BS, B32, OP1)
+    ts(TG1, ab, -0.5, A.mult, C3, A.add)
+    scatter(VW, VS, OP1)
+    ts(OFF3, BS, I16, A.add, off=TG1)
+    ts(TL, VW, I16, A.add, off=TG1)
+    pick(v("S3"), v("PG"), v(OFF3, 8 * par, 8 * par + 8))
+    bown = v("W3", 32 + 32 * k4, 64 + 32 * k4)
+    ks = [(k4 + i) % 4 for i in (1, 2, 3)]
+    h, r = ne // 2, ne // 4
+    for x, cuts in ((True, (0, h, h + r, ne)), (False, (0, r, h, ne))):
+        send(x, [([T.cores[par + 2 * k]], bown, v("S3", 32 * k, 32 * k + 32), _bits(engs[cuts[i]:cuts[i + 1]]), "arr3" if x else "arr4")
+                 for i, k in enumerate(ks)])
+
+    landed(hown, 0, 128, ("arr2", bcast))
     H = v("W2", 0, 128)
-    mm(PS, v("UQ"), H)
     mm(PX, v("UQ"), H, True, False)
     mm(PX, H, v("NUQ"), False, True)
     for b in range(4):
-        mm(v("PV", 512 * b, 512 * b + 128), E[b], H)
-    Kp, nx, sj, sg, ab, Mp, BS, O1, A1 = sm(8), sm(), sm(8), sm(), sm(), sm(), sm(160), sm(160), sm(16)
-    OP1, TG1, OFF3, OFFG = of(2), of(), of(16), of(32)
-    ts(v("IND"), PS, 0.0, A.is_gt)
-    tt(v("INP"), PS, v("THP"), A.is_gt)
-    op("v", lambda: g.vector.tensor_tensor_scan(ap(v("CS")), ap(v("RM")), ap(v("IND")), 0.0, A.min, A.add), [v("RM"), v("IND")], [v("CS")])
-    act(v("CMP"), v("INP"), F.Identity, scale=-1.0, accum_out=nx)
-    tt(v("CM1"), PX, v("TI1"), A.is_lt)
-    tt(Kp, v("CS", 15, 128, 16), KBp, A.add)
-    act(sj, Kp, F.Sign, bias=nx, accum_out=sg)
-    act(ab, sg, F.Abs)
+        mm(PV(b, 128), E[b], H)
+    Mp, G2, b01, nb, FL, OD = sm(), sm(32), sm(2), sm(), sm(2), sm(24)
+    G1, NL, HL, OFFF, TM = v(of(34), 1, 33), of(2), of(2), of(16), v(TL, im, im + 2)
+    ts(G1, v("TAB"), I16, A.add, off=TM)
+    tt(CM1, PX, TI0, A.is_lt)
+    gather(G2, v("TAB"), TM)
+    act(v("Z2", 0, 32), CM1, F.Identity, off=LP, accum_out=Mp)
+    ts(el("CM", 0, 16, 48), v("MW"), Mp, A.mult, off=TM)
+    ts(OFFF, v("FLA"), 0.0, A.add, off=col(G1, 17))
+    quant(v("CQ"), v("CM"))
+    mm(PL, v("SCQ"), v("CQ"))
+    act(v(DWb[0], 0, 128), PV(0, 128))
+    lin(nb, I16, col(G2, 4), -8.0)
+    DS = [v("DS", 32 * b, 32 * b + 32) for b in range(4)]
     for b in range(4):
-        act(v("D5", b, 512, 4), v("PV", 512 * b, 512 * b + 128))
-    red(Mp, v("CM1"))
-    tt(v("INFO", 10, 264, 4), v("V0"), v("MASK"), A.mult, off=OX2)
-    ts(OP1, C2, sg, A.add, 0.5, A.mult)
-    ts(v("INFO", 272, 400, 4), v("M32"), Mp, A.mult)
-    ts(v("INFO", 401, 432, 4), THM, Mp, A.mult)
-    scatter(BS, B32, OP1)
-    ts(TG1, ab, -0.5, A.mult, C3, A.add)
-    quant(v("MQ"), v("INFO"))
-    mm(PL, v("SCQ"), v("MQ"))
-    ts(OFF3, BS, I16, A.add, off=TG1)
-    scatter(O1, JB, OP1)
-    pick(v("S3"), v("PG"), v(OFF3, 8, 14))
-    bown = v("W3", 32 + 32 * k4, 64 + 32 * k4)
-    grp = [T.cores[par + 2 * ((k4 + i) % 4)] for i in (1, 2, 3)]
-    h, q = ne // 2, ne // 4
-    for x, cuts in ((True, (0, h, h + q, ne)), (False, (0, q, h, ne))):
-        send(x, [([c], bown, v("S3", 32 * i, 32 * i + 32), _bits(engs[cuts[i]:cuts[i + 1]]), "arr3" if x else "arr4") for i, c in enumerate(grp)])
+        if b < 3:
+            act(v(DWb[b + 1], 0, 128), PV(b + 1, 128))
+        act(DS[b], DWb[b], off=v(G1, 15, 17))
+    lin(b01, v(G2, 5, 17, 11), 1.0, I16)
+    pick(bown, v("PG"), v(OFF3, im, im + 2))
+    PR = v(PL, 16, 33, 16)
+    ts(NL, PR, 0.5, A.mult, nb, A.add)
+    ts(FL, PR, col(G2, 3), A.is_lt)
+    for b in range(4):
+        tt(el("V0", b, 0, 32), v("NZ1", 48 * b, 48 * b + 48), DS[b], A.add, off=NL)
+    for c in range(2):
+        ts(col(HL, c), col(FL, c), col(G2, 2 + 20 * c), A.mult, col(b01, c), A.add)
+    quant(v("W2", 128, 256), v("V0", 0, 512))
+    scatter(v(OD, 0, 16), RM, OP0)
+    pick(v("W3", 0, 32), v("W2"), HL)
 
-    xa, xb, xc, d1, d2, hx, ho, fs = sm(), sm(), sm(), sm(), sm(), sm(), sm(), sm(8)
-    E0, E1, E2, HL0, HL1, OFFF = of(), of(), of(), of(16), of(16), of(16)
-    X, O = v(A1, 14, 15), v(A1, 15, 16)
-    ts(OFFG, v("PC", 68, 100), Q4, A.add)
-    gather(A1, O1, TG1)
-    quant(v("W2", 256, 400), v("V1"))
-    act(d1, X, F.Sign, bias=float(-me))
-    act(d2, O, F.Sign, scale=-1.0, bias=X)
-    act(fs, v("PC", 100, 108), F.Sign, scale=-1.0, bias=31.0)
-    act(FLA, v("PC", 2, 66))
-    act(xa, d1, F.Abs, scale=8.0)
-    act(xb, d2, F.Abs, scale=16.0)
-    act(xc, d2, F.Abs)
-    lin(v(FLW, 24, 32), fs, 64.0, 64.0)
-    lin(hx, X, 16.0, I16)
-    lin(ho, O, 16.0, I16)
-    tt(v("VT"), v("NZ1"), v("D5"), A.add, off=OFFG)
-    ts(E0, xa, xb, A.add, X, A.add)
-    ts(E1, xa, xc, A.mult, O, A.add)
-    ts(E2, O, 8.0, A.mult, Q8, A.add)
-    quant(v("W2", 128, 256), v("VT"))
-    ts(HL0, FLW, hx, A.add, off=E0)
-    ts(HL1, v(FLW, 16, 32), ho, A.add, off=E1)
-    pick(bown, v("PG"), v(OFF3, 14, 16))
-    ts(OFFF, FLA, 0.0, A.add, off=E2)
-    pick(v("W3", 0, 16), v("W2"), v(HL0, 0, 1))
-    pick(v("W3", 16, 32), v("W2"), v(HL1, 0, 1))
-
-    landed("W3", 32, bown[1], ("arr3", ne), ("arr4", ne))
-    landed("W3", bown[2], 160, ("arr3", ne), ("arr4", ne))
+    landed(bown, 32, 160, ("arr3", ne), ("arr4", ne))
     pick(v("FT"), v("W3"), v(OFFF, 0, 8))
     dma("s", HBM, v("FT"), T.oc[:, :], codes(v("FT")))
     mm(PS, v("WQ"), v("FT"))
+    scatter(v(OD, 8, 24), RM, OP1)
     for k in range(4):
-        dma("a", HBM, v("FTs"), T.osc[4 * k:4 * k + 4, :], T.FTs[32 * k:32 * k + 4, 0:128])
-    for t, x in enumerate((OD0, O1)):
-        dma("a", HBM, x, T.od[t:t + 1, :], T.SM[0:1, x[1]:x[1] + 8])
+        dma("s" if k == 3 else "a", HBM, v("FTs"), T.osc[4 * k:4 * k + 4, :], T.FTs[32 * k:32 * k + 4, 0:128])
+    dma("s", HBM, OD, T.od[:, :], T.SM[0:1, OD[1]:OD[1] + 16])
     cp(v("Y"), PS)
     dma("s", HBM, v("Y"), T.y[:, :])
 
-    for q in ("v", "a", "t", "g"):
-        g.wait_ge(T.sem[SEM[q]], cnt[q])
+    for i in ORDER or range(len(items)):
+        issue(*items[i])
+    for e in ("v", "a", "t", "g"):
+        g.wait_ge(T.sem[SEM[e]], cnt[e])
     for s, n in ends:
         g.wait_ge(T.sem[s], n)

from concourse.bass import DstId, RemoteDMATransfer
from concourse.mybir import dt, AluOpType, AxisListType, ActivationFunctionType

A = AluOpType
F = ActivationFunctionType
NR, SL, NI = 8, 17, 3
NL1, DP = NR * SL, 288
TINY, MK, RND = 2.0 ** -100, 256.0, 2.0 ** 27

ORDER = [0,9,6,5,8,17,10,16,51,11,15,7,18,19,78,32,23,27,21,25,22,28,24,26,1,2,3,34,29,45,20,62,46,47,31,30,35,36,4,40,41,48,49,33,53,54,55,56,57,13,12,85,37,14,58,68,38,59,39,87,76,52,84,61,103,64,86,82,105,102,83,92,91,90,107,80,50,63,108,89,116,79,119,69,70,43,42,44,60,88,65,66,73,67,120,121,77,75,74,72,71,145,147,106,81,101,144,125,104,118,133,141,124,140,111,95,96,100,93,94,97,99,98,137,132,110,109,114,122,123,157,117,163,162,115,139,112,135,165,160,158,159,161,136,113,169,164,167,170,168,138,129,166,171,172,134,173,174,188,177,176,175,185,210,180,189,200,184,178,203,202,142,181,192,193,179,186,187,128,195,194,130,196,209,206,207,190,205,277,197,182,183,191,198,199,149,152,151,148,146,155,154,153,150,156,211,201,127,214,143,204,208,215,213,218,217,228,224,131,229,216,126,230,231,212,223,220,222,232,219,233,234,221,245,242,243,244,235,236,225,239,249,237,246,226,247,240,238,258,251,241,250,252,248,256,257,254,255,227,259,261,260,262,263,264,253,268,269,265,266,270,271,272,273,274,275,276,267,278,280,279,281,284,283,290,282,289,288,291,285,287,286]

_f, _b, _u = "float32", "bfloat16", "uint16"
SCRATCH = {}
for _n, _w, _t in (
        ("TB", 512, _b), ("UC", 4, _b), ("WT", 512, _b), ("ZB", 148, _b), ("UT", 512, _b), ("NU", 512, _b),
        ("CI", 8, "int32"), ("CF", 8, _f), ("CK", 128, _f), ("J32", 32, _f), ("KI", 128, _b), ("IREF", 128, _b),
        ("QREF", 128, _b), ("G128", 128, _b), ("ZE", 520, _b), ("TIE", 128, _b),
        ("ZW", 512, _b), ("CM", 512, _b), ("INF", 580, _b), ("S1", 512, _b), ("SC", 512, _b), ("NT", 608, _b),
        ("SM", 1024, _f), ("V0", 4 * NL1, _b), ("DW", 16 + 4 * DP, _b), ("NZ1", 192, _f), ("DS", 128, _f), ("Z2", 128, _f),
        ("CMT", 256, _f), ("MW", 256, _b), ("TAB", 256, _f), ("FLA", 80, _f), ("SG", NL1 + 16, _f),
        ("Y", 128, _f), ("OF", 256, _u), ("KY", 64, _b), ("KS", 64, _f), ("OK", 8, _u)):
    SCRATCH[_n] = ("sbuf", [128, _w], _t)
for _n, _w in (("UQ", 128), ("NUQ", 128), ("TQ", 128), ("ZWQ", 128), ("CQ", 128), ("S1Q", 128), ("EQ", 512), ("NQ", 152),
               ("WQ", 128), ("SCQ", 128), ("L1S", 144), ("L0", 128), ("LD1", 160), ("NB", 152), ("HS", 144), ("W2", 272), ("PH1", 128), ("PG", 128),
               ("S3", 128), ("W3", 160), ("ZQ", 128), ("FT", 128), ("HT", 32), ("RI", NI), ("R2", 16), ("R3", 32)):
    SCRATCH[_n] = ("sbuf", [128, _w], "float8_e4m3fn_x4")
    SCRATCH[_n + "s"] = ("sbuf", [128, _w], "uint8")
for _n, _w in (("PV", 2048), ("PA", 512), ("PB", 512), ("PC", 512), ("PD", 512)):
    SCRATCH[_n] = ("psum", [128, _w], _f)

SEMAPHORES = ["sv", "sa", "st", "sg", "arrh", "arrg", "arr1", "arr2", "arr3", "arr4", "arrp", "arrx", "arri", "arrk", "ri", "rj", "r2", "r3"]
SEMAPHORES += ["d%d" % i for i in range(32)] + ["l%d" % i for i in range(20)]


def _slot(r):
    return r % 2 * (NR // 2) + r // 2


def _helpers(topo, core):
    return [c for c in topo.cores_of(core) if topo.die(c) != topo.die(core)]


def _neighbours(topo, core):
    return [c for c in topo.cores_of(core) if topo.die(c) == topo.die(core) and c != core]


def _bits(es):
    return sum(1 << e for e in es)


def _dst(topo, d, s):
    rid, pid = topo.addr(d, s)
    return DstId(rid=rid, pnc=pid)


def _hand_on(g, core, T, topo, owner, j):
    me = T.rank_of(owner)
    q = _slot(me)
    engs = topo.engines(core, T.cores[me - 1])
    near = len(topo.engines(owner, core))
    far = near - len(engs)
    role = (j - me // 2) % 4
    done = []

    def call(sem, n, tr):
        g.wait_ge(T.sem[sem], n)
        s = "l%d" % len(done)
        g.remote_dma_fused(tr, local_sem=T.sem[s])
        done.append((s, len(engs)))

    def view(n, lo, hi, x):
        return T[n][:, lo:hi].bitcast(dt.uint8) if x else T[n + "s"][:, lo:hi]

    def pieces(x):
        ds = [d for d in (2 * j, 2 * j + 1) if d != me]
        k = len(engs) // len(ds)
        call("arrh" if x else "arrg", far // 4 if x or j in (1, 2) else (len(engs) if j == 0 else far // 2),
             [RemoteDMATransfer(dst_ids=[_dst(topo, T.cores[d], core)], dma_engine_mask=_bits(engs[k * i:k * i + k]), remote_sem=T.sem.arrp,
                                srcs=[view("HT", 16 * (d % 2), 16 * (d % 2) + 16, x)], dsts=[view("PH1", 16 * q, 16 * q + 16, x)])
              for i, d in enumerate(ds)])

    def relay(src, n, dst, lo, w, sem, first):
        x = role < 2
        cs = [T.cores[(me + i) % NR] for i in range(first, NR)]
        k = (len(cs) + 1) // 2
        cs = (cs[:k], cs[k:], cs[-k:], cs[:-k])[role]
        call(src.lower(), n,
             [RemoteDMATransfer(dst_ids=[_dst(topo, c, core) for c in cs], dma_engine_mask=_bits(engs), remote_sem=T.sem[sem],
                                srcs=[view(src, 0, w, x)], dsts=[view(dst, lo + w * q, lo + w * q + w, x) for c in cs])])

    pieces(True)
    pieces(False)
    relay("R2", far // 2, "W2", 0, 16, "arr2", 3)
    for s, n in done:
        g.wait_ge(T.sem[s], n)


def _hand_info(g, core, T, topo, owner, j):
    me = T.rank_of(owner)
    lo = NL1 + NI * _slot(me)
    engs = topo.engines(core, T.cores[me - 1])
    far = len(topo.engines(owner, core)) - len(engs)
    cs = [T.cores[(me + i) % NR] for i in ((1, 2, 3, 4, 5), (3, 4, 5, 6, 7), (6, 7), (1, 2))[j]], [T.cores[(me + i) % NR] for i in (1, 2)]
    jobs = ((True,), (False,), (True, False))[j]
    for k, x in enumerate(jobs):
        g.wait_ge(T.sem["ri" if x else "rj"], far // 2)
        src = T.RI[:, 0:NI].bitcast(dt.uint8) if x else T.RIs[:, 0:NI]
        dst = T.LD1[:, lo:lo + NI].bitcast(dt.uint8) if x else T.LD1s[:, lo:lo + NI]
        g.remote_dma_fused([RemoteDMATransfer(dst_ids=[_dst(topo, c, core) for c in cs[k]], dma_engine_mask=_bits(engs), remote_sem=T.sem.arri,
                                              srcs=[src], dsts=[dst for c in cs[k]])], local_sem=T.sem["l%d" % k])
    if j < 2:
        lo, two = 16 * _slot(me), [T.cores[(me + i) % NR] for i in (1, 2)]
        g.wait_ge(T.sem.r2, len(engs))
        src = T.R2s[:, 0:16] if j else T.R2[:, 0:16].bitcast(dt.uint8)
        dst = T.W2s[:, lo:lo + 16] if j else T.W2[:, lo:lo + 16].bitcast(dt.uint8)
        g.remote_dma_fused([RemoteDMATransfer(dst_ids=[_dst(topo, c, core) for c in two], dma_engine_mask=_bits(engs), remote_sem=T.sem.arr2,
                                              srcs=[src], dsts=[dst for c in two])], local_sem=T.sem.l1)
    for k in range(2):
        g.wait_ge(T.sem["l%d" % k], len(engs))


def rank_program(g, core, T, topo):
    me = T.rank_of(core)
    if me is None:
        for c in T.cores:
            if core in _helpers(topo, c):
                _hand_on(g, core, T, topo, c, _helpers(topo, c).index(core))
            if core in _neighbours(topo, c):
                _hand_info(g, core, T, topo, c, _neighbours(topo, c).index(core))
        return
    ENG = {"v": g.vector, "a": g.scalar, "t": g.tensor, "g": g, "s": g.sync}
    SEM = {"v": "sv", "a": "sa", "t": "st", "g": "sg"}
    cnt, seen, acc, nd, nl, ends, items = {}, {q: {} for q in ENG}, {}, [0], [0], [], []

    def clash(a, lo, hi, st):
        if a[1] <= lo or hi <= a[0]:
            return False
        return not (a[2] == st and st > 1 and a[0] % st != lo % st)

    def span(x):
        if SCRATCH[x[0]][0] == "psum":
            return x[0], x[1] // 512 * 512, (x[2] + 511) // 512 * 512, 1
        return x[0], x[1], x[2], x[3]

    def waits(q, rd, wr, dma=False):
        need = {}
        for w, xs in ((False, rd), (True, wr)):
            for x in xs:
                if x[0] not in SCRATCH:
                    continue
                n, lo, hi, st = span(x)
                ps = SCRATCH[n][0] == "psum"
                for a in acc.get(n, []):
                    if not clash(a, lo, hi, st):
                        continue
                    same = a[4] == q and not dma and not a[6]
                    if same and q == "t":
                        continue
                    if not (w or a[3]) and (same or not ps):
                        continue
                    need[a[5][0]] = max(need.get(a[5][0], 0), a[5][1])
        for s, val in need.items():
            if seen[q].get(s, 0) < val:
                ENG[q].wait_ge(T.sem[s], val)
                seen[q][s] = val

    def note(q, rd, wr, tok, dma=False):
        for w, xs in ((False, rd), (True, wr)):
            for x in xs:
                if x[0] in SCRATCH:
                    n, lo, hi, st = span(x)
                    acc.setdefault(n, []).append((lo, hi, st, w, q, tok, dma))

    def issue(kind, q, fn, rd, wr):
        waits(q, rd, wr, kind != "op")
        if kind == "op":
            cnt[q] = cnt.get(q, 0) + 1
            tok = (SEM[q], cnt[q])
            fn().then_inc(T.sem[tok[0]], 1)
        elif kind == "dma":
            tok = ("d%d" % nd[0], 16)
            nd[0] += 1
            fn().then_inc(T.sem[tok[0]], 16)
        else:
            tok = ("l%d" % nl[0], fn[1])
            nl[0] += 1
            g.remote_dma_fused(fn[0], local_sem=T.sem[tok[0]])
        note(q, rd, wr, tok, kind != "op")
        if kind != "op":
            ends.append(tok)

    def v(n, lo=0, hi=None, st=1):
        if isinstance(n, tuple):
            return (n[0], n[1] + lo, n[2] if hi is None else n[1] + hi, st)
        return (n, lo, SCRATCH[n][1][1] if hi is None else hi, st)

    def ap(x):
        return T[x[0]][:, x[1]:x[2]] if x[3] == 1 else T[x[0]][:, x[1]:x[2]:x[3]]

    def op(q, fn, rd, wr):
        items.append(("op", q, fn, rd, wr))

    def sc(x):
        return ap(x) if isinstance(x, tuple) else x

    def ts(out, in0, s1, op0, s2=None, op1=None, off=None):
        rd = [in0] + [s for s in (s1, s2, off) if isinstance(s, tuple)]
        a = ap(in0) if off is None else ap(in0).indirect(ap(off))
        if op1 is None:
            op("v", lambda: g.vector.tensor_scalar(ap(out), a, sc(s1), None, op0), rd, [out])
        else:
            op("v", lambda: g.vector.tensor_scalar(ap(out), a, sc(s1), sc(s2), op0, op1), rd, [out])

    def tt(out, a, b, o, off=None):
        x = ap(a) if off is None else ap(a).indirect(ap(off))
        op("v", lambda: g.vector.tensor_tensor(ap(out), x, ap(b), o), [a, b] + ([off] if off else []), [out])

    def red(out, a, o=A.add, neg=False):
        op("v", lambda: g.vector.tensor_reduce(ap(out), ap(a), AxisListType.X, o, negate=neg), [a], [out])

    def least(out, a):
        op("v", lambda: g.vector.tensor_reduce(ap(out), ap(a), AxisListType.X, A.min, apply_absolute_value=True), [a], [out])

    def cp(out, a):
        op("v", lambda: g.vector.tensor_copy(ap(out), ap(a)), [a], [out])

    def ms(out, c):
        op("v", lambda: g.vector.memset(ap(out), c), [], [out])

    def act(out, a, fn=F.Copy, off=None, **kw):
        k2 = {k: sc(x) for k, x in kw.items()}
        x = ap(a) if off is None else ap(a).indirect(ap(off))
        op("a", lambda: g.scalar.activation(ap(out), x, fn, **k2),
           [a] + ([off] if off else []) + [y for k, y in kw.items() if isinstance(y, tuple) and k != "accum_out"],
           [out] + [y for k, y in kw.items() if k == "accum_out"])

    def lin(out, x, a, b):
        act(out, x, F.Identity, scale=a, bias=b)

    def pl(x):
        return (x[0] + "s", x[1], x[2], 1)

    def quant(out, in_):
        op("v", lambda: g.vector.quantize_mx(ap(out), ap(pl(out)), ap(in_)), [in_], [out, pl(out)])

    def mm(out, w, x, start=True, stop=True):
        op("t", lambda: g.tensor.matmul_mx(ap(out), ap(w), ap(pl(w)), ap(x), ap(pl(x)), start, stop), [w, pl(w), x, pl(x)], [out])

    def scatter(out, in_, off):
        op("v", lambda: g.vector.tensor_copy(ap(out).indirect(ap(off)), ap(in_)), [in_, off], [out])

    def gather(out, win, off):
        op("v", lambda: g.vector.tensor_copy(ap(out), ap(win).indirect(ap(off))), [win, off], [out])

    def pick(out, win, off):
        act(pl(out), pl(win), off=off)
        op("v", lambda: g.vector.tensor_copy(ap(out).bitcast(dt.uint32), ap(win).bitcast(dt.uint32).indirect(ap(off))), [win, off], [out])

    def dma(q, out, in_, oap=None, iap=None, after=()):
        items.append(("dma", q, lambda: ENG[q].dma_start(ap(out) if oap is None else oap, ap(in_) if iap is None else iap), [in_] + list(after), [out]))

    def codes(x):
        return ap(x).bitcast(dt.uint8)

    def copy(out, in_, after=()):
        dma("s", out, in_, codes(out), codes(in_), after)
        dma("s", pl(out), pl(in_), None, None, after)

    def landed(own, lo, hi, tok, tok2=None):
        for a, b in ((lo, own[1]), (own[2], hi)):
            if b > a:
                note("-", [], [v(own[0], a, b)], tok, True)
                note("-", [], [v(own[0] + "s", a, b)], tok2 or tok, True)

    def send(x, transfers):
        transfers = [(t[0], pl(t[1]), pl(t[2]), t[3], t[4]) if x is False else t for t in transfers]
        cast = codes if x else ap
        out = [RemoteDMATransfer(dst_ids=[_dst(topo, c, core) for c in dc], dma_engine_mask=mask, remote_sem=T.sem[sem],
                                 srcs=[cast(z)], dsts=[cast(y) for c in dc]) for dc, y, z, mask, sem in transfers]
        items.append(("send", "g", (out, sum(bin(t[3]).count("1") for t in transfers)), [t[2] for t in transfers], []))

    oc_ = [T.cores[(me + i) % NR] for i in range(1, NR)]
    hs = _helpers(topo, core)
    engs = topo.engines(core, oc_[0])
    ne = len(engs)
    m_all = topo.mask(core, oc_[0])
    far = [e for e in topo.engines(core, hs[0]) if e not in engs]
    bcast = 2 * ne * (NR - 1)
    par, k4, q = me % 2, me // 2, _slot(me)
    im = 2 * q
    HBM = ("hbm", 0, 1, 1)

    ns = _neighbours(topo, core)
    h2, h4 = len(far) // 2, len(far) // 4

    def shared(via, src):
        for x in (True, False):
            to = [hs[(k4 + i + (0 if x else 2)) % 4] for i in range(2)] + [ns[0 if x else 1]]
            send(x, [([c], v(via), src, _bits(es), via.lower()) for c, es in zip(to, (far[:h2], far[h2:], engs))])

    def to_helpers(x, parts, sem):
        send(x, [([hs[j]], v("HT"), v("TQ", 32 * j, 32 * j + 32), _bits(es), sem) for j, es in parts])

    top = {"SM": 0, "CK": 0, "OF": 0}

    def new(n, w, al):
        lo = (top[n] + al - 1) // al * al
        top[n] = lo + w
        return (n, lo, lo + w, 1)

    def sm(n=1):
        return new("SM", n, 8 if n >= 8 else 1)

    def ck(n=1):
        return new("CK", n, 8 if n >= 8 else 1)

    def of(n=1):
        return new("OF", n, 2)

    def col(x, i):
        return v(x, i, i + 1)

    def iota(out, pattern, mult=0, base=0, small=True):
        if small:
            op("g", lambda: g.iota(ap(out), pattern, base, mult, allow_small_or_imprecise_dtypes=True), [], [out])
        else:
            op("g", lambda: g.iota(ap(out), pattern, base, mult), [], [out])

    def el(n, b, lo=0, hi=128, at=0):
        return v(n, at + 4 * lo + b, at + 4 * hi, 4)

    ci, cf = (lambda i: v("CI", i, i + 1)), (lambda i: v("CF", i, i + 1))
    P, I16, S16, H2, QP, S2 = cf(0), cf(1), cf(2), cf(3), cf(4), cf(5)
    KI, IREF, G128, Z128, HD = v("KI"), v("IREF"), v("G128"), v("ZB", 0, 128), v("ZE", 4, 516, 4)
    J8, J16 = v("J32", 0, 8), v("J32", 0, 16)
    dma("s", v("UC"), HBM, None, T.u[:, 0:4])
    dma("s", v("TB"), HBM, None, T.tb[:, :])
    dma("s", v("NT", 64, 64 + 4 * SL), HBM, None, T.nz[:, 0:4 * SL])
    dma("s", v("NT", 0, 64), v("TB"), None, T.nz[:, 64:128])
    dma("s", v("WT"), v("TB"), None, T.w[:, :])
    iota(P, [[0, 1]], 1)
    iota(KI, [[1, 128]])
    iota(IREF, [[0, 8], [1, 16]])
    iota(ci(0), [[0, 1]], 1, 0, False)

    E = [v("EQ", 128 * b, 128 * b + 128) for b in range(4)]

    def PV(b, n):
        return v("PV", 512 * b, 512 * b + n)

    ms(v("ZB"), 0.0)
    ms(v("CM"), 1.0)
    for a in range(4):
        act(v("INF", 145 * a, 145 * a + 145), v("ZB", 0, 145))
    lin(el("ZW", 0), Z128, 1.0, MK)
    lin(el("ZW", 1), Z128, 1.0, 1.0)
    ms(v("ZE"), 0.0)
    ts(v("TIE"), KI, P, A.is_gt, TINY, A.mult)
    ts(el("CM", 1), KI, P, A.is_gt)
    ts(HD, KI, P, A.is_equal, 0.5, A.mult)
    for b in range(4):
        ts(el("NU", b), Z128, v("UC", b, b + 1), A.subtract)
        lin(el("UT", b), Z128, 1.0, v("UC", b, b + 1))
    quant(v("NUQ"), v("NU"))
    for b in (2, 3):
        lin(el("ZW", b), IREF, -1.0, 0.0)
    op("v", lambda: g.vector.memset(T.INF[32:33, 65:66], -0.125 * me), [], [v("INF", 65, 66)])
    ts(v("INF", 66, 67), P, float(q), A.is_equal, MK, A.mult)

    TQ = v("TQ")
    quant(TQ, v("TB"))
    to_helpers(False, [(0, engs)], "arrg")
    to_helpers(True, [(j, far[h4 * j:h4 * j + h4]) for j in range(4)], "arrh")
    for a in (1, 2, 4):
        act(v("NT", 64 + 4 * SL * a, 64 + 8 * SL * a), v("NT", 64, 64 + 4 * SL * a))
    pown = v("PH1", 16 * q, 16 * q + 16)
    copy(pown, v("TQ", 16 * me, 16 * me + 16))
    iota(v("QREF"), [[0, 8], [1, 8], [0, 2]])
    iota(v("J32"), [[1, 32]])
    iota(G128, [[1, 8], [0, 16]])
    quant(v("UQ"), v("UT"))
    PX, PS, PL, PF = v("PA", 0, 128), v("PB", 0, 128), v("PC", 0, 128), v("PD", 0, 128)
    mm(PX, v("NUQ"), TQ, True, False)
    mm(PX, TQ, v("UQ"), False, True)
    mm(PS, TQ, v("UQ"))
    quant(v("ZWQ"), v("ZW"))
    for b in (0, 1, 3):
        lin(el("S1", b), Z128, 1.0, 1.0)
    PO, OFF1, OFF2 = sm(3), of(), of()
    tt(el("CM", 0), PX, v("TIE"), A.is_lt)
    ts(v("INF", 64, 65), v("PB", 0, 1), 0.0, A.is_gt)
    quant(v("CQ"), v("CM"))
    mm(PL, v("ZWQ"), v("CQ"))
    mm(PF, v("UQ"), TQ)
    quant(v("L1S", 16, 144), v("INF", 64, 576))
    least(col(PO, 0), PL)
    ts(ci(1), ci(0), 15, A.bitwise_and)
    cp(OFF1, col(PO, 0))
    ts(ci(2), ci(0), 4, A.logical_shift_right)
    pick(v("L1S", 0, 16), TQ, OFF1)
    own, mine = v("LD1", SL * q, SL * q + SL), v("L1S", 0, SL)
    for x in (True, False):
        send(x, [(oc_, own, mine, m_all, "arr1")])
    to_helpers(False, [(1, far[:h4]), (2, far[h4:h2]), (3, far[h2:])], "arrg")
    quant(v("L0"), v("INF", 0, 512))
    copy(own, v("L0", 0, SL))

    WN, WW, FS, FR, J17, JJ, QI, RM, JS = [sm(16) for i in range(9)]
    TMP, TMB, TI8, CC = ck(8), ck(8), ck(8), ck(2)
    nsg, fo, P32, CZ, G8, rq, rk, va, h8, mz = [ck() for i in range(10)]
    C3, C7 = col(CC, 0), col(CC, 1)
    K0, K1 = sm(16), v("KS", 8, 22)
    LP, OFG, OX = of(2), of(2), of(8)
    iota(v(J17, 0, 16, 2), [[SL, 8]])
    iota(v(J17, 1, 16, 2), [[0, 8]], 0, NL1)
    iota(RM, [[1, 2], [2, 4], [0, 2]])
    iota(v(K0, 8, 16), [[0, 8]])
    iota(WW, [[1, 2], [0, 8]], 0, -1)
    lin(P32, P, 1.0, 32.0)
    iota(QI, [[1, 8], [0, 2]])
    ts(ci(3), ci(0), 1, A.bitwise_and)
    ts(ci(4), ci(0), 1, A.logical_shift_right, 7, A.bitwise_and)
    quant(E[0], v("ZE", 4, 516))
    cp(v("CF", 1, 5), v("CI", 1, 5))
    quant(v("NQ"), v("NT"))
    for b in range(1, 4):
        quant(E[b], v("ZE", 4 - b, 516 - b))
    act(v("Z2"), PL, F.Abs, bias=-16.0 * MK)
    act(v("Y"), el("CM", 0), F.Identity, scale=-1.0, bias=127.0 / 128.0, accum_out=rk)
    ts(el("S1", 2), v("QREF"), P, A.is_equal)
    for b in range(4):
        mm(PV(b, 128), E[b], v("NQ", 0, 128))
    for b in range(4):
        act(v("NZ1", 48 * b, 48 * b + 48), PV(b, 48))
    for b in range(4):
        mm(PV(b, NL1), E[b], v("NQ", 16, 16 + NL1), True, False)
    quant(v("S1Q"), v("S1"))
    red(col(PO, 1), v("Z2"), A.min)
    ts(va, rk, 31.5, A.is_gt, 1000.0, A.mult)
    ts(TMB, J8, QP, A.not_equal, -MK, A.mult)
    ts(col(PO, 2), va, rk, A.add, P32, A.min)
    cp(OFF2, col(PO, 1))
    ts(v("INF", 72, 84, 4), PO, RND, A.add, RND, A.subtract)
    act(v("DS"), PF, F.Sign, scale=-1.0, bias=TINY, accum_out=fo)
    lin(h8, H2, 8.0, 0.0)
    lin(S2, S16, 2.0, 0.0)
    lin(TMP, v(RM, 0, 16, 2), -0.125, MK)
    lin(CC, v("J32", 1, 3), 3.5, h8)
    lin(v(FR, 1, 16, 2), v(WW, 0, 8), -112.0, fo)
    pick(v("NB", NL1, NL1 + 16), TQ, OFF2)
    tt(v("INF", 73, 84, 4), PO, v("INF", 72, 84, 4), A.subtract)
    ts(OFG, v("J32", 0, 32, 16), S2, A.add)
    cp(col(LP, 0), P)
    quant(v("HS", 16, 144), v("INF", 64, 576))
    for x in (True, False):
        send(x, [([ns[j]], v("RI"), v("HS", 18, 18 + NI), _bits(es), "ri" if x else "rj")
                 for j, es in ((0 if x else 1, far[:len(far) // 2]), (2, far[len(far) // 2:]))])
    iown = v("LD1", NL1 + NI * q, NL1 + NI * q + NI)
    copy(iown, v("HS", 18, 18 + NI), [v("LD1", 0, NL1)])
    ts(nsg, QP, float(q), A.is_equal, 0.5, A.subtract)
    ts(G8, I16, 7.5, A.is_gt)
    pick(v("W2", 256, 272), TQ, OFF1)
    lin(rq, QP, 0.125, 0.0)
    lin(CZ, H2, float(DP), 280.0)
    lin(rq, G8, -0.4375, rq)
    lin(TI8, v(RM, 0, 16, 2), -0.0625, rq)
    lin(JS, J16, 16.0, 0.0)
    ts(mz, QP, S16, A.is_equal)
    ts(v("MW", 0, 128), G128, S16, A.is_equal)
    act(v("MW", 128, 256), Z128)
    act(v("DW", 0, 16), v(Z128, 0, 16))
    act(v("SG", NL1), v(Z128, 0, 16))
    for b in (1, 3):
        act(el("SC", b), Z128)
    for b in (0, 2):
        ts(el("SC", b), IREF, I16, A.is_equal, 2.0, A.mult)
    ts(OX, v("J32", 2, 26, 3), CZ, A.add, mz, A.mult)
    quant(v("SCQ"), v("SC"))
    quant(v("WQ"), v("WT"))
    iota(JJ, [[64, 2], [16, 8]])
    iota(v("KS", 16, 24), [[0, 8]])

    def tab(j, lo=0, hi=16):
        return v("TAB", 16 * lo + j, 16 * hi, 16)

    iota(v("TAB"), [[16, 16], [0, 16]])
    iota(tab(1), [[8, 16]])
    iota(tab(2), [[-16, 16]], 0, 128)
    iota(tab(3), [[-47, 2], [0, 8]], 0, 47)
    iota(tab(4), [[1, 2], [0, 8]])
    iota(tab(5, 8), [[0, 8]], 0, 128)
    iota(tab(6), [[-16, 16]], 0, 144)
    iota(tab(15, 8), [[SL, 8]], 0, 128)
    iota(tab(5, 8 + q, 9 + q), [[0, 1]], 0, 256)
    iota(tab(3, q, q + 1), [[0, 1]])

    landed(own, 0, NL1, ("arr1", bcast))
    mm(PF, v("S1Q"), v("LD1", 8, NL1))
    for b in range(4):
        mm(PV(b, NL1), E[b], v("LD1", 0, NL1), False, True)
    FIT = v("PD", 8, 128, SL)
    mx, cm, s0, gv, FM, bb, ww, ac, ab0, O0 = sm(), sm(16), sm(), sm(), sm(8), sm(16), sm(16), sm(), sm(), sm(16)
    OP0, OX0, OFFH, OFE, TG0, XL = of(), of(), of(16), of(4), of(), of()
    red(mx, FIT, A.max, True)
    tt(v(K0, 0, 8), FIT, TMB, A.subtract)
    act(v(cm, 0, 15), v(K0, 0, 15), F.Sign, bias=mx, accum_out=s0)
    tt(FM, v(K0, 0, 8), TMP, A.subtract)
    for b in range(4):
        (cp if b == 0 else act)(v("V0", b, 4 * NL1, 4), PV(b, NL1))
        if b == 1:
            act(v(FR, 0, 16, 2), FM, F.Relu, scale=-2.0, bias=224.0)
    ts(OP0, s0, 0.5, A.mult, C7, A.add)
    ts(gv, s0, -7.0, A.is_lt, 8.0, A.mult)
    scatter(WN, J17, OP0)
    ts(OX0, s0, -0.5, A.mult, gv, A.add)
    scatter(FS, FR, OP0)
    ts(OFFH, WN, I16, A.add, off=OX0)
    quant(v("NB", 0, NL1), v("V0"))
    ts(ww, WW, nsg, A.mult, off=OX0)
    hown = v("W2", 16 * q, 16 * q + 16)
    pick(v("HS", 0, 16), v("NB"), col(OFFH, im))
    mm(v("PB", 0, NL1), v("UQ"), v("NB", 0, NL1))
    shared("R2", v("HS", 0, 16))
    ts(bb, FS, -242.0, A.add, nsg, A.mult, off=OX0)
    scatter(O0, QI, OP0)
    act(v("SG", 0, NL1), v("PB", 0, NL1), F.Sign, bias=-TINY)
    act(cm, v("SG"), F.Identity, off=col(OFFH, im), accum_out=ac)
    act(ab0, s0, F.Abs, bias=7.0)
    ts(OFE, v(O0, 0, 4), 16.0, A.mult, I16, A.add)
    kown = v("KY", 8 * q, 8 * q + 1)
    ts(kown, ac, col(ww, im), A.mult, col(bb, im), A.add)
    send(None, [(oc_, kown, kown, m_all, "arrk")])

    landed(pown, 0, 128, ("arrp", ne * NR))
    landed(iown, NL1, NL1 + NI * NR, ("arri", bcast))
    gown = v("PG", 64 * par, 64 * par + 64)
    BP, B32, BSp, VS, DG, Zp, t1 = sm(32), sm(16), sm(32), sm(16), sm(16), sm(), sm()
    BR = v(BP, 0, 16)
    LZ = of()
    CM1, TI0 = v("CMT", 0, 128), v("CMT", 128, 256)
    DWb = [v("DW", 16 + DP * b, 16 + DP * (b + 1)) for b in range(4)]
    for b in range(4):
        mm(PV(b, 160), E[b], v("LD1"))
    pick(gown, v("PH1"), OFE)
    for x in (True, False):
        send(x, [([T.cores[me ^ 1]], gown, gown, m_all, "arrx")])
    ts(TG0, ab0, -0.5, A.mult, C3, A.add)
    ts(XL, gv, QP, A.add)
    gather(v(BP, 16, 32), O0, OX0)
    gather(BR, O0, TG0)
    gather(B32, JJ, TG0)
    gather(BSp, BP, OFG)
    for b in range(2):
        act(v(DWb[b], 128), PV(b, 160))
    gather(VS, JS, XL)
    pick(hown, v("NB"), col(OFFH, im))
    ts(t1, col(BSp, 0), S16, A.is_equal, CZ, A.add)
    lin(v(VS, 1, 16, 2), v(BR, 1, 16, 2), 16.0, 0.0)
    ts(col(LP, 1), col(BSp, 16), 16.0, A.mult, I16, A.add)
    ts(LZ, col(BSp, 0), float(NI), A.mult, t1, A.add)
    gather(DG, v("DW", 0, 16 + 2 * DP), LZ)
    act(v("CM", 192, 448, 2), v("DW", 0, 16 + 2 * DP), off=OX)
    for b in range(2):
        ts(el("INF", b, at=68), HD, col(DG, b), A.mult)
    ts(Zp, col(DG, 0), col(DG, 1), A.add, 0.5, A.mult)
    quant(v("ZQ"), v("INF", 68, 580))
    mm(PL, v("S1Q"), v("ZQ"))
    quant(v("CQ"), v("CM"))
    for b in range(2, 4):
        act(v(DWb[b], 128), PV(b, 160))
    ts(TI0, PL, Zp, A.is_lt, TINY, A.mult)
    mm(PF, v("SCQ"), v("CQ"))
    act(v("FLA"), v(PF, 48))

    for j in range(NR):
        if j != q:
            note("-", [], [v("KY", 8 * j, 8 * j + 1)], ("arrk", ne * (NR - 1)), True)
    landed(gown, 0, 128, ("arrx", 2 * ne))
    K = v("KY", 0, 64, 8)
    nk, sg, ab, sj = v("KS", 0, 1), v("KS", 1, 2), v("KS", 2, 3), v("KS", 24, 38)
    OP1, TG1 = v("OK", 0, 1), v("OK", 2, 3)
    BS, VW, OFF3, TL = sm(16), sm(16), of(16), of(16)
    red(nk, K, A.min)
    tt(v(K1, 0, 8), K, TI8, A.add)
    act(sj, K1, F.Sign, bias=nk, accum_out=sg)
    act(ab, sg, F.Abs, bias=7.0)
    ts(OP1, sg, 0.5, A.mult, C7, A.add)
    scatter(BS, B32, OP1)
    ts(TG1, ab, -0.5, A.mult, C3, A.add)
    scatter(VW, VS, OP1)
    ts(OFF3, BS, I16, A.add, off=TG1)
    ts(TL, VW, I16, A.add, off=TG1)
    pick(v("S3"), v("PG"), v(OFF3, 8 * par, 8 * par + 8))
    bown = v("W3", 32 + 32 * k4, 64 + 32 * k4)
    ks = [(k4 + i) % 4 for i in (1, 2, 3)]
    h, r = ne // 2, ne // 4
    for x, cuts in ((True, (0, h, h + r, ne)), (False, (0, r, h, ne))):
        send(x, [([T.cores[par + 2 * k]], bown, v("S3", 32 * k, 32 * k + 32), _bits(engs[cuts[i]:cuts[i + 1]]), "arr3" if x else "arr4")
                 for i, k in enumerate(ks)])

    landed(hown, 0, 128, ("arr2", bcast))
    H = v("W2", 0, 128)
    mm(PX, v("UQ"), H, True, False)
    mm(PX, H, v("NUQ"), False, True)
    for b in range(4):
        mm(PV(b, 128), E[b], H)
    Mp, G2, b01, nb, FL, OD = sm(), sm(32), sm(2), sm(), sm(2), sm(24)
    G1, NL, HL, OFFF, TM = v(of(34), 1, 33), of(2), of(2), of(16), v(TL, im, im + 2)
    ts(G1, v("TAB"), I16, A.add, off=TM)
    tt(CM1, PX, TI0, A.is_lt)
    gather(G2, v("TAB"), TM)
    act(v("Z2", 0, 32), CM1, F.Identity, off=LP, accum_out=Mp)
    ts(el("CM", 0, 16, 48), v("MW"), Mp, A.mult, off=TM)
    ts(OFFF, v("FLA"), 0.0, A.add, off=col(G1, 17))
    quant(v("CQ"), v("CM"))
    mm(PL, v("SCQ"), v("CQ"))
    act(v(DWb[0], 0, 128), PV(0, 128))
    lin(nb, I16, col(G2, 4), -8.0)
    DS = [v("DS", 32 * b, 32 * b + 32) for b in range(4)]
    for b in range(4):
        if b < 3:
            act(v(DWb[b + 1], 0, 128), PV(b + 1, 128))
        act(DS[b], DWb[b], off=v(G1, 15, 17))
    lin(b01, v(G2, 5, 17, 11), 1.0, I16)
    pick(bown, v("PG"), v(OFF3, im, im + 2))
    PR = v(PL, 16, 33, 16)
    ts(NL, PR, 0.5, A.mult, nb, A.add)
    ts(FL, PR, col(G2, 3), A.is_lt)
    for b in range(4):
        tt(el("V0", b, 0, 32), v("NZ1", 48 * b, 48 * b + 48), DS[b], A.add, off=NL)
    for c in range(2):
        ts(col(HL, c), col(FL, c), col(G2, 2 + 20 * c), A.mult, col(b01, c), A.add)
    quant(v("W2", 128, 256), v("V0", 0, 512))
    scatter(v(OD, 0, 16), RM, OP0)
    pick(v("W3", 0, 32), v("W2"), HL)

    landed(bown, 32, 160, ("arr3", ne), ("arr4", ne))
    pick(v("FT"), v("W3"), v(OFFF, 0, 8))
    dma("s", HBM, v("FT"), T.oc[:, :], codes(v("FT")))
    mm(PS, v("WQ"), v("FT"))
    scatter(v(OD, 8, 24), RM, OP1)
    for k in range(4):
        dma("s" if k == 3 else "a", HBM, v("FTs"), T.osc[4 * k:4 * k + 4, :], T.FTs[32 * k:32 * k + 4, 0:128])
    dma("s", HBM, OD, T.od[:, :], T.SM[0:1, OD[1]:OD[1] + 16])
    cp(v("Y"), PS)
    dma("s", HBM, v("Y"), T.y[:, :])

    for i in ORDER or range(len(items)):
        issue(*items[i])
    for e in ("v", "a", "t", "g"):
        g.wait_ge(T.sem[SEM[e]], cnt[e])
    for s, n in ends:
        g.wait_ge(T.sem[s], n)
